import numpy as np
import ml_dtypes


def mxq(x, axis, fmt="e4m3"):
    dtype, down = {"e4m3": (ml_dtypes.float8_e4m3fn, 7), "e5m2": (ml_dtypes.float8_e5m2, 14)}[fmt]
    v = np.moveaxis(np.asarray(x, np.float32).astype(ml_dtypes.bfloat16).astype(np.float64), axis, -1)
    blocks = v.reshape(v.shape[:-1] + (-1, 32))
    amax = np.abs(blocks).max(-1, keepdims=True)
    byte = np.maximum(np.where(amax > 0, np.frexp(amax)[1] - 1 + 127, 0) - down, 1)
    scale = np.exp2(byte - 127.0)
    codes = (blocks / scale).astype(np.float32).astype(dtype).astype(np.float64)
    return np.moveaxis((codes * scale).reshape(v.shape), -1, axis)


WIDE = False


def mx_kscale(k):
    if not WIDE:
        return np.ones(k)
    levels = np.array([10, -10, 5, -5, 0])
    if k % 512:
        return np.exp2(np.random.permutation(np.resize(levels, k // 32))).repeat(32)
    a = np.empty((k // 512, 16))
    for p in range(k // 512):
        a[p, :8] = np.random.permutation(np.resize(levels, 8))
        for g in range(8):
            far = levels[np.abs(levels - a[p, g]) >= 10]
            a[p, g + 8] = far[np.random.randint(len(far))]
    return np.exp2(a.ravel()).repeat(32)


def f64(x):
    return np.asarray(x).astype(np.float64)


def striped(idx):
    return np.tile(idx.reshape(-1, 16).T, (8, 1)).astype(np.uint16)


def unstriped(offs):
    return offs[:16].T.reshape(-1).astype(np.int64)


E2M1 = np.array([0.0, 0.5, 1.0, 1.5, 2.0, 3.0, 4.0, 6.0, -0.0, -0.5, -1.0, -1.5, -2.0, -3.0, -4.0, -6.0])


def pack_weight(w, fmt):
    k, n = w.shape
    w = f64(np.asarray(w, np.float32).astype(ml_dtypes.bfloat16)).reshape(k // 32, 32, n)
    amax = np.abs(w).max(1)
    if fmt == "e4m3":
        byte = np.frexp(amax)[1] - 1 + 127 - 7
    else:
        mant, ex = np.frexp(amax / 6.0)
        byte = np.where(mant > 0.5, ex, ex - 1) + 127
    byte = np.clip(np.where(amax > 0, byte, 1), 1, 254)
    scaled = (w * np.exp2(127.0 - byte)[:, None, :]).reshape(k, n).astype(np.float32)
    by_word = np.ascontiguousarray(scaled.reshape(k // 512, 128, 4, n).transpose(0, 1, 3, 2))
    if fmt == "e4m3":
        words = by_word.astype(ml_dtypes.float8_e4m3fn).view(np.uint8)
    else:
        c = by_word.astype(ml_dtypes.float4_e2m1fn).view(np.uint8) & 0xF
        words = (c[..., 0::2] | (c[..., 1::2] << 4)).reshape(k // 512, 128, 2 * n)
    return np.ascontiguousarray(words), np.ascontiguousarray(byte.astype(np.uint8).reshape(k // 512, 16, n))


def unpack_weight(words, scales, fmt):
    g, _, n = scales.shape
    words = np.ascontiguousarray(words).reshape(g, 128, n, -1)
    if fmt == "e4m3":
        vals = words.view(ml_dtypes.float8_e4m3fn).astype(np.float64)
    else:
        nib = np.empty((g, 128, n, 4), np.uint8)
        nib[..., 0::2] = words & 0xF
        nib[..., 1::2] = words >> 4
        vals = E2M1[nib]
    vals = vals * np.repeat(np.exp2(scales.astype(np.float64) - 127.0), 8, axis=1)[..., None]
    return vals.transpose(0, 1, 3, 2).reshape(g * 512, n)


def relu2(v):
    return np.maximum(v, 0.0) ** 2


K, T, E, C, H, N = 1024, 640, 2, 256, 1024, 384


def by_expert(wq, xq):
    return np.concatenate([wq[e].T @ xq[:, e * C:(e + 1) * C] for e in range(E)], axis=1)


def setup_inputs():
    n = np.random.standard_normal
    s = mx_kscale(K)[:, None]
    u = mx_kscale(H)
    w1 = [pack_weight(m, "e2m1") for m in n((E, K, H)) / np.sqrt(K) / s[None] * u[None, None, :]]
    w2 = [pack_weight(m, "e2m1") for m in n((E, H, N)) / np.sqrt(H) / u[None, :, None] ** 2]
    return {
        "xT": (n((K, T)) * s).astype(np.float32),
        "xr": n((N, T)).astype(np.float32),
        "w1_words": np.stack([m[0] for m in w1]),
        "w1_scales": np.stack([m[1] for m in w1]),
        "w2_words": np.stack([m[0] for m in w2]),
        "w2_scales": np.stack([m[1] for m in w2]),
        "gate": np.tile(np.random.uniform(0.2, 1.0, E * C), (N, 1)).astype(np.float32),
        "offs": striped(np.random.permutation(T)[:E * C]),
    }


def reference(xT, xr, w1_words, w1_scales, w2_words, w2_scales, gate, offs):
    idx = unstriped(offs)
    w1 = np.stack([unpack_weight(w1_words[e], w1_scales[e], "e2m1") for e in range(E)])
    w2 = np.stack([unpack_weight(w2_words[e], w2_scales[e], "e2m1") for e in range(E)])
    xq = mxq(f64(xT)[:, idx], 0, "e4m3")
    h = relu2(by_expert(w1, xq))
    y = by_expert(w2, mxq(h, 0, "e4m3"))
    out = f64(xr).copy()
    out[:, idx] += f64(gate) * y
    return out

@@ -1,0 +1,228 @@
+from contextlib import ExitStack
+
+import concourse.mybir as mybir
+from concourse.masks import make_identity
+
+K, T, E, C, H, N = 1024, 640, 2, 256, 1024, 384
+S = E * C
+FLOPS = 2 * S * (K * H + H * N)
+
+F32 = mybir.dt.float32
+BF16 = mybir.dt.bfloat16
+I32 = mybir.dt.int32
+U32 = mybir.dt.uint32
+U16 = mybir.dt.uint16
+U8 = mybir.dt.uint8
+E4M3 = mybir.dt.float8_e4m3fn_x4
+E2M1 = mybir.dt.float4_e2m1fn_x4
+ACT = mybir.ActivationFunctionType
+ALU = mybir.AluOpType
+
+P = 128
+KP = K // 512
+HP = H // 512
+ST = S // P
+NT = N // P
+
+CHUNKS = (((0, 640),), ((0, 384), (384, 640)))
+SCALAR_SHARE = {(0, 0): 256, (1, 0): 384, (1, 1): 128}
+QCOLS = (((0, 256), (256, 384)), ((384, 640),))
+H_SLOT = ("h0", "h1", "h2", "h3")
+Y_SLOT = ("h1", "h2", "h3", "y3")
+
+
+def tile_moe_res_mlp_relu2_kernel(tc, xT, xr, w1_words, w1_scales, w2_words, w2_scales, gate, offs, out):
+    nc = tc.nc
+    with ExitStack() as ctx:
+        keep = ctx.enter_context(tc.tile_pool(name="keep", bufs=1))
+        work = ctx.enter_context(tc.tile_pool(name="work", bufs=3))
+        ps_a = ctx.enter_context(tc.psum_pool(name="ps_a", bufs=3))
+        ps_t = ctx.enter_context(tc.psum_pool(name="ps_t", bufs=2))
+        ps_y = ctx.enter_context(tc.psum_pool(name="ps_y", bufs=3))
+
+        offsets = keep.tile([P, S // 16], U16, name="offsets")
+
+        raw = {}
+        for s in range(KP):
+            rows = xT[s * 512 : (s + 1) * 512, :].rearrange("(q j) w -> q j w", j=4)
+            for c, (c0, c1) in enumerate(CHUNKS[s]):
+                t = keep.tile([P, 4, c1 - c0], F32, name=f"raw{s}_{c}")
+                nc.sync.dma_start(out=t[:], in_=rows[:, :, c0:c1])
+                raw[s, c] = t
+            if s == 0:
+                nc.sync.dma_start(offsets[:], offs)
+
+        ident = keep.tile([P, P], F32, name="ident")
+        make_identity(nc, ident[:])
+        x_scales = [keep.tile([P, T], U8, name=f"x_scales{s}", align_bytes=64) for s in range(KP)]
+        for s in range(KP):
+            nc.gpsimd.memset(x_scales[s][:], 0)
+        w1s = keep.tile([P, E * KP, H], U8, name="w1s", align_bytes=64)
+        w2s = keep.tile([P, E * HP, N], U8, name="w2s", align_bytes=64)
+        nc.vector.memset(w1s[:].rearrange("p g i -> p (g i)").bitcast(I32), 0)
+        nc.vector.memset(w2s[:].rearrange("p g i -> p (g i)").bitcast(I32), 0)
+        warm = keep.tile([P, 1], F32, name="warm")
+        nc.vector.memset(warm[:], 0.0)
+        nc.scalar.activation(warm[:], warm[:], ACT.Square)
+        windows = [keep.tile([P, T], F32, name=f"window{n}") for n in range(NT)]
+        for n in range(NT):
+            nc.vector.memset(windows[n][:], 0.0)
+
+        w1s_rows = w1_scales.bitcast(I32).rearrange("e s q i -> q (e s) i")
+        w2s_rows = w2_scales.bitcast(I32).rearrange("e s q i -> q (e s) i")
+        for q in range(4):
+            nc.sync.dma_start(out=w1s[32 * q : 32 * q + 4, :, :].bitcast(I32), in_=w1s_rows[4 * q : 4 * q + 4, :, :])
+
+        w1w = [keep.tile([P, KP, 2 * H], U8, name=f"w1w{e}", align_bytes=64) for e in range(E)]
+        w1_rows = w1_words.bitcast(I32).rearrange("e s p w -> e p s w")
+        for e in range(E):
+            nc.sync.dma_start(out=w1w[e][:].bitcast(I32), in_=w1_rows[e])
+        for q in range(4):
+            nc.sync.dma_start(out=w2s[32 * q : 32 * q + 4, :, :].bitcast(I32), in_=w2s_rows[4 * q : 4 * q + 4, :, :])
+        w2w = keep.tile([P, E * HP, 2 * N], U8, name="w2w", align_bytes=64)
+        nc.sync.dma_start(out=w2w[:].bitcast(I32), in_=w2_words.bitcast(I32).rearrange("e s p w -> p (e s) w"))
+        gates = keep.tile([P, NT, S], F32, name="gates")
+        nc.sync.dma_start(out=gates[:], in_=gate.rearrange("(n p) s -> p n s", p=P))
+        residual = [keep.tile([P, T], F32, name=f"residual{n}") for n in range(NT)]
+        for n in range(NT):
+            nc.sync.dma_start(out=residual[n][:], in_=xr[n * P : (n + 1) * P, :])
+
+        grouped = [keep.tile([P, T, 4], BF16, name=f"grouped{s}", align_bytes=64) for s in range(KP)]
+        x_words = [keep.tile([P, T], U32, name=f"x_words{s}", align_bytes=64) for s in range(KP)]
+        g_words = {}
+        g_scales = {}
+        for s in range(KP):
+            for e in range(E):
+                g_words[s, e] = keep.tile([P, C], U32, name=f"g_words{s}_{e}", align_bytes=64)
+                g_scales[s, e] = keep.tile([P, C], U8, name=f"g_scales{s}_{e}", align_bytes=64)
+
+        def group_tokens(s):
+            for c, (c0, c1) in enumerate(CHUNKS[s]):
+                src = raw[s, c][:].rearrange("p j w -> p w j")
+                share = SCALAR_SHARE[s, c]
+                nc.scalar.activation(grouped[s][:, c0 : c0 + share, :], src[:, :share, :], ACT.Copy)
+                if c0 + share < c1:
+                    nc.vector.tensor_copy(out=grouped[s][:, c0 + share : c1, :], in_=src[:, share:, :])
+
+        def quantize_tokens(s):
+            for c0, c1 in QCOLS[0] + QCOLS[1]:
+                nc.vector.quantize_mx(
+                    out=x_words[s][:, c0:c1].bitcast(E4M3),
+                    scales=x_scales[s][:, c0:c1],
+                    in_=grouped[s][:, c0:c1, :].rearrange("p w j -> p (w j)"),
+                )
+
+        def gather_tokens(s, j0, j1):
+            e, i0, i1 = j0 // C, j0 % C, (j1 - 1) % C + 1
+            lists = offsets[:, j0 // 16 : j1 // 16]
+            nc.vector.tensor_copy(out=g_words[s, e][:, i0:i1], in_=x_words[s][:].indirect(lists))
+            nc.vector.tensor_copy(out=g_scales[s, e][:, i0:i1], in_=x_scales[s][:].indirect(lists))
+
+        group_tokens(0)
+        quantize_tokens(0)
+        gather_tokens(0, 0, C)
+        gather_tokens(0, C, S)
+        group_tokens(1)
+        quantize_tokens(1)
+        gather_tokens(1, 0, P)
+        gather_tokens(1, P, C)
+        gather_tokens(1, C, S)
+
+        def first_product(st):
+            e, c0 = st // 2, (st % 2) * P
+            relus = []
+            banks = [ps_a.tile([P, 512], F32, name="bank_a") for g in range(HP)]
+            for s in range(KP):
+                for g in range(HP):
+                    nc.tensor.matmul_mx(
+                        out=banks[g][:],
+                        lhsT=g_words[s, e][:, c0 : c0 + P].bitcast(E4M3),
+                        lhsT_scale=g_scales[s, e][:, c0 : c0 + P],
+                        rhs=w1w[e][:, s, g * 1024 : (g + 1) * 1024].bitcast(E2M1),
+                        rhs_scale=w1s[:, e * KP + s, g * 512 : (g + 1) * 512],
+                        start=(s == 0),
+                        stop=(s == KP - 1),
+                    )
+            for g in range(HP):
+                r = work.tile([P, 4, P], F32, name=f"relu{g}")
+                src = banks[g][:].rearrange("p (m t) -> p t m", t=4)
+                nc.scalar.activation(r[:], src, ACT.Relu)
+                relus.append(r)
+            return relus
+
+        def turn_and_square(st, relus):
+            h = keep.tile([P, HP, P, 4], BF16, name="h", tag=H_SLOT[st], align_bytes=64)
+            for g in range(HP):
+                bank = ps_t.tile([P, 4, P], F32, name="bank_t")
+                for t in range(4):
+                    nc.tensor.transpose(bank[:, t, :], relus[g][:, t, :], ident[:])
+                nc.scalar.activation(h[:, g, :, :], bank[:].rearrange("p t c -> p c t"), ACT.Square)
+            return h
+
+        def quantize_hidden(h):
+            h_words = work.tile([P, HP, P], U32, name="h_words", align_bytes=64)
+            h_scales = work.tile([P, HP, P], U8, name="h_scales", align_bytes=64)
+            nc.vector.quantize_mx(
+                out=h_words[:].rearrange("p g c -> p (g c)").bitcast(E4M3),
+                scales=h_scales[:].rearrange("p g c -> p (g c)"),
+                in_=h[:].rearrange("p g c t -> p (g c t)"),
+            )
+            return h_words, h_scales
+
+        def second_product(st, h_words, h_scales):
+            e = st // 2
+            bank = ps_y.tile([P, NT, P], F32, name="bank_y")
+            for n in range(NT):
+                for g in range(HP):
+                    nc.tensor.matmul_mx(
+                        out=bank[:, n, :],
+                        lhsT=w2w[:, e * HP + g, 256 * n : 256 * (n + 1)].bitcast(E2M1),
+                        lhsT_scale=w2s[:, e * HP + g, P * n : P * (n + 1)],
+                        rhs=h_words[:, g, :].bitcast(E4M3),
+                        rhs_scale=h_scales[:, g, :],
+                        start=(g == 0),
+                        stop=(g == HP - 1),
+                    )
+            return bank
+
+        def empty(st, bank):
+            first = keep.tile([P, 1, P], F32, name=f"y_first{st}")
+            rest = keep.tile([P, NT - 1, P], F32, name="y_rest", tag=Y_SLOT[st], align_bytes=64)
+            nc.scalar.activation(first[:], bank[:, 0:1, :], ACT.Copy)
+            nc.scalar.activation(rest[:], bank[:, 1:NT, :], ACT.Copy)
+            return [first[:, 0, :], rest[:, 0, :], rest[:, 1, :]]
+
+        def scatter(j0, j1, y, n):
+            nc.vector.tensor_tensor(
+                windows[n][:].indirect(offsets[:, j0 // 16 : j1 // 16]), y[n], gates[:, n, j0:j1], ALU.mult
+            )
+
+        def hidden(st, relus):
+            return second_product(st, *quantize_hidden(turn_and_square(st, relus)))
+
+        def scatter_all(st, y):
+            for n in range(NT):
+                scatter(st * P, (st + 1) * P, y, n)
+
+        relus = [first_product(0), first_product(1)]
+        banks = [hidden(0, relus[0]), hidden(1, relus[1])]
+        relus.append(first_product(2))
+        scatter_all(0, empty(0, banks[0]))
+        banks.append(hidden(2, relus[2]))
+        relus.append(first_product(3))
+        scatter_all(1, empty(1, banks[1]))
+        banks.append(hidden(3, relus[3]))
+        scatter_all(2, empty(2, banks[2]))
+        y = empty(3, banks[3])
+
+        def finish(n, c0, c1):
+            nc.vector.tensor_add(out=residual[n][:, c0:c1], in0=windows[n][:, c0:c1], in1=residual[n][:, c0:c1])
+            nc.sync.dma_start(out=out[n * P : (n + 1) * P, c0:c1], in_=residual[n][:, c0:c1])
+
+        scatter(S - P, S, y, 0)
+        scatter(S - P, S, y, 1)
+        finish(0, 0, T)
+        scatter(S - P, S, y, 2)
+        finish(1, 0, T)
+        finish(2, 0, T // 2)
+        finish(2, T // 2, T)

@@ -24,136 +24,165 @@ HP = H // 512
 ST = S // P
 NT = N // P
 
-CHUNKS = (((0, 640),), ((0, 384), (384, 640)))
-SCALAR_SHARE = {(0, 0): 256, (1, 0): 384, (1, 1): 128}
-QCOLS = (((0, 256), (256, 384)), ((384, 640),))
-H_SLOT = ("h0", "h1", "h2", "h3")
-Y_SLOT = ("h1", "h2", "h3", "y3")
+CHUNKS = (((0, 320), (320, 640)), ((0, 256), (256, 640)))
+PIECES = (((0, 256, 64), (256, 320, 64), (320, 384, 0), (384, 640, 192)), ((0, 256, 256), (256, 384, 0), (384, 640, 192)))
+SUM_BANK = ((0, 1), (2, 3), (0, 1), (4, 5))
+TURN_BANK = ((4, 5), (6, 7), (4, 5), (6, 7))
+OUT_BANK = (3, 1, 5, 0)
+RELU_ON_VECTOR = ((1, 1), (2, 0))
+SLOT = 2048
 
 
 def tile_moe_res_mlp_relu2_kernel(tc, xT, xr, w1_words, w1_scales, w2_words, w2_scales, gate, offs, out):
     nc = tc.nc
     with ExitStack() as ctx:
         keep = ctx.enter_context(tc.tile_pool(name="keep", bufs=1))
+        shared = ctx.enter_context(tc.tile_pool(name="shared", bufs=1))
         work = ctx.enter_context(tc.tile_pool(name="work", bufs=3))
-        ps_a = ctx.enter_context(tc.psum_pool(name="ps_a", bufs=3))
-        ps_t = ctx.enter_context(tc.psum_pool(name="ps_t", bufs=2))
-        ps_y = ctx.enter_context(tc.psum_pool(name="ps_y", bufs=3))
+        ps_m = ctx.enter_context(tc.psum_pool(name="ps_m", bufs=1))
 
         offsets = keep.tile([P, S // 16], U16, name="offsets")
 
-        raw = {}
-        for s in range(KP):
-            rows = xT[s * 512 : (s + 1) * 512, :].rearrange("(q j) w -> q j w", j=4)
-            for c, (c0, c1) in enumerate(CHUNKS[s]):
-                t = keep.tile([P, 4, c1 - c0], F32, name=f"raw{s}_{c}")
-                nc.sync.dma_start(out=t[:], in_=rows[:, :, c0:c1])
-                raw[s, c] = t
-            if s == 0:
-                nc.sync.dma_start(offsets[:], offs)
-
-        ident = keep.tile([P, P], F32, name="ident")
-        make_identity(nc, ident[:])
-        x_scales = [keep.tile([P, T], U8, name=f"x_scales{s}", align_bytes=64) for s in range(KP)]
-        for s in range(KP):
-            nc.gpsimd.memset(x_scales[s][:], 0)
-        w1s = keep.tile([P, E * KP, H], U8, name="w1s", align_bytes=64)
+        w1s = [keep.tile([P, KP, H], U8, name=f"w1s{e}", align_bytes=64) for e in range(E)]
         w2s = keep.tile([P, E * HP, N], U8, name="w2s", align_bytes=64)
-        nc.vector.memset(w1s[:].rearrange("p g i -> p (g i)").bitcast(I32), 0)
-        nc.vector.memset(w2s[:].rearrange("p g i -> p (g i)").bitcast(I32), 0)
         warm = keep.tile([P, 1], F32, name="warm")
         nc.vector.memset(warm[:], 0.0)
         nc.scalar.activation(warm[:], warm[:], ACT.Square)
+        nc.gpsimd.memset(w2s[:].rearrange("p g i -> p (g i)").bitcast(I32), 0)
+        for e in range(E):
+            nc.vector.memset(w1s[e][:].rearrange("p g i -> p (g i)").bitcast(I32), 0)
+        x_scales = [keep.tile([P, T], U8, name=f"x_scales{s}", align_bytes=64) for s in range(KP)]
+        for s in range(KP):
+            nc.vector.memset(x_scales[s][:].bitcast(I32), 0)
+        ident = keep.tile([P, P], F32, name="ident")
+        make_identity(nc, ident[:])
         windows = [keep.tile([P, T], F32, name=f"window{n}") for n in range(NT)]
         for n in range(NT):
             nc.vector.memset(windows[n][:], 0.0)
 
-        w1s_rows = w1_scales.bitcast(I32).rearrange("e s q i -> q (e s) i")
-        w2s_rows = w2_scales.bitcast(I32).rearrange("e s q i -> q (e s) i")
-        for q in range(4):
-            nc.sync.dma_start(out=w1s[32 * q : 32 * q + 4, :, :].bitcast(I32), in_=w1s_rows[4 * q : 4 * q + 4, :, :])
+        raw = {}
+        for s in range(KP):
+            rows = xT[s * 512 : (s + 1) * 512, :].rearrange("(q j) w -> q j w", j=4)
+            for c0, c1 in CHUNKS[s]:
+                t = keep.tile([P, 4, c1 - c0], F32, name=f"raw{s}_{c0}")
+                nc.sync.dma_start(out=t[:], in_=rows[:, :, c0:c1])
+                raw[s, c0] = t
+            if s == 0:
+                nc.sync.dma_start(offsets[:], offs)
 
-        w1w = [keep.tile([P, KP, 2 * H], U8, name=f"w1w{e}", align_bytes=64) for e in range(E)]
+        def load_scales(plane, rows, queue):
+            for r in range(4):
+                queue.dma_start(out=plane[r:P:32, :, :].bitcast(I32), in_=rows[r])
+
+        w1s_rows = w1_scales.bitcast(I32).rearrange("e s (a r) i -> e r a s i", r=4)
+        w2s_rows = w2_scales.bitcast(I32).rearrange("e s (a r) i -> r a (e s) i", r=4)
         w1_rows = w1_words.bitcast(I32).rearrange("e s p w -> e p s w")
+        w1w = [keep.tile([P, KP, 2 * H], U8, name=f"w1w{e}", align_bytes=64) for e in range(E)]
+        load_scales(w2s, w2s_rows, nc.gpsimd)
         for e in range(E):
+            load_scales(w1s[e], w1s_rows[e], nc.sync)
             nc.sync.dma_start(out=w1w[e][:].bitcast(I32), in_=w1_rows[e])
-        for q in range(4):
-            nc.sync.dma_start(out=w2s[32 * q : 32 * q + 4, :, :].bitcast(I32), in_=w2s_rows[4 * q : 4 * q + 4, :, :])
         w2w = keep.tile([P, E * HP, 2 * N], U8, name="w2w", align_bytes=64)
         nc.sync.dma_start(out=w2w[:].bitcast(I32), in_=w2_words.bitcast(I32).rearrange("e s p w -> p (e s) w"))
-        gates = keep.tile([P, NT, S], F32, name="gates")
-        nc.sync.dma_start(out=gates[:], in_=gate.rearrange("(n p) s -> p n s", p=P))
+        gates = keep.tile([P, S], F32, name="gates")
+        nc.sync.dma_start(out=gates[:], in_=gate[0:P, :])
         residual = [keep.tile([P, T], F32, name=f"residual{n}") for n in range(NT)]
         for n in range(NT):
             nc.sync.dma_start(out=residual[n][:], in_=xr[n * P : (n + 1) * P, :])
 
-        grouped = [keep.tile([P, T, 4], BF16, name=f"grouped{s}", align_bytes=64) for s in range(KP)]
         x_words = [keep.tile([P, T], U32, name=f"x_words{s}", align_bytes=64) for s in range(KP)]
+
+        def interleave(dst, src, c0, c1, on_scalar):
+            d = dst.rearrange("p (c i) t -> p c t i", i=4)
+            r = src[:, :, c0:c1].rearrange("p t (c i) -> p c t i", i=4)
+            if on_scalar:
+                nc.scalar.activation(d, r, ACT.Copy)
+            else:
+                nc.vector.tensor_copy(out=d, in_=r)
+
+        def group_tokens(s, piece):
+            c0, c1, share = PIECES[s][piece]
+            base = max(b0 for b0, b1 in CHUNKS[s] if b0 <= c0)
+            if (s, c1) == (KP - 1, T):
+                grouped = shared.tile([P, c1 - c0, 4], BF16, name="grouped_last", align_bytes=64, offset=0)
+            else:
+                grouped = keep.tile([P, c1 - c0, 4], BF16, name=f"grouped{s}_{piece}", align_bytes=64)
+            cut = c1 - share
+            if share > 0:
+                interleave(grouped[:, cut - c0 :, :], raw[s, base], cut - base, c1 - base, True)
+            if cut > c0:
+                interleave(grouped[:, : cut - c0, :], raw[s, base], c0 - base, cut - base, False)
+            return grouped
+
+        def quantize_tokens(s, piece, grouped):
+            c0, c1, share = PIECES[s][piece]
+            nc.vector.quantize_mx(
+                out=x_words[s][:, c0:c1].bitcast(E4M3),
+                scales=x_scales[s][:, c0:c1],
+                in_=grouped[:].rearrange("p w j -> p (w j)"),
+            )
+
         g_words = {}
         g_scales = {}
-        for s in range(KP):
-            for e in range(E):
-                g_words[s, e] = keep.tile([P, C], U32, name=f"g_words{s}_{e}", align_bytes=64)
-                g_scales[s, e] = keep.tile([P, C], U8, name=f"g_scales{s}_{e}", align_bytes=64)
 
-        def group_tokens(s):
-            for c, (c0, c1) in enumerate(CHUNKS[s]):
-                src = raw[s, c][:].rearrange("p j w -> p w j")
-                share = SCALAR_SHARE[s, c]
-                nc.scalar.activation(grouped[s][:, c0 : c0 + share, :], src[:, :share, :], ACT.Copy)
-                if c0 + share < c1:
-                    nc.vector.tensor_copy(out=grouped[s][:, c0 + share : c1, :], in_=src[:, share:, :])
+        def gather_tokens(s, st0, st1, place=None):
+            width = (st1 - st0) * P
+            if place is None:
+                words = keep.tile([P, width], U32, name=f"g_words{s}_{st0}", align_bytes=64)
+                scales = keep.tile([P, width], U8, name=f"g_scales{s}_{st0}", align_bytes=64)
+            else:
+                words = shared.tile([P, width], U32, name=f"g_words{s}_{st0}", align_bytes=64, offset=place)
+                scales = shared.tile([P, width], U8, name=f"g_scales{s}_{st0}", align_bytes=64, offset=place + 4 * width)
+            lists = offsets[:, st0 * P // 16 : st1 * P // 16]
+            nc.vector.tensor_copy(out=words[:], in_=x_words[s][:].indirect(lists))
+            nc.vector.tensor_copy(out=scales[:], in_=x_scales[s][:].indirect(lists))
+            for st in range(st0, st1):
+                g_words[s, st] = words[:, (st - st0) * P : (st - st0 + 1) * P]
+                g_scales[s, st] = scales[:, (st - st0) * P : (st - st0 + 1) * P]
 
-        def quantize_tokens(s):
-            for c0, c1 in QCOLS[0] + QCOLS[1]:
-                nc.vector.quantize_mx(
-                    out=x_words[s][:, c0:c1].bitcast(E4M3),
-                    scales=x_scales[s][:, c0:c1],
-                    in_=grouped[s][:, c0:c1, :].rearrange("p w j -> p (w j)"),
-                )
+        def relu_place(st, g):
+            return SLOT * (1 + HP * st + g)
 
-        def gather_tokens(s, j0, j1):
-            e, i0, i1 = j0 // C, j0 % C, (j1 - 1) % C + 1
-            lists = offsets[:, j0 // 16 : j1 // 16]
-            nc.vector.tensor_copy(out=g_words[s, e][:, i0:i1], in_=x_words[s][:].indirect(lists))
-            nc.vector.tensor_copy(out=g_scales[s, e][:, i0:i1], in_=x_scales[s][:].indirect(lists))
+        def sum_bank(st, g):
+            return f"bank{SUM_BANK[st][g]}"
 
-        group_tokens(0)
-        quantize_tokens(0)
-        gather_tokens(0, 0, C)
-        gather_tokens(0, C, S)
-        group_tokens(1)
-        quantize_tokens(1)
-        gather_tokens(1, 0, P)
-        gather_tokens(1, P, C)
-        gather_tokens(1, C, S)
+        def first_pass(st, s, g, bank):
+            e = st // 2
+            nc.tensor.matmul_mx(
+                out=bank[:],
+                lhsT=g_words[s, st].bitcast(E4M3),
+                lhsT_scale=g_scales[s, st],
+                rhs=w1w[e][:, s, g * 1024 : (g + 1) * 1024].bitcast(E2M1),
+                rhs_scale=w1s[e][:, s, g * 512 : (g + 1) * 512],
+                start=(s == 0),
+                stop=(s == KP - 1),
+            )
 
         def first_product(st):
-            e, c0 = st // 2, (st % 2) * P
-            relus = []
-            banks = [ps_a.tile([P, 512], F32, name="bank_a") for g in range(HP)]
-            for s in range(KP):
-                for g in range(HP):
-                    nc.tensor.matmul_mx(
-                        out=banks[g][:],
-                        lhsT=g_words[s, e][:, c0 : c0 + P].bitcast(E4M3),
-                        lhsT_scale=g_scales[s, e][:, c0 : c0 + P],
-                        rhs=w1w[e][:, s, g * 1024 : (g + 1) * 1024].bitcast(E2M1),
-                        rhs_scale=w1s[:, e * KP + s, g * 512 : (g + 1) * 512],
-                        start=(s == 0),
-                        stop=(s == KP - 1),
-                    )
+            banks = []
             for g in range(HP):
-                r = work.tile([P, 4, P], F32, name=f"relu{g}")
-                src = banks[g][:].rearrange("p (m t) -> p t m", t=4)
-                nc.scalar.activation(r[:], src, ACT.Relu)
-                relus.append(r)
-            return relus
+                bank = ps_m.tile([P, 512], F32, name="bank_a", tag=sum_bank(st, g))
+                for s in range(KP):
+                    first_pass(st, s, g, bank)
+                banks.append(bank)
+            return banks
 
-        def turn_and_square(st, relus):
-            h = keep.tile([P, HP, P, 4], BF16, name="h", tag=H_SLOT[st], align_bytes=64)
+        def relu(st, g, bank, on_scalar=True):
+            r = shared.tile([P, 4, P], F32, name=f"relu{st}_{g}", align_bytes=64, offset=relu_place(st, g))
+            src = bank[:].rearrange("p (m t) -> p t m", t=4)
+            if on_scalar:
+                nc.scalar.activation(r[:], src, ACT.Relu)
+            else:
+                nc.vector.tensor_scalar_max(r[:], src, 0.0)
+            return r
+
+        def turn_and_square(st, relus, place=None):
+            if place is None:
+                h = work.tile([P, HP, P, 4], BF16, name="h", align_bytes=64)
+            else:
+                h = shared.tile([P, HP, P, 4], BF16, name="h_first", align_bytes=64, offset=place)
             for g in range(HP):
-                bank = ps_t.tile([P, 4, P], F32, name="bank_t")
+                bank = ps_m.tile([P, 4, P], F32, name="bank_t", tag=f"bank{TURN_BANK[st][g]}")
                 for t in range(4):
                     nc.tensor.transpose(bank[:, t, :], relus[g][:, t, :], ident[:])
                 nc.scalar.activation(h[:, g, :, :], bank[:].rearrange("p t c -> p c t"), ACT.Square)
@@ -171,7 +200,7 @@ def tile_moe_res_mlp_relu2_kernel(tc, xT, xr, w1_words, w1_scales, w2_words, w2_
 
         def second_product(st, h_words, h_scales):
             e = st // 2
-            bank = ps_y.tile([P, NT, P], F32, name="bank_y")
+            bank = ps_m.tile([P, NT, P], F32, name="bank_y", tag=f"bank{OUT_BANK[st]}")
             for n in range(NT):
                 for g in range(HP):
                     nc.tensor.matmul_mx(
@@ -186,43 +215,63 @@ def tile_moe_res_mlp_relu2_kernel(tc, xT, xr, w1_words, w1_scales, w2_words, w2_
             return bank
 
         def empty(st, bank):
-            first = keep.tile([P, 1, P], F32, name=f"y_first{st}")
-            rest = keep.tile([P, NT - 1, P], F32, name="y_rest", tag=Y_SLOT[st], align_bytes=64)
-            nc.scalar.activation(first[:], bank[:, 0:1, :], ACT.Copy)
-            nc.scalar.activation(rest[:], bank[:, 1:NT, :], ACT.Copy)
-            return [first[:, 0, :], rest[:, 0, :], rest[:, 1, :]]
+            if st + 1 < ST:
+                y = shared.tile([P, NT, P], F32, name="y", tag=f"y{st}", align_bytes=64, offset=relu_place(st + 1, HP - 1))
+            else:
+                y = keep.tile([P, NT, P], F32, name="y_last")
+            nc.scalar.activation(y[:], bank[:], ACT.Copy)
+            return y
 
-        def scatter(j0, j1, y, n):
+        def scatter(st, y, n):
             nc.vector.tensor_tensor(
-                windows[n][:].indirect(offsets[:, j0 // 16 : j1 // 16]), y[n], gates[:, n, j0:j1], ALU.mult
+                windows[n][:].indirect(offsets[:, st * P // 16 : (st + 1) * P // 16]),
+                y[:, n, :],
+                gates[:, st * P : (st + 1) * P],
+                ALU.mult,
             )
-
-        def hidden(st, relus):
-            return second_product(st, *quantize_hidden(turn_and_square(st, relus)))
-
-        def scatter_all(st, y):
-            for n in range(NT):
-                scatter(st * P, (st + 1) * P, y, n)
-
-        relus = [first_product(0), first_product(1)]
-        banks = [hidden(0, relus[0]), hidden(1, relus[1])]
-        relus.append(first_product(2))
-        scatter_all(0, empty(0, banks[0]))
-        banks.append(hidden(2, relus[2]))
-        relus.append(first_product(3))
-        scatter_all(1, empty(1, banks[1]))
-        banks.append(hidden(3, relus[3]))
-        scatter_all(2, empty(2, banks[2]))
-        y = empty(3, banks[3])
 
         def finish(n, c0, c1):
             nc.vector.tensor_add(out=residual[n][:, c0:c1], in0=windows[n][:, c0:c1], in1=residual[n][:, c0:c1])
             nc.sync.dma_start(out=out[n * P : (n + 1) * P, c0:c1], in_=residual[n][:, c0:c1])
 
-        scatter(S - P, S, y, 0)
-        scatter(S - P, S, y, 1)
+        grouped = [group_tokens(0, piece) for piece in range(len(PIECES[0]))]
+        for piece in range(len(PIECES[0])):
+            quantize_tokens(0, piece, grouped[piece])
+        gather_tokens(0, 0, 2)
+        banks0 = [ps_m.tile([P, 512], F32, name="bank_a", tag=sum_bank(0, g)) for g in range(HP)]
+        for g in range(HP):
+            first_pass(0, 0, g, banks0[g])
+        grouped = [group_tokens(1, piece) for piece in range(len(PIECES[1]))]
+        for piece in range(len(PIECES[1])):
+            quantize_tokens(1, piece, grouped[piece])
+        gather_tokens(1, 0, 1)
+        for g in range(HP):
+            first_pass(0, 1, g, banks0[g])
+        gather_tokens(1, 1, 2)
+        banks1 = first_product(1)
+        relus0 = [relu(0, g, banks0[g], (0, g) not in RELU_ON_VECTOR) for g in range(HP)]
+        gather_tokens(0, 2, 3, 0)
+        gather_tokens(1, 2, 3)
+        relus = [relu(1, g, banks1[g], (1, g) not in RELU_ON_VECTOR) for g in range(HP)]
+        h = turn_and_square(0, relus0, SLOT * (1 + HP * ST))
+        gather_tokens(0, 3, 4, relu_place(0, 0))
+        gather_tokens(1, 3, 4, relu_place(0, 0) + 5 * P)
+        codes = quantize_hidden(h)
+        for st in range(1, ST):
+            h = turn_and_square(st, relus)
+            bank_y = second_product(st - 1, *codes)
+            codes = quantize_hidden(h)
+            y = empty(st - 1, bank_y)
+            if st + 1 < ST:
+                banks = first_product(st + 1)
+                relus = [relu(st + 1, g, banks[g], (st + 1, g) not in RELU_ON_VECTOR) for g in range(HP)]
+            for n in range(NT):
+                scatter(st - 1, y, n)
+        y = empty(ST - 1, second_product(ST - 1, *codes))
+        scatter(ST - 1, y, 0)
+        scatter(ST - 1, y, 1)
         finish(0, 0, T)
-        scatter(S - P, S, y, 2)
+        scatter(ST - 1, y, 2)
         finish(1, 0, T)
         finish(2, 0, T // 2)
         finish(2, T // 2, T)

@@ -26,9 +26,10 @@ NT = N // P
 
 CHUNKS = (((0, 320), (320, 640)), ((0, 256), (256, 640)))
 PIECES = (((0, 256, 64), (256, 320, 64), (320, 384, 0), (384, 640, 192)), ((0, 256, 256), (256, 384, 0), (384, 640, 192)))
-SUM_BANK = ((0, 1), (2, 3), (0, 1), (4, 5))
-TURN_BANK = ((4, 5), (6, 7), (4, 5), (6, 7))
-OUT_BANK = (3, 1, 5, 0)
+SUM_BANK = ((0, 1), (2, 3), (0, 1), (4, 4))
+TURN_BANK = ((4, 5), (6, 7), (3, 5), (6, 7))
+OUT_BANK = (((4, 0, 1), (3, 1, 3)), ((1, 0, 3),), ((4, 0, 3),), ((0, 0, 3),))
+W1_LOADS = (((0, 1), (1, 2)), ((0, 2),))
 RELU_ON_VECTOR = ((1, 1), (2, 0))
 SLOT = 2048
 
@@ -48,9 +49,9 @@ def tile_moe_res_mlp_relu2_kernel(tc, xT, xr, w1_words, w1_scales, w2_words, w2_
         warm = keep.tile([P, 1], F32, name="warm")
         nc.vector.memset(warm[:], 0.0)
         nc.scalar.activation(warm[:], warm[:], ACT.Square)
-        nc.gpsimd.memset(w2s[:].rearrange("p g i -> p (g i)").bitcast(I32), 0)
         for e in range(E):
             nc.vector.memset(w1s[e][:].rearrange("p g i -> p (g i)").bitcast(I32), 0)
+        nc.vector.memset(w2s[:].rearrange("p g i -> p (g i)").bitcast(I32), 0)
         x_scales = [keep.tile([P, T], U8, name=f"x_scales{s}", align_bytes=64) for s in range(KP)]
         for s in range(KP):
             nc.vector.memset(x_scales[s][:].bitcast(I32), 0)
@@ -77,15 +78,20 @@ def tile_moe_res_mlp_relu2_kernel(tc, xT, xr, w1_words, w1_scales, w2_words, w2_
         w1s_rows = w1_scales.bitcast(I32).rearrange("e s (a r) i -> e r a s i", r=4)
         w2s_rows = w2_scales.bitcast(I32).rearrange("e s (a r) i -> r a (e s) i", r=4)
         w1_rows = w1_words.bitcast(I32).rearrange("e s p w -> e p s w")
-        w1w = [keep.tile([P, KP, 2 * H], U8, name=f"w1w{e}", align_bytes=64) for e in range(E)]
-        load_scales(w2s, w2s_rows, nc.gpsimd)
+        w1w = []
         for e in range(E):
             load_scales(w1s[e], w1s_rows[e], nc.sync)
-            nc.sync.dma_start(out=w1w[e][:].bitcast(I32), in_=w1_rows[e])
-        w2w = keep.tile([P, E * HP, 2 * N], U8, name="w2w", align_bytes=64)
-        nc.sync.dma_start(out=w2w[:].bitcast(I32), in_=w2_words.bitcast(I32).rearrange("e s p w -> p (e s) w"))
+            words = []
+            for s0, s1 in W1_LOADS[e]:
+                t = keep.tile([P, s1 - s0, 2 * H], U8, name=f"w1w{e}_{s0}", align_bytes=64)
+                nc.sync.dma_start(out=t[:].bitcast(I32), in_=w1_rows[e, :, s0:s1, :])
+                words.extend(t[:, s, :] for s in range(s1 - s0))
+            w1w.append(words)
         gates = keep.tile([P, S], F32, name="gates")
         nc.sync.dma_start(out=gates[:], in_=gate[0:P, :])
+        load_scales(w2s, w2s_rows, nc.sync)
+        w2w = keep.tile([P, E * HP, 2 * N], U8, name="w2w", align_bytes=64)
+        nc.sync.dma_start(out=w2w[:].bitcast(I32), in_=w2_words.bitcast(I32).rearrange("e s p w -> p (e s) w"))
         residual = [keep.tile([P, T], F32, name=f"residual{n}") for n in range(NT)]
         for n in range(NT):
             nc.sync.dma_start(out=residual[n][:], in_=xr[n * P : (n + 1) * P, :])
@@ -152,7 +158,7 @@ def tile_moe_res_mlp_relu2_kernel(tc, xT, xr, w1_words, w1_scales, w2_words, w2_
                 out=bank[:],
                 lhsT=g_words[s, st].bitcast(E4M3),
                 lhsT_scale=g_scales[s, st],
-                rhs=w1w[e][:, s, g * 1024 : (g + 1) * 1024].bitcast(E2M1),
+                rhs=w1w[e][s][:, g * 1024 : (g + 1) * 1024].bitcast(E2M1),
                 rhs_scale=w1s[e][:, s, g * 512 : (g + 1) * 512],
                 start=(s == 0),
                 stop=(s == KP - 1),
@@ -188,8 +194,11 @@ def tile_moe_res_mlp_relu2_kernel(tc, xT, xr, w1_words, w1_scales, w2_words, w2_
                 nc.scalar.activation(h[:, g, :, :], bank[:].rearrange("p t c -> p c t"), ACT.Square)
             return h
 
-        def quantize_hidden(h):
-            h_words = work.tile([P, HP, P], U32, name="h_words", align_bytes=64)
+        def quantize_hidden(h, place=None):
+            if place is None:
+                h_words = work.tile([P, HP, P], U32, name="h_words", align_bytes=64)
+            else:
+                h_words = shared.tile([P, HP, P], U32, name="h_words_first", align_bytes=64, offset=place)
             h_scales = work.tile([P, HP, P], U8, name="h_scales", align_bytes=64)
             nc.vector.quantize_mx(
                 out=h_words[:].rearrange("p g c -> p (g c)").bitcast(E4M3),
@@ -200,32 +209,38 @@ def tile_moe_res_mlp_relu2_kernel(tc, xT, xr, w1_words, w1_scales, w2_words, w2_
 
         def second_product(st, h_words, h_scales):
             e = st // 2
-            bank = ps_m.tile([P, NT, P], F32, name="bank_y", tag=f"bank{OUT_BANK[st]}")
-            for n in range(NT):
-                for g in range(HP):
-                    nc.tensor.matmul_mx(
-                        out=bank[:, n, :],
-                        lhsT=w2w[:, e * HP + g, 256 * n : 256 * (n + 1)].bitcast(E2M1),
-                        lhsT_scale=w2s[:, e * HP + g, P * n : P * (n + 1)],
-                        rhs=h_words[:, g, :].bitcast(E4M3),
-                        rhs_scale=h_scales[:, g, :],
-                        start=(g == 0),
-                        stop=(g == HP - 1),
-                    )
-            return bank
+            parts = []
+            for bank_no, n0, n1 in OUT_BANK[st]:
+                bank = ps_m.tile([P, n1 - n0, P], F32, name="bank_y", tag=f"bank{bank_no}")
+                for n in range(n0, n1):
+                    for g in range(HP):
+                        nc.tensor.matmul_mx(
+                            out=bank[:, n - n0, :],
+                            lhsT=w2w[:, e * HP + g, 256 * n : 256 * (n + 1)].bitcast(E2M1),
+                            lhsT_scale=w2s[:, e * HP + g, P * n : P * (n + 1)],
+                            rhs=h_words[:, g, :].bitcast(E4M3),
+                            rhs_scale=h_scales[:, g, :],
+                            start=(g == 0),
+                            stop=(g == HP - 1),
+                        )
+                parts.append((bank, n0, n1))
+            return parts
 
-        def empty(st, bank):
-            if st + 1 < ST:
-                y = shared.tile([P, NT, P], F32, name="y", tag=f"y{st}", align_bytes=64, offset=relu_place(st + 1, HP - 1))
-            else:
-                y = keep.tile([P, NT, P], F32, name="y_last")
-            nc.scalar.activation(y[:], bank[:], ACT.Copy)
-            return y
+        def empty(st, parts):
+            rows = []
+            for bank, n0, n1 in parts:
+                if st + 1 < ST:
+                    y = shared.tile([P, n1 - n0, P], F32, name=f"y{st}_{n0}", align_bytes=64, offset=relu_place(st + 1, HP - 1) + 4 * P * n0)
+                else:
+                    y = keep.tile([P, n1 - n0, P], F32, name=f"y_last{n0}")
+                nc.scalar.activation(y[:], bank[:], ACT.Copy)
+                rows.extend(y[:, n, :] for n in range(n1 - n0))
+            return rows
 
         def scatter(st, y, n):
             nc.vector.tensor_tensor(
                 windows[n][:].indirect(offsets[:, st * P // 16 : (st + 1) * P // 16]),
-                y[:, n, :],
+                y[n],
                 gates[:, st * P : (st + 1) * P],
                 ALU.mult,
             )
@@ -256,7 +271,7 @@ def tile_moe_res_mlp_relu2_kernel(tc, xT, xr, w1_words, w1_scales, w2_words, w2_
         h = turn_and_square(0, relus0, SLOT * (1 + HP * ST))
         gather_tokens(0, 3, 4, relu_place(0, 0))
         gather_tokens(1, 3, 4, relu_place(0, 0) + 5 * P)
-        codes = quantize_hidden(h)
+        codes = quantize_hidden(h, relu_place(2, 1))
         for st in range(1, ST):
             h = turn_and_square(st, relus)
             bank_y = second_product(st - 1, *codes)

@@ -24,11 +24,11 @@ HP = H // 512
 ST = S // P
 NT = N // P
 
-CHUNKS = (((0, 320), (320, 640)), ((0, 256), (256, 640)))
-PIECES = (((0, 256, 64), (256, 320, 64), (320, 384, 0), (384, 640, 192)), ((0, 256, 256), (256, 384, 0), (384, 640, 192)))
+CHUNKS = (((0, 640),), ((0, 384), (384, 640)))
+PIECES = (((0, 256, 0), (256, 384, 0), (384, 640, 256)), ((0, 256, 256), (256, 384, 128), (384, 640, 64)))
 SUM_BANK = ((0, 1), (2, 3), (0, 1), (4, 4))
 TURN_BANK = ((4, 5), (6, 7), (3, 5), (6, 7))
-OUT_BANK = (((4, 0, 1), (3, 1, 3)), ((1, 0, 3),), ((4, 0, 3),), ((0, 0, 3),))
+OUT_BANK = (((4, 0, 1), (3, 1, 3)), ((1, 0, 3),), ((4, 0, 2), (6, 2, 3)), ((0, 0, 2), (0, 2, 3)))
 W1_LOADS = (((0, 1), (1, 2)), ((0, 2),))
 RELU_ON_VECTOR = ((1, 1), (2, 0))
 SLOT = 2048
@@ -62,34 +62,39 @@ def tile_moe_res_mlp_relu2_kernel(tc, xT, xr, w1_words, w1_scales, w2_words, w2_
             nc.vector.memset(windows[n][:], 0.0)
 
         raw = {}
-        for s in range(KP):
+
+        def load_tokens(s, part=slice(0, 3)):
             rows = xT[s * 512 : (s + 1) * 512, :].rearrange("(q j) w -> q j w", j=4)
-            for c0, c1 in CHUNKS[s]:
+            for c0, c1 in CHUNKS[s][part]:
                 t = keep.tile([P, 4, c1 - c0], F32, name=f"raw{s}_{c0}")
                 nc.sync.dma_start(out=t[:], in_=rows[:, :, c0:c1])
                 raw[s, c0] = t
-            if s == 0:
-                nc.sync.dma_start(offsets[:], offs)
 
-        def load_scales(plane, rows, queue):
+        def load_scales(plane, rows):
             for r in range(4):
-                queue.dma_start(out=plane[r:P:32, :, :].bitcast(I32), in_=rows[r])
+                nc.sync.dma_start(out=plane[r:P:32, :, :].bitcast(I32), in_=rows[r])
 
         w1s_rows = w1_scales.bitcast(I32).rearrange("e s (a r) i -> e r a s i", r=4)
         w2s_rows = w2_scales.bitcast(I32).rearrange("e s (a r) i -> r a (e s) i", r=4)
         w1_rows = w1_words.bitcast(I32).rearrange("e s p w -> e p s w")
-        w1w = []
-        for e in range(E):
-            load_scales(w1s[e], w1s_rows[e], nc.sync)
-            words = []
-            for s0, s1 in W1_LOADS[e]:
-                t = keep.tile([P, s1 - s0, 2 * H], U8, name=f"w1w{e}_{s0}", align_bytes=64)
-                nc.sync.dma_start(out=t[:].bitcast(I32), in_=w1_rows[e, :, s0:s1, :])
-                words.extend(t[:, s, :] for s in range(s1 - s0))
-            w1w.append(words)
+        w1w = [[], []]
+
+        def load_words(e, s0, s1):
+            t = keep.tile([P, s1 - s0, 2 * H], U8, name=f"w1w{e}_{s0}", align_bytes=64)
+            nc.sync.dma_start(out=t[:].bitcast(I32), in_=w1_rows[e, :, s0:s1, :])
+            w1w[e].extend(t[:, s, :] for s in range(s1 - s0))
+
+        load_tokens(0)
+        nc.sync.dma_start(offsets[:], offs)
+        load_tokens(1)
+        load_scales(w1s[0], w1s_rows[0])
+        load_words(0, 0, 1)
+        load_words(0, 1, 2)
+        load_scales(w1s[1], w1s_rows[1])
+        load_words(1, 0, 2)
         gates = keep.tile([P, S], F32, name="gates")
         nc.sync.dma_start(out=gates[:], in_=gate[0:P, :])
-        load_scales(w2s, w2s_rows, nc.sync)
+        load_scales(w2s, w2s_rows)
         w2w = keep.tile([P, E * HP, 2 * N], U8, name="w2w", align_bytes=64)
         nc.sync.dma_start(out=w2w[:].bitcast(I32), in_=w2_words.bitcast(I32).rearrange("e s p w -> p (e s) w"))
         residual = [keep.tile([P, T], F32, name=f"residual{n}") for n in range(NT)]
@@ -207,10 +212,10 @@ def tile_moe_res_mlp_relu2_kernel(tc, xT, xr, w1_words, w1_scales, w2_words, w2_
             )
             return h_words, h_scales
 
-        def second_product(st, h_words, h_scales):
+        def second_product(st, h_words, h_scales, parts=slice(0, 2)):
             e = st // 2
-            parts = []
-            for bank_no, n0, n1 in OUT_BANK[st]:
+            done = []
+            for bank_no, n0, n1 in OUT_BANK[st][parts]:
                 bank = ps_m.tile([P, n1 - n0, P], F32, name="bank_y", tag=f"bank{bank_no}")
                 for n in range(n0, n1):
                     for g in range(HP):
@@ -223,8 +228,8 @@ def tile_moe_res_mlp_relu2_kernel(tc, xT, xr, w1_words, w1_scales, w2_words, w2_
                             start=(g == 0),
                             stop=(g == HP - 1),
                         )
-                parts.append((bank, n0, n1))
-            return parts
+                done.append((bank, n0, n1))
+            return done
 
         def empty(st, parts):
             rows = []
@@ -237,6 +242,8 @@ def tile_moe_res_mlp_relu2_kernel(tc, xT, xr, w1_words, w1_scales, w2_words, w2_
                 rows.extend(y[:, n, :] for n in range(n1 - n0))
             return rows
 
+        y_tail = keep.tile([P, 2, P], F32, name="y_tail")
+
         def scatter(st, y, n):
             nc.vector.tensor_tensor(
                 windows[n][:].indirect(offsets[:, st * P // 16 : (st + 1) * P // 16]),
@@ -245,9 +252,9 @@ def tile_moe_res_mlp_relu2_kernel(tc, xT, xr, w1_words, w1_scales, w2_words, w2_
                 ALU.mult,
             )
 
-        def finish(n, c0, c1):
+        def finish(n, c0, c1, queue):
             nc.vector.tensor_add(out=residual[n][:, c0:c1], in0=windows[n][:, c0:c1], in1=residual[n][:, c0:c1])
-            nc.sync.dma_start(out=out[n * P : (n + 1) * P, c0:c1], in_=residual[n][:, c0:c1])
+            queue.dma_start(out=out[n * P : (n + 1) * P, c0:c1], in_=residual[n][:, c0:c1])
 
         grouped = [group_tokens(0, piece) for piece in range(len(PIECES[0]))]
         for piece in range(len(PIECES[0])):
@@ -272,21 +279,35 @@ def tile_moe_res_mlp_relu2_kernel(tc, xT, xr, w1_words, w1_scales, w2_words, w2_
         gather_tokens(0, 3, 4, relu_place(0, 0))
         gather_tokens(1, 3, 4, relu_place(0, 0) + 5 * P)
         codes = quantize_hidden(h, relu_place(2, 1))
-        for st in range(1, ST):
+        for st in range(1, ST - 1):
             h = turn_and_square(st, relus)
             bank_y = second_product(st - 1, *codes)
             codes = quantize_hidden(h)
             y = empty(st - 1, bank_y)
-            if st + 1 < ST:
-                banks = first_product(st + 1)
-                relus = [relu(st + 1, g, banks[g], (st + 1, g) not in RELU_ON_VECTOR) for g in range(HP)]
+            banks = first_product(st + 1)
+            relus = [relu(st + 1, g, banks[g], (st + 1, g) not in RELU_ON_VECTOR) for g in range(HP)]
             for n in range(NT):
                 scatter(st - 1, y, n)
-        y = empty(ST - 1, second_product(ST - 1, *codes))
+        h = turn_and_square(ST - 1, relus)
+        parts = second_product(ST - 2, *codes)
+        codes = quantize_hidden(h)
+        y = empty(ST - 2, parts[:1])
+        nc.scalar.activation(y_tail[:, 0:1, :], parts[1][0][:], ACT.Copy)
+        scatter(ST - 2, y, 0)
+        scatter(ST - 2, y, 1)
+        y = empty(ST - 1, second_product(ST - 1, *codes, parts=slice(0, 1)))
+        parts = second_product(ST - 1, *codes, parts=slice(1, 2))
+        nc.scalar.activation(y_tail[:, 1:2, :], parts[0][0][:], ACT.Copy)
         scatter(ST - 1, y, 0)
         scatter(ST - 1, y, 1)
-        finish(0, 0, T)
-        scatter(ST - 1, y, 2)
-        finish(1, 0, T)
-        finish(2, 0, T // 2)
-        finish(2, T // 2, T)
+        finish(0, 0, T, nc.sync)
+        finish(1, 0, 384, nc.sync)
+        nc.vector.tensor_tensor(
+            windows[2][:].indirect(offsets[:, 2 * P // 16 : S // 16]),
+            y_tail[:].rearrange("p t c -> p (t c)"),
+            gates[:, 2 * P : S],
+            ALU.mult,
+        )
+        finish(1, 384, T, nc.sync)
+        finish(2, 0, 448, nc.sync)
+        finish(2, 448, T, nc.sync)

@@ -104,8 +104,8 @@ def tile_moe_res_mlp_relu2_kernel(tc, xT, xr, w1_words, w1_scales, w2_words, w2_
         x_words = [keep.tile([P, T], U32, name=f"x_words{s}", align_bytes=64) for s in range(KP)]
 
         def interleave(dst, src, c0, c1, on_scalar):
-            d = dst.rearrange("p (c i) t -> p c t i", i=4)
-            r = src[:, :, c0:c1].rearrange("p t (c i) -> p c t i", i=4)
+            d = dst
+            r = src[:, :, c0:c1].rearrange("p t c -> p c t")
             if on_scalar:
                 nc.scalar.activation(d, r, ACT.Copy)
             else:
@@ -301,13 +301,13 @@ def tile_moe_res_mlp_relu2_kernel(tc, xT, xr, w1_words, w1_scales, w2_words, w2_
         scatter(ST - 1, y, 0)
         scatter(ST - 1, y, 1)
         finish(0, 0, T, nc.sync)
-        finish(1, 0, 384, nc.sync)
+        finish(1, 0, 448, nc.sync)
         nc.vector.tensor_tensor(
             windows[2][:].indirect(offsets[:, 2 * P // 16 : S // 16]),
             y_tail[:].rearrange("p t c -> p (t c)"),
             gates[:, 2 * P : S],
             ALU.mult,
         )
-        finish(1, 384, T, nc.sync)
-        finish(2, 0, 448, nc.sync)
-        finish(2, 448, T, nc.sync)
+        finish(1, 448, T, nc.sync)
+        finish(2, 0, 320, nc.sync)
+        finish(2, 320, T, nc.sync)

@@ -28,7 +28,7 @@ CHUNKS = (((0, 640),), ((0, 384), (384, 640)))
 PIECES = (((0, 256, 0), (256, 384, 0), (384, 640, 256)), ((0, 256, 256), (256, 384, 128), (384, 640, 64)))
 SUM_BANK = ((0, 1), (2, 3), (0, 1), (4, 4))
 TURN_BANK = ((4, 5), (6, 7), (3, 5), (6, 7))
-OUT_BANK = (((4, 0, 1), (3, 1, 3)), ((1, 0, 3),), ((4, 0, 2), (6, 2, 3)), ((0, 0, 2), (0, 2, 3)))
+OUT_BANK = (((4, 0, 1), (3, 1, 3)), ((1, 0, 3),), ((4, 0, 2), (6, 2, 3)), ((0, 0, 1), (2, 1, 2), (2, 2, 3)))
 W1_LOADS = (((0, 1), (1, 2)), ((0, 2),))
 RELU_ON_VECTOR = ((1, 1), (2, 0))
 SLOT = 2048
@@ -212,7 +212,7 @@ def tile_moe_res_mlp_relu2_kernel(tc, xT, xr, w1_words, w1_scales, w2_words, w2_
             )
             return h_words, h_scales
 
-        def second_product(st, h_words, h_scales, parts=slice(0, 2)):
+        def second_product(st, h_words, h_scales, parts=slice(0, 3)):
             e = st // 2
             done = []
             for bank_no, n0, n1 in OUT_BANK[st][parts]:
@@ -295,8 +295,8 @@ def tile_moe_res_mlp_relu2_kernel(tc, xT, xr, w1_words, w1_scales, w2_words, w2_
         nc.scalar.activation(y_tail[:, 0:1, :], parts[1][0][:], ACT.Copy)
         scatter(ST - 2, y, 0)
         scatter(ST - 2, y, 1)
-        y = empty(ST - 1, second_product(ST - 1, *codes, parts=slice(0, 1)))
-        parts = second_product(ST - 1, *codes, parts=slice(1, 2))
+        y = empty(ST - 1, second_product(ST - 1, *codes, parts=slice(0, 2)))
+        parts = second_product(ST - 1, *codes, parts=slice(2, 3))
         nc.scalar.activation(y_tail[:, 1:2, :], parts[0][0][:], ACT.Copy)
         scatter(ST - 1, y, 0)
         scatter(ST - 1, y, 1)

@@ -46,9 +46,6 @@ def tile_moe_res_mlp_relu2_kernel(tc, xT, xr, w1_words, w1_scales, w2_words, w2_
 
         w1s = [keep.tile([P, KP, H], U8, name=f"w1s{e}", align_bytes=64) for e in range(E)]
         w2s = keep.tile([P, E * HP, N], U8, name="w2s", align_bytes=64)
-        warm = keep.tile([P, 1], F32, name="warm")
-        nc.vector.memset(warm[:], 0.0)
-        nc.scalar.activation(warm[:], warm[:], ACT.Square)
         for e in range(E):
             nc.vector.memset(w1s[e][:].rearrange("p g i -> p (g i)").bitcast(I32), 0)
         nc.vector.memset(w2s[:].rearrange("p g i -> p (g i)").bitcast(I32), 0)

@@ -24,14 +24,36 @@ HP = H // 512
 ST = S // P
 NT = N // P
 
-CHUNKS = (((0, 640),), ((0, 384), (384, 640)))
-PIECES = (((0, 256, 0), (256, 384, 0), (384, 640, 256)), ((0, 256, 256), (256, 384, 128), (384, 640, 64)))
-SUM_BANK = ((0, 1), (2, 3), (0, 1), (4, 4))
-TURN_BANK = ((4, 5), (6, 7), (3, 5), (6, 7))
-OUT_BANK = (((4, 0, 1), (3, 1, 3)), ((1, 0, 3),), ((4, 0, 2), (6, 2, 3)), ((0, 0, 1), (2, 1, 2), (2, 2, 3)))
-W1_LOADS = (((0, 1), (1, 2)), ((0, 2),))
-RELU_ON_VECTOR = ((1, 1), (2, 0))
-SLOT = 2048
+PIECES = ((0, 256, False), (256, 384, False), (384, 640, True))
+SUM_BANK = ((0, 1), (2, 3), (0, 1), (1, 2))
+TURN_BANK = ((4, 5), (6, 7), (2, 4), (0, 5))
+OUT_BANK = (((2, 0, 1), (3, 1, 3)), ((3, 0, 3),), ((1, 0, 3),), ((6, 0, 1), (7, 1, 2), (0, 2, 3)))
+SLOT = 4096
+PLACE = {
+    "grouped1_1": 0 * SLOT,
+    "g_words0_2": 0 * SLOT,
+    "grouped1_2": 1 * SLOT,
+    "g_scales0_2": 1 * SLOT,
+    "g_words1_1": 2 * SLOT + 512,
+    "g_words0_3": 2 * SLOT + 64,
+    "g_words1_3": 2 * SLOT + 960,
+    "g_scales1_1": 3 * SLOT + 64,
+    "g_scales1_2": 3 * SLOT,
+    "g_scales0_3": 3 * SLOT + 128,
+    "relu1_1": 4 * SLOT,
+    "g_scales1_3": 4 * SLOT,
+    "g_words1_2": 5 * SLOT,
+    "h_words1": 5 * SLOT,
+    "h_words0": 6 * SLOT,
+    "relu2_1": 6 * SLOT,
+    "y1_1": 6 * SLOT,
+    "relu3_1": 7 * SLOT,
+    "y2_1": 7 * SLOT,
+    "y3_1": 8 * SLOT,
+    "y3_2": 8 * SLOT,
+}
+BLOCK1_CUT = 448
+BLOCK2_CUT = 320
 
 
 def tile_moe_res_mlp_relu2_kernel(tc, xT, xr, w1_words, w1_scales, w2_words, w2_scales, gate, offs, out):
@@ -39,17 +61,20 @@ def tile_moe_res_mlp_relu2_kernel(tc, xT, xr, w1_words, w1_scales, w2_words, w2_
     with ExitStack() as ctx:
         keep = ctx.enter_context(tc.tile_pool(name="keep", bufs=1))
         shared = ctx.enter_context(tc.tile_pool(name="shared", bufs=1))
-        work = ctx.enter_context(tc.tile_pool(name="work", bufs=3))
-        ps_m = ctx.enter_context(tc.psum_pool(name="ps_m", bufs=1))
+        psum = ctx.enter_context(tc.psum_pool(name="psum", bufs=1))
+
+        def new_tile(shape, dtype, name):
+            if name in PLACE:
+                return shared.tile(shape, dtype, name=name, align_bytes=64, offset=PLACE[name])
+            return keep.tile(shape, dtype, name=name, align_bytes=64)
 
         offsets = keep.tile([P, S // 16], U16, name="offsets")
 
-        w1s = [keep.tile([P, KP, H], U8, name=f"w1s{e}", align_bytes=64) for e in range(E)]
-        w2s = keep.tile([P, E * HP, N], U8, name="w2s", align_bytes=64)
-        for e in range(E):
-            nc.vector.memset(w1s[e][:].rearrange("p g i -> p (g i)").bitcast(I32), 0)
-        nc.vector.memset(w2s[:].rearrange("p g i -> p (g i)").bitcast(I32), 0)
-        x_scales = [keep.tile([P, T], U8, name=f"x_scales{s}", align_bytes=64) for s in range(KP)]
+        w1s = [new_tile([P, KP, H], U8, f"w1s{e}") for e in range(E)]
+        w2s = new_tile([P, E * HP, N], U8, "w2s")
+        for plane in (*w1s, w2s):
+            nc.vector.memset(plane[:].rearrange("p g i -> p (g i)").bitcast(I32), 0)
+        x_scales = [new_tile([P, T], U8, f"x_scales{s}") for s in range(KP)]
         for s in range(KP):
             nc.vector.memset(x_scales[s][:].bitcast(I32), 0)
         ident = keep.tile([P, P], F32, name="ident")
@@ -58,14 +83,10 @@ def tile_moe_res_mlp_relu2_kernel(tc, xT, xr, w1_words, w1_scales, w2_words, w2_
         for n in range(NT):
             nc.vector.memset(windows[n][:], 0.0)
 
-        raw = {}
-
-        def load_tokens(s, part=slice(0, 3)):
-            rows = xT[s * 512 : (s + 1) * 512, :].rearrange("(q j) w -> q j w", j=4)
-            for c0, c1 in CHUNKS[s][part]:
-                t = keep.tile([P, 4, c1 - c0], F32, name=f"raw{s}_{c0}")
-                nc.sync.dma_start(out=t[:], in_=rows[:, :, c0:c1])
-                raw[s, c0] = t
+        def load_tokens(s):
+            raw = keep.tile([P, 4, T], F32, name=f"raw{s}")
+            nc.sync.dma_start(out=raw[:], in_=xT[s * 512 : (s + 1) * 512, :].rearrange("(q j) w -> q j w", j=4))
+            return raw
 
         def load_scales(plane, rows):
             for r in range(4):
@@ -77,87 +98,72 @@ def tile_moe_res_mlp_relu2_kernel(tc, xT, xr, w1_words, w1_scales, w2_words, w2_
         w1w = [[], []]
 
         def load_words(e, s0, s1):
-            t = keep.tile([P, s1 - s0, 2 * H], U8, name=f"w1w{e}_{s0}", align_bytes=64)
+            t = new_tile([P, s1 - s0, 2 * H], U8, f"w1w{e}_{s0}")
             nc.sync.dma_start(out=t[:].bitcast(I32), in_=w1_rows[e, :, s0:s1, :])
             w1w[e].extend(t[:, s, :] for s in range(s1 - s0))
 
-        load_tokens(0)
+        raw = [load_tokens(0)]
         nc.sync.dma_start(offsets[:], offs)
-        load_tokens(1)
+        raw.append(load_tokens(1))
         load_scales(w1s[0], w1s_rows[0])
         load_words(0, 0, 1)
         load_words(0, 1, 2)
         load_scales(w1s[1], w1s_rows[1])
-        load_words(1, 0, 2)
+        load_words(1, 0, KP)
+        load_scales(w2s, w2s_rows)
+        w2w = new_tile([P, E * HP, 2 * N], U8, "w2w")
+        nc.sync.dma_start(out=w2w[:].bitcast(I32), in_=w2_words.bitcast(I32).rearrange("e s p w -> p (e s) w"))
         gates = keep.tile([P, S], F32, name="gates")
         nc.sync.dma_start(out=gates[:], in_=gate[0:P, :])
-        load_scales(w2s, w2s_rows)
-        w2w = keep.tile([P, E * HP, 2 * N], U8, name="w2w", align_bytes=64)
-        nc.sync.dma_start(out=w2w[:].bitcast(I32), in_=w2_words.bitcast(I32).rearrange("e s p w -> p (e s) w"))
         residual = [keep.tile([P, T], F32, name=f"residual{n}") for n in range(NT)]
         for n in range(NT):
             nc.sync.dma_start(out=residual[n][:], in_=xr[n * P : (n + 1) * P, :])
 
-        x_words = [keep.tile([P, T], U32, name=f"x_words{s}", align_bytes=64) for s in range(KP)]
+        x_words = [new_tile([P, T], U32, f"x_words{s}") for s in range(KP)]
 
-        def interleave(dst, src, c0, c1, on_scalar):
-            d = dst
-            r = src[:, :, c0:c1].rearrange("p t c -> p c t")
-            if on_scalar:
-                nc.scalar.activation(d, r, ACT.Copy)
-            else:
-                nc.vector.tensor_copy(out=d, in_=r)
+        def quantize_tokens(s):
+            grouped = []
+            for piece, (c0, c1, on_scalar) in enumerate(PIECES):
+                t = new_tile([P, c1 - c0, 4], BF16, f"grouped{s}_{piece}")
+                src = raw[s][:, :, c0:c1].rearrange("p t c -> p c t")
+                if on_scalar:
+                    nc.scalar.activation(t[:], src, ACT.Copy)
+                else:
+                    nc.vector.tensor_copy(out=t[:], in_=src)
+                grouped.append(t)
+            for t, (c0, c1, on_scalar) in zip(grouped, PIECES):
+                nc.vector.quantize_mx(
+                    out=x_words[s][:, c0:c1].bitcast(E4M3),
+                    scales=x_scales[s][:, c0:c1],
+                    in_=t[:].rearrange("p w j -> p (w j)"),
+                )
 
-        def group_tokens(s, piece):
-            c0, c1, share = PIECES[s][piece]
-            base = max(b0 for b0, b1 in CHUNKS[s] if b0 <= c0)
-            if (s, c1) == (KP - 1, T):
-                grouped = shared.tile([P, c1 - c0, 4], BF16, name="grouped_last", align_bytes=64, offset=0)
-            else:
-                grouped = keep.tile([P, c1 - c0, 4], BF16, name=f"grouped{s}_{piece}", align_bytes=64)
-            cut = c1 - share
-            if share > 0:
-                interleave(grouped[:, cut - c0 :, :], raw[s, base], cut - base, c1 - base, True)
-            if cut > c0:
-                interleave(grouped[:, : cut - c0, :], raw[s, base], c0 - base, cut - base, False)
-            return grouped
-
-        def quantize_tokens(s, piece, grouped):
-            c0, c1, share = PIECES[s][piece]
-            nc.vector.quantize_mx(
-                out=x_words[s][:, c0:c1].bitcast(E4M3),
-                scales=x_scales[s][:, c0:c1],
-                in_=grouped[:].rearrange("p w j -> p (w j)"),
-            )
+        def slots(st0, st1):
+            return offsets[:, st0 * P // 16 : st1 * P // 16]
 
         g_words = {}
         g_scales = {}
 
-        def gather_tokens(s, st0, st1, place=None):
-            width = (st1 - st0) * P
-            if place is None:
-                words = keep.tile([P, width], U32, name=f"g_words{s}_{st0}", align_bytes=64)
-                scales = keep.tile([P, width], U8, name=f"g_scales{s}_{st0}", align_bytes=64)
-            else:
-                words = shared.tile([P, width], U32, name=f"g_words{s}_{st0}", align_bytes=64, offset=place)
-                scales = shared.tile([P, width], U8, name=f"g_scales{s}_{st0}", align_bytes=64, offset=place + 4 * width)
-            lists = offsets[:, st0 * P // 16 : st1 * P // 16]
-            nc.vector.tensor_copy(out=words[:], in_=x_words[s][:].indirect(lists))
-            nc.vector.tensor_copy(out=scales[:], in_=x_scales[s][:].indirect(lists))
-            for st in range(st0, st1):
-                g_words[s, st] = words[:, (st - st0) * P : (st - st0 + 1) * P]
-                g_scales[s, st] = scales[:, (st - st0) * P : (st - st0 + 1) * P]
+        def gather_words(s, st0, tiles=1):
+            t = new_tile([P, tiles, P], U32, f"g_words{s}_{st0}")
+            nc.vector.tensor_copy(out=t[:].rearrange("p a c -> p (a c)"), in_=x_words[s][:].indirect(slots(st0, st0 + tiles)))
+            for a in range(tiles):
+                g_words[s, st0 + a] = t[:, a, :]
 
-        def relu_place(st, g):
-            return SLOT * (1 + HP * st + g)
+        def gather_scales(s, st0, tiles=1):
+            t = new_tile([P, tiles, P], U8, f"g_scales{s}_{st0}")
+            nc.vector.tensor_copy(out=t[:].rearrange("p a c -> p (a c)"), in_=x_scales[s][:].indirect(slots(st0, st0 + tiles)))
+            for a in range(tiles):
+                g_scales[s, st0 + a] = t[:, a, :]
 
-        def sum_bank(st, g):
-            return f"bank{SUM_BANK[st][g]}"
+        sums = {}
 
-        def first_pass(st, s, g, bank):
-            e = st // 2
+        def first_pass(st, s, g):
+            if s == 0:
+                sums[st, g] = psum.tile([P, 512], F32, name="sums", tag=f"bank{SUM_BANK[st][g]}")
+            e = st * P // C
             nc.tensor.matmul_mx(
-                out=bank[:],
+                out=sums[st, g][:],
                 lhsT=g_words[s, st].bitcast(E4M3),
                 lhsT_scale=g_scales[s, st],
                 rhs=w1w[e][s][:, g * 1024 : (g + 1) * 1024].bitcast(E2M1),
@@ -166,54 +172,55 @@ def tile_moe_res_mlp_relu2_kernel(tc, xT, xr, w1_words, w1_scales, w2_words, w2_
                 stop=(s == KP - 1),
             )
 
-        def first_product(st):
-            banks = []
-            for g in range(HP):
-                bank = ps_m.tile([P, 512], F32, name="bank_a", tag=sum_bank(st, g))
-                for s in range(KP):
-                    first_pass(st, s, g, bank)
-                banks.append(bank)
-            return banks
+        def first_product(st, g):
+            for s in range(KP):
+                first_pass(st, s, g)
 
-        def relu(st, g, bank, on_scalar=True):
-            r = shared.tile([P, 4, P], F32, name=f"relu{st}_{g}", align_bytes=64, offset=relu_place(st, g))
-            src = bank[:].rearrange("p (m t) -> p t m", t=4)
-            if on_scalar:
-                nc.scalar.activation(r[:], src, ACT.Relu)
-            else:
-                nc.vector.tensor_scalar_max(r[:], src, 0.0)
-            return r
+        relus = {}
 
-        def turn_and_square(st, relus, place=None):
-            if place is None:
-                h = work.tile([P, HP, P, 4], BF16, name="h", align_bytes=64)
-            else:
-                h = shared.tile([P, HP, P, 4], BF16, name="h_first", align_bytes=64, offset=place)
-            for g in range(HP):
-                bank = ps_m.tile([P, 4, P], F32, name="bank_t", tag=f"bank{TURN_BANK[st][g]}")
-                for t in range(4):
-                    nc.tensor.transpose(bank[:, t, :], relus[g][:, t, :], ident[:])
-                nc.scalar.activation(h[:, g, :, :], bank[:].rearrange("p t c -> p c t"), ACT.Square)
-            return h
+        def relu(st, g, on_vector=False, parts=1):
+            r = new_tile([P, 4, P], F32, f"relu{st}_{g}")
+            src = sums[st, g][:].rearrange("p (m t) -> p t m", t=4)
+            for a in range(parts):
+                blocks = slice(4 * a // parts, 4 * (a + 1) // parts)
+                if on_vector:
+                    nc.vector.tensor_scalar_max(r[:, blocks, :], src[:, blocks, :], 0.0)
+                else:
+                    nc.scalar.activation(r[:, blocks, :], src[:, blocks, :], ACT.Relu)
+            relus[st, g] = r
 
-        def quantize_hidden(h, place=None):
-            if place is None:
-                h_words = work.tile([P, HP, P], U32, name="h_words", align_bytes=64)
-            else:
-                h_words = shared.tile([P, HP, P], U32, name="h_words_first", align_bytes=64, offset=place)
-            h_scales = work.tile([P, HP, P], U8, name="h_scales", align_bytes=64)
+        turned = {}
+
+        def turn(st, g):
+            bank = psum.tile([P, 4, P], F32, name="turned", tag=f"bank{TURN_BANK[st][g]}")
+            for t in range(4):
+                nc.tensor.transpose(bank[:, t, :], relus[st, g][:, t, :], ident[:])
+            turned[st, g] = bank
+
+        hidden = [new_tile([P, HP, P, 4], BF16, f"hidden{st}") for st in range(ST)]
+
+        def square(st, g):
+            nc.scalar.activation(hidden[st][:, g, :, :], turned[st, g][:].rearrange("p t c -> p c t"), ACT.Square)
+
+        codes = {}
+
+        def quantize_hidden(st):
+            h_words = new_tile([P, HP, P], U32, f"h_words{st}")
+            h_scales = new_tile([P, HP, P], U8, f"h_scales{st}")
             nc.vector.quantize_mx(
                 out=h_words[:].rearrange("p g c -> p (g c)").bitcast(E4M3),
                 scales=h_scales[:].rearrange("p g c -> p (g c)"),
-                in_=h[:].rearrange("p g c t -> p (g c t)"),
+                in_=hidden[st][:].rearrange("p g c t -> p (g c t)"),
             )
-            return h_words, h_scales
+            codes[st] = (h_words, h_scales)
 
-        def second_product(st, h_words, h_scales, parts=slice(0, 3)):
-            e = st // 2
-            done = []
-            for bank_no, n0, n1 in OUT_BANK[st][parts]:
-                bank = ps_m.tile([P, n1 - n0, P], F32, name="bank_y", tag=f"bank{bank_no}")
+        y_banks = {}
+
+        def second_product(st):
+            e = st * P // C
+            h_words, h_scales = codes[st]
+            for bank_no, n0, n1 in OUT_BANK[st]:
+                bank = psum.tile([P, n1 - n0, P], F32, name="y_bank", tag=f"bank{bank_no}")
                 for n in range(n0, n1):
                     for g in range(HP):
                         nc.tensor.matmul_mx(
@@ -225,86 +232,99 @@ def tile_moe_res_mlp_relu2_kernel(tc, xT, xr, w1_words, w1_scales, w2_words, w2_
                             start=(g == 0),
                             stop=(g == HP - 1),
                         )
-                done.append((bank, n0, n1))
-            return done
+                    y_banks[st, n] = (bank, n0)
 
-        def empty(st, parts):
-            rows = []
-            for bank, n0, n1 in parts:
-                if st + 1 < ST:
-                    y = shared.tile([P, n1 - n0, P], F32, name=f"y{st}_{n0}", align_bytes=64, offset=relu_place(st + 1, HP - 1) + 4 * P * n0)
-                else:
-                    y = keep.tile([P, n1 - n0, P], F32, name=f"y_last{n0}")
-                nc.scalar.activation(y[:], bank[:], ACT.Copy)
-                rows.extend(y[:, n, :] for n in range(n1 - n0))
-            return rows
+        y_rows = {}
 
-        y_tail = keep.tile([P, 2, P], F32, name="y_tail")
+        def empty(st, n0, n1):
+            bank, first = y_banks[st, n0]
+            y = new_tile([P, n1 - n0, P], F32, f"y{st}_{n0}")
+            nc.scalar.activation(y[:], bank[:, n0 - first : n1 - first, :], ACT.Copy)
+            for n in range(n0, n1):
+                y_rows[st, n] = y[:, n - n0, :]
 
-        def scatter(st, y, n):
-            nc.vector.tensor_tensor(
-                windows[n][:].indirect(offsets[:, st * P // 16 : (st + 1) * P // 16]),
-                y[n],
-                gates[:, st * P : (st + 1) * P],
-                ALU.mult,
-            )
+        def scatter(st, n):
+            nc.vector.tensor_tensor(windows[n][:].indirect(slots(st, st + 1)), y_rows[st, n], gates[:, st * P : (st + 1) * P], ALU.mult)
 
-        def finish(n, c0, c1, queue):
+        def finish(n, c0, c1):
             nc.vector.tensor_add(out=residual[n][:, c0:c1], in0=windows[n][:, c0:c1], in1=residual[n][:, c0:c1])
-            queue.dma_start(out=out[n * P : (n + 1) * P, c0:c1], in_=residual[n][:, c0:c1])
+            nc.sync.dma_start(out=out[n * P : (n + 1) * P, c0:c1], in_=residual[n][:, c0:c1])
 
-        grouped = [group_tokens(0, piece) for piece in range(len(PIECES[0]))]
-        for piece in range(len(PIECES[0])):
-            quantize_tokens(0, piece, grouped[piece])
-        gather_tokens(0, 0, 2)
-        banks0 = [ps_m.tile([P, 512], F32, name="bank_a", tag=sum_bank(0, g)) for g in range(HP)]
+        quantize_tokens(0)
+        gather_words(0, 0, 2)
+        gather_scales(0, 0, 2)
+        for st in range(2):
+            for g in range(HP):
+                first_pass(st, 0, g)
+        quantize_tokens(1)
+        gather_words(0, 2)
+        for st in range(2):
+            gather_words(1, st)
+            gather_scales(1, st)
+            for g in range(HP):
+                first_pass(st, 1, g)
+        gather_scales(0, 2)
+        gather_words(1, 2)
+        relu(0, 0, parts=2)
+        relu(0, 1, on_vector=True)
+        relu(1, 0)
+        relu(1, 1, on_vector=True)
+        gather_scales(1, 2)
+        gather_words(0, 3)
+        gather_scales(0, 3)
+        gather_words(1, 3)
+        for st in range(2):
+            for g in range(HP):
+                turn(st, g)
         for g in range(HP):
-            first_pass(0, 0, g, banks0[g])
-        grouped = [group_tokens(1, piece) for piece in range(len(PIECES[1]))]
-        for piece in range(len(PIECES[1])):
-            quantize_tokens(1, piece, grouped[piece])
-        gather_tokens(1, 0, 1)
+            square(0, g)
+        quantize_hidden(0)
+        gather_scales(1, 3)
         for g in range(HP):
-            first_pass(0, 1, g, banks0[g])
-        gather_tokens(1, 1, 2)
-        banks1 = first_product(1)
-        relus0 = [relu(0, g, banks0[g], (0, g) not in RELU_ON_VECTOR) for g in range(HP)]
-        gather_tokens(0, 2, 3, 0)
-        gather_tokens(1, 2, 3)
-        relus = [relu(1, g, banks1[g], (1, g) not in RELU_ON_VECTOR) for g in range(HP)]
-        h = turn_and_square(0, relus0, SLOT * (1 + HP * ST))
-        gather_tokens(0, 3, 4, relu_place(0, 0))
-        gather_tokens(1, 3, 4, relu_place(0, 0) + 5 * P)
-        codes = quantize_hidden(h, relu_place(2, 1))
-        for st in range(1, ST - 1):
-            h = turn_and_square(st, relus)
-            bank_y = second_product(st - 1, *codes)
-            codes = quantize_hidden(h)
-            y = empty(st - 1, bank_y)
-            banks = first_product(st + 1)
-            relus = [relu(st + 1, g, banks[g], (st + 1, g) not in RELU_ON_VECTOR) for g in range(HP)]
-            for n in range(NT):
-                scatter(st - 1, y, n)
-        h = turn_and_square(ST - 1, relus)
-        parts = second_product(ST - 2, *codes)
-        codes = quantize_hidden(h)
-        y = empty(ST - 2, parts[:1])
-        nc.scalar.activation(y_tail[:, 0:1, :], parts[1][0][:], ACT.Copy)
-        scatter(ST - 2, y, 0)
-        scatter(ST - 2, y, 1)
-        y = empty(ST - 1, second_product(ST - 1, *codes, parts=slice(0, 2)))
-        parts = second_product(ST - 1, *codes, parts=slice(2, 3))
-        nc.scalar.activation(y_tail[:, 1:2, :], parts[0][0][:], ACT.Copy)
-        scatter(ST - 1, y, 0)
-        scatter(ST - 1, y, 1)
-        finish(0, 0, T, nc.sync)
-        finish(1, 0, 448, nc.sync)
-        nc.vector.tensor_tensor(
-            windows[2][:].indirect(offsets[:, 2 * P // 16 : S // 16]),
-            y_tail[:].rearrange("p t c -> p (t c)"),
-            gates[:, 2 * P : S],
-            ALU.mult,
-        )
-        finish(1, 448, T, nc.sync)
-        finish(2, 0, 320, nc.sync)
-        finish(2, 320, T, nc.sync)
+            first_product(2, g)
+            square(1, g)
+        relu(2, 0, on_vector=True)
+        quantize_hidden(1)
+        second_product(0)
+        empty(0, 0, 1)
+        empty(0, 1, NT)
+        relu(2, 1)
+        for n in range(NT):
+            scatter(0, n)
+        turn(2, 0)
+        second_product(1)
+        turn(2, 1)
+        square(2, 0)
+        empty(1, 0, 1)
+        square(2, 1)
+        empty(1, 1, NT)
+        for g in range(HP):
+            first_product(3, g)
+            relu(3, g)
+        scatter(1, 0)
+        quantize_hidden(2)
+        scatter(1, 1)
+        scatter(1, 2)
+        turn(3, 0)
+        second_product(2)
+        turn(3, 1)
+        square(3, 0)
+        empty(2, 0, 1)
+        square(3, 1)
+        empty(2, 1, NT)
+        scatter(2, 0)
+        quantize_hidden(3)
+        scatter(2, 1)
+        scatter(2, 2)
+        second_product(3)
+        empty(3, 0, 1)
+        empty(3, 1, 2)
+        scatter(3, 0)
+        scatter(3, 1)
+        empty(3, 2, NT)
+        finish(0, 0, T)
+        finish(1, 0, BLOCK1_CUT)
+        scatter(3, 2)
+        finish(1, BLOCK1_CUT, T)
+        finish(2, 0, BLOCK2_CUT)
+        finish(2, BLOCK2_CUT, T)

@@ -24,7 +24,8 @@ HP = H // 512
 ST = S // P
 NT = N // P
 
-PIECES = ((0, 256, False), (256, 384, False), (384, 640, True))
+PIECES = ((0, 256), (256, 384), (384, 640))
+SCALAR_FROM = ((384, 384), (192, 384))
 SUM_BANK = ((0, 1), (2, 3), (0, 1), (1, 2))
 TURN_BANK = ((4, 5), (6, 7), (2, 4), (0, 5))
 OUT_BANK = (((2, 0, 1), (3, 1, 3)), ((3, 0, 3),), ((1, 0, 3),), ((6, 0, 1), (7, 1, 2), (0, 2, 3)))
@@ -70,7 +71,8 @@ def tile_moe_res_mlp_relu2_kernel(tc, xT, xr, w1_words, w1_scales, w2_words, w2_
 
         offsets = keep.tile([P, S // 16], U16, name="offsets")
 
-        w1s = [new_tile([P, KP, H], U8, f"w1s{e}") for e in range(E)]
+        w1s = [new_tile([P, 1, H], U8, "w1s0_0"), new_tile([P, 1, H], U8, "w1s0_1"), new_tile([P, KP, H], U8, "w1s1")]
+        w1_planes = [[w1s[0][:, 0, :], w1s[1][:, 0, :]], [w1s[2][:, s, :] for s in range(KP)]]
         w2s = new_tile([P, E * HP, N], U8, "w2s")
         for plane in (*w1s, w2s):
             nc.vector.memset(plane[:].rearrange("p g i -> p (g i)").bitcast(I32), 0)
@@ -84,9 +86,13 @@ def tile_moe_res_mlp_relu2_kernel(tc, xT, xr, w1_words, w1_scales, w2_words, w2_
             nc.vector.memset(windows[n][:], 0.0)
 
         def load_tokens(s):
-            raw = keep.tile([P, 4, T], F32, name=f"raw{s}")
-            nc.sync.dma_start(out=raw[:], in_=xT[s * 512 : (s + 1) * 512, :].rearrange("(q j) w -> q j w", j=4))
-            return raw
+            rows = xT[s * 512 : (s + 1) * 512, :].rearrange("(q u j) w -> u q j w", u=2, j=2)
+            halves = []
+            for u in range(2):
+                t = keep.tile([P, 2, T], F32, name=f"raw{s}_{u}")
+                nc.sync.dma_start(out=t[:], in_=rows[u])
+                halves.append(t)
+            return halves
 
         def load_scales(plane, rows):
             for r in range(4):
@@ -105,37 +111,49 @@ def tile_moe_res_mlp_relu2_kernel(tc, xT, xr, w1_words, w1_scales, w2_words, w2_
         raw = [load_tokens(0)]
         nc.sync.dma_start(offsets[:], offs)
         raw.append(load_tokens(1))
-        load_scales(w1s[0], w1s_rows[0])
-        load_words(0, 0, 1)
+        load_scales(w1s[0], w1s_rows[0, :, :, 0:1, :])
+        halves = []
+        for g in range(HP):
+            t = new_tile([P, H], U8, f"w1w0_0_{g}")
+            nc.sync.dma_start(out=t[:].bitcast(I32), in_=w1_rows[0, :, 0, g * 256 : (g + 1) * 256])
+            halves.append(t)
+        w1w[0].append(halves)
         load_words(0, 1, 2)
-        load_scales(w1s[1], w1s_rows[1])
+        load_scales(w1s[1], w1s_rows[0, :, :, 1:2, :])
         load_words(1, 0, KP)
+        load_scales(w1s[2], w1s_rows[1])
+        w2w = [new_tile([P, HP, 2 * N], U8, f"w2w{e}") for e in range(E)]
+        w2_rows = w2_words.bitcast(I32).rearrange("e s p w -> e p s w")
+        nc.sync.dma_start(out=w2w[0][:].bitcast(I32), in_=w2_rows[0])
         load_scales(w2s, w2s_rows)
-        w2w = new_tile([P, E * HP, 2 * N], U8, "w2w")
-        nc.sync.dma_start(out=w2w[:].bitcast(I32), in_=w2_words.bitcast(I32).rearrange("e s p w -> p (e s) w"))
         gates = keep.tile([P, S], F32, name="gates")
         nc.sync.dma_start(out=gates[:], in_=gate[0:P, :])
+        nc.sync.dma_start(out=w2w[1][:].bitcast(I32), in_=w2_rows[1])
         residual = [keep.tile([P, T], F32, name=f"residual{n}") for n in range(NT)]
         for n in range(NT):
             nc.sync.dma_start(out=residual[n][:], in_=xr[n * P : (n + 1) * P, :])
 
         x_words = [new_tile([P, T], U32, f"x_words{s}") for s in range(KP)]
 
+        grouped = [[new_tile([P, c1 - c0, 2, 2], BF16, f"grouped{s}_{piece}") for piece, (c0, c1) in enumerate(PIECES)] for s in range(KP)]
+
+        def group_tokens(s, u):
+            cut = SCALAR_FROM[s][u]
+            for t, (c0, c1) in zip(grouped[s], PIECES):
+                for a, b in ((c0, min(c1, cut)), (max(c0, cut), c1)):
+                    if a < b:
+                        src = raw[s][u][:, :, a:b].rearrange("p j c -> p c j")
+                        if a >= cut:
+                            nc.scalar.activation(t[:, a - c0 : b - c0, u, :], src, ACT.Copy)
+                        else:
+                            nc.vector.tensor_copy(out=t[:, a - c0 : b - c0, u, :], in_=src)
+
         def quantize_tokens(s):
-            grouped = []
-            for piece, (c0, c1, on_scalar) in enumerate(PIECES):
-                t = new_tile([P, c1 - c0, 4], BF16, f"grouped{s}_{piece}")
-                src = raw[s][:, :, c0:c1].rearrange("p t c -> p c t")
-                if on_scalar:
-                    nc.scalar.activation(t[:], src, ACT.Copy)
-                else:
-                    nc.vector.tensor_copy(out=t[:], in_=src)
-                grouped.append(t)
-            for t, (c0, c1, on_scalar) in zip(grouped, PIECES):
+            for t, (c0, c1) in zip(grouped[s], PIECES):
                 nc.vector.quantize_mx(
                     out=x_words[s][:, c0:c1].bitcast(E4M3),
                     scales=x_scales[s][:, c0:c1],
-                    in_=t[:].rearrange("p w j -> p (w j)"),
+                    in_=t[:].rearrange("p w u j -> p (w u j)"),
                 )
 
         def slots(st0, st1):
@@ -166,8 +184,8 @@ def tile_moe_res_mlp_relu2_kernel(tc, xT, xr, w1_words, w1_scales, w2_words, w2_
                 out=sums[st, g][:],
                 lhsT=g_words[s, st].bitcast(E4M3),
                 lhsT_scale=g_scales[s, st],
-                rhs=w1w[e][s][:, g * 1024 : (g + 1) * 1024].bitcast(E2M1),
-                rhs_scale=w1s[e][:, s, g * 512 : (g + 1) * 512],
+                rhs=(w1w[e][s][g][:] if (e, s) == (0, 0) else w1w[e][s][:, g * 1024 : (g + 1) * 1024]).bitcast(E2M1),
+                rhs_scale=w1_planes[e][s][:, g * 512 : (g + 1) * 512],
                 start=(s == 0),
                 stop=(s == KP - 1),
             )
@@ -225,7 +243,7 @@ def tile_moe_res_mlp_relu2_kernel(tc, xT, xr, w1_words, w1_scales, w2_words, w2_
                     for g in range(HP):
                         nc.tensor.matmul_mx(
                             out=bank[:, n - n0, :],
-                            lhsT=w2w[:, e * HP + g, 256 * n : 256 * (n + 1)].bitcast(E2M1),
+                            lhsT=w2w[e][:, g, 256 * n : 256 * (n + 1)].bitcast(E2M1),
                             lhsT_scale=w2s[:, e * HP + g, P * n : P * (n + 1)],
                             rhs=h_words[:, g, :].bitcast(E4M3),
                             rhs_scale=h_scales[:, g, :],
@@ -250,19 +268,27 @@ def tile_moe_res_mlp_relu2_kernel(tc, xT, xr, w1_words, w1_scales, w2_words, w2_
             nc.vector.tensor_add(out=residual[n][:, c0:c1], in0=windows[n][:, c0:c1], in1=residual[n][:, c0:c1])
             nc.sync.dma_start(out=out[n * P : (n + 1) * P, c0:c1], in_=residual[n][:, c0:c1])
 
+        group_tokens(0, 0)
+        group_tokens(0, 1)
         quantize_tokens(0)
         gather_words(0, 0, 2)
         gather_scales(0, 0, 2)
-        for st in range(2):
-            for g in range(HP):
-                first_pass(st, 0, g)
+        group_tokens(1, 0)
+        group_tokens(1, 1)
+        first_pass(0, 0, 0)
+        first_pass(1, 0, 0)
+        first_pass(0, 0, 1)
+        first_pass(1, 0, 1)
         quantize_tokens(1)
         gather_words(0, 2)
-        for st in range(2):
-            gather_words(1, st)
-            gather_scales(1, st)
-            for g in range(HP):
-                first_pass(st, 1, g)
+        gather_words(1, 0)
+        gather_scales(1, 0)
+        first_pass(0, 1, 0)
+        first_pass(0, 1, 1)
+        gather_words(1, 1)
+        gather_scales(1, 1)
+        first_pass(1, 1, 0)
+        first_pass(1, 1, 1)
         gather_scales(0, 2)
         gather_words(1, 2)
         relu(0, 0, parts=2)
@@ -273,34 +299,42 @@ def tile_moe_res_mlp_relu2_kernel(tc, xT, xr, w1_words, w1_scales, w2_words, w2_
         gather_words(0, 3)
         gather_scales(0, 3)
         gather_words(1, 3)
-        for st in range(2):
-            for g in range(HP):
-                turn(st, g)
-        for g in range(HP):
-            square(0, g)
+        turn(0, 0)
+        turn(0, 1)
+        turn(1, 0)
+        turn(1, 1)
+        square(0, 0)
+        square(0, 1)
         quantize_hidden(0)
         gather_scales(1, 3)
-        for g in range(HP):
-            first_product(2, g)
-            square(1, g)
+        first_pass(2, 0, 0)
+        first_pass(2, 1, 0)
+        square(1, 0)
+        first_pass(2, 0, 1)
+        first_pass(2, 1, 1)
+        square(1, 1)
         relu(2, 0, on_vector=True)
         quantize_hidden(1)
         second_product(0)
         empty(0, 0, 1)
-        empty(0, 1, NT)
+        empty(0, 1, 3)
         relu(2, 1)
-        for n in range(NT):
-            scatter(0, n)
+        scatter(0, 0)
+        scatter(0, 1)
+        scatter(0, 2)
         turn(2, 0)
         second_product(1)
         turn(2, 1)
         square(2, 0)
         empty(1, 0, 1)
         square(2, 1)
-        empty(1, 1, NT)
-        for g in range(HP):
-            first_product(3, g)
-            relu(3, g)
+        empty(1, 1, 3)
+        first_pass(3, 0, 0)
+        first_pass(3, 1, 0)
+        relu(3, 0)
+        first_pass(3, 0, 1)
+        first_pass(3, 1, 1)
+        relu(3, 1)
         scatter(1, 0)
         quantize_hidden(2)
         scatter(1, 1)
@@ -311,7 +345,7 @@ def tile_moe_res_mlp_relu2_kernel(tc, xT, xr, w1_words, w1_scales, w2_words, w2_
         square(3, 0)
         empty(2, 0, 1)
         square(3, 1)
-        empty(2, 1, NT)
+        empty(2, 1, 3)
         scatter(2, 0)
         quantize_hidden(3)
         scatter(2, 1)
@@ -321,10 +355,10 @@ def tile_moe_res_mlp_relu2_kernel(tc, xT, xr, w1_words, w1_scales, w2_words, w2_
         empty(3, 1, 2)
         scatter(3, 0)
         scatter(3, 1)
-        empty(3, 2, NT)
-        finish(0, 0, T)
-        finish(1, 0, BLOCK1_CUT)
+        empty(3, 2, 3)
+        finish(0, 0, 640)
+        finish(1, 0, 448)
         scatter(3, 2)
-        finish(1, BLOCK1_CUT, T)
-        finish(2, 0, BLOCK2_CUT)
-        finish(2, BLOCK2_CUT, T)
+        finish(1, 448, 640)
+        finish(2, 0, 320)
+        finish(2, 320, 640)

@@ -28,7 +28,7 @@ PIECES = ((0, 256), (256, 384), (384, 640))
 SCALAR_FROM = ((384, 384), (192, 384))
 SUM_BANK = ((0, 1), (2, 3), (0, 1), (1, 2))
 TURN_BANK = ((4, 5), (6, 7), (2, 4), (0, 5))
-OUT_BANK = (((2, 0, 1), (3, 1, 3)), ((3, 0, 3),), ((1, 0, 3),), ((6, 0, 1), (7, 1, 2), (0, 2, 3)))
+OUT_BANK = (((2, 0, 1), (3, 1, 3)), ((3, 0, 3),), ((2, 0, 3),), ((6, 0, 1), (7, 1, 2), (3, 2, 3)))
 SLOT = 4096
 PLACE = {
     "grouped1_1": 0 * SLOT,
@@ -48,9 +48,10 @@ PLACE = {
     "h_words0": 6 * SLOT,
     "relu2_1": 6 * SLOT,
     "y1_1": 6 * SLOT,
-    "relu3_1": 7 * SLOT,
-    "y2_1": 7 * SLOT,
-    "y3_1": 8 * SLOT,
+    "y1_2": 6 * SLOT + 512,
+    "h_words3": 7 * SLOT,
+    "y2_2": 7 * SLOT,
+    "y3_0": 8 * SLOT,
     "y3_2": 8 * SLOT,
 }
 BLOCK1_CUT = 448
@@ -268,6 +269,45 @@ def tile_moe_res_mlp_relu2_kernel(tc, xT, xr, w1_words, w1_scales, w2_words, w2_
             nc.vector.tensor_add(out=residual[n][:, c0:c1], in0=windows[n][:, c0:c1], in1=residual[n][:, c0:c1])
             nc.sync.dma_start(out=out[n * P : (n + 1) * P, c0:c1], in_=residual[n][:, c0:c1])
 
+        there = {}
+        summed = {}
+
+        def open_sum(n, b, bank_no):
+            there[n, b] = psum.tile([P, P], F32, name="there", tag=f"bank{bank_no}")
+            nc.tensor.matmul(there[n, b][:], residual[n][:, b * P : (b + 1) * P], ident[:], start=True, stop=False, is_transpose=True)
+
+        def close_sum(n, b):
+            nc.tensor.matmul(there[n, b][:], windows[n][:, b * P : (b + 1) * P], ident[:], start=False, stop=True, is_transpose=True)
+
+        def leave_bank(n, b):
+            summed[n, b] = new_tile([P, P], F32, f"summed{n}_{b}")
+            nc.scalar.activation(summed[n, b][:], there[n, b][:], ACT.Copy)
+
+        backs = {}
+
+        def turn_back(n, b0, b1, bank_no):
+            backs[n, b0] = psum.tile([P, b1 - b0, P], F32, name="back", tag=f"bank{bank_no}")
+            for b in range(b0, b1):
+                nc.tensor.transpose(backs[n, b0][:, b - b0, :], summed[n, b][:], ident[:])
+
+        results = {}
+
+        def copy_back(n, b0, b1):
+            results[n, b0] = new_tile([P, (b1 - b0) * P], F32, f"result{n}_{b0}")
+            nc.scalar.activation(results[n, b0][:], backs[n, b0][:].rearrange("p b c -> p (b c)"), ACT.Copy)
+
+        def store_back(n, b0, b1):
+            nc.scalar.dma_start(out=out[n * P : (n + 1) * P, b0 * P : b1 * P], in_=results[n, b0][:])
+
+        y_last = new_tile([P, 2, P], F32, "y_last")
+
+        def empty_last(st):
+            bank, first = y_banks[st, NT - 1]
+            nc.scalar.activation(y_last[:, st - 2, :], bank[:, NT - 1 - first, :], ACT.Copy)
+
+        def scatter_last():
+            nc.vector.tensor_tensor(windows[NT - 1][:].indirect(slots(2, ST)), y_last[:].rearrange("p a c -> p (a c)"), gates[:, 2 * P : S], ALU.mult)
+
         group_tokens(0, 0)
         group_tokens(0, 1)
         quantize_tokens(0)
@@ -328,37 +368,59 @@ def tile_moe_res_mlp_relu2_kernel(tc, xT, xr, w1_words, w1_scales, w2_words, w2_
         square(2, 0)
         empty(1, 0, 1)
         square(2, 1)
-        empty(1, 1, 3)
+        empty(1, 1, 2)
         first_pass(3, 0, 0)
         first_pass(3, 1, 0)
-        relu(3, 0)
+        relu(3, 0, parts=2)
         first_pass(3, 0, 1)
         first_pass(3, 1, 1)
-        relu(3, 1)
+        relu(3, 1, parts=2)
+        empty(1, 2, 3)
         scatter(1, 0)
         quantize_hidden(2)
         scatter(1, 1)
         scatter(1, 2)
         turn(3, 0)
-        second_product(2)
         turn(3, 1)
+        second_product(2)
         square(3, 0)
-        empty(2, 0, 1)
         square(3, 1)
-        empty(2, 1, 3)
-        scatter(2, 0)
+        empty(2, 0, 1)
+        empty(2, 1, 2)
         quantize_hidden(3)
+        scatter(2, 0)
         scatter(2, 1)
-        scatter(2, 2)
         second_product(3)
         empty(3, 0, 1)
         empty(3, 1, 2)
+        empty(2, 2, 3)
+        open_sum(0, 0, 0)
+        open_sum(0, 1, 5)
+        open_sum(0, 2, 6)
+        open_sum(0, 3, 7)
+        open_sum(0, 4, 2)
         scatter(3, 0)
-        scatter(3, 1)
         empty(3, 2, 3)
-        finish(0, 0, 640)
-        finish(1, 0, 448)
+        scatter(3, 1)
+        close_sum(0, 0)
+        close_sum(0, 1)
+        close_sum(0, 2)
+        close_sum(0, 3)
+        close_sum(0, 4)
+        leave_bank(0, 0)
+        leave_bank(0, 1)
+        leave_bank(0, 2)
+        leave_bank(0, 3)
+        leave_bank(0, 4)
+        turn_back(0, 0, 1, 1)
+        turn_back(0, 1, 5, 4)
+        copy_back(0, 0, 1)
+        store_back(0, 0, 1)
+        copy_back(0, 1, 5)
+        store_back(0, 1, 5)
+        scatter(2, 2)
+        finish(1, 0, 384)
         scatter(3, 2)
-        finish(1, 448, 640)
+        finish(1, 384, 640)
         finish(2, 0, 320)
         finish(2, 320, 640)

@@ -49,10 +49,8 @@ PLACE = {
     "relu2_1": 6 * SLOT,
     "y1_1": 6 * SLOT,
     "y1_2": 6 * SLOT + 512,
-    "h_words3": 7 * SLOT,
-    "y2_2": 7 * SLOT,
     "y3_0": 8 * SLOT,
-    "y3_2": 8 * SLOT,
+    "y_last": 8 * SLOT,
 }
 BLOCK1_CUT = 448
 BLOCK2_CUT = 320
@@ -297,16 +295,25 @@ def tile_moe_res_mlp_relu2_kernel(tc, xT, xr, w1_words, w1_scales, w2_words, w2_
             nc.scalar.activation(results[n, b0][:], backs[n, b0][:].rearrange("p b c -> p (b c)"), ACT.Copy)
 
         def store_back(n, b0, b1):
-            nc.scalar.dma_start(out=out[n * P : (n + 1) * P, b0 * P : b1 * P], in_=results[n, b0][:])
+            nc.sync.dma_start(out=out[n * P : (n + 1) * P, b0 * P : b1 * P], in_=results[n, b0][:])
 
-        y_last = new_tile([P, 2, P], F32, "y_last")
+        last = {}
 
         def empty_last(st):
+            if not last:
+                last["y"] = new_tile([P, 2, P], F32, "y_last")
+            y_last = last["y"]
             bank, first = y_banks[st, NT - 1]
             nc.scalar.activation(y_last[:, st - 2, :], bank[:, NT - 1 - first, :], ACT.Copy)
 
         def scatter_last():
-            nc.vector.tensor_tensor(windows[NT - 1][:].indirect(slots(2, ST)), y_last[:].rearrange("p a c -> p (a c)"), gates[:, 2 * P : S], ALU.mult)
+            nc.vector.tensor_tensor(windows[NT - 1][:].indirect(slots(2, ST)), last["y"][:].rearrange("p a c -> p (a c)"), gates[:, 2 * P : S], ALU.mult)
+
+        def finish_in_two(n, c0, c1):
+            nc.vector.tensor_add(out=residual[n][:, c0:c1], in0=windows[n][:, c0:c1], in1=residual[n][:, c0:c1])
+            mid = (c0 + c1) // 2
+            for a, b in ((c0, mid), (mid, c1)):
+                nc.sync.dma_start(out=out[n * P : (n + 1) * P, a:b], in_=residual[n][:, a:b])
 
         group_tokens(0, 0)
         group_tokens(0, 1)
@@ -393,34 +400,25 @@ def tile_moe_res_mlp_relu2_kernel(tc, xT, xr, w1_words, w1_scales, w2_words, w2_
         second_product(3)
         empty(3, 0, 1)
         empty(3, 1, 2)
-        empty(2, 2, 3)
         open_sum(0, 0, 0)
         open_sum(0, 1, 5)
         open_sum(0, 2, 6)
-        open_sum(0, 3, 7)
-        open_sum(0, 4, 2)
         scatter(3, 0)
-        empty(3, 2, 3)
+        empty_last(2)
+        empty_last(3)
         scatter(3, 1)
         close_sum(0, 0)
         close_sum(0, 1)
         close_sum(0, 2)
-        close_sum(0, 3)
-        close_sum(0, 4)
         leave_bank(0, 0)
         leave_bank(0, 1)
         leave_bank(0, 2)
-        leave_bank(0, 3)
-        leave_bank(0, 4)
-        turn_back(0, 0, 1, 1)
-        turn_back(0, 1, 5, 4)
-        copy_back(0, 0, 1)
-        store_back(0, 0, 1)
-        copy_back(0, 1, 5)
-        store_back(0, 1, 5)
-        scatter(2, 2)
-        finish(1, 0, 384)
-        scatter(3, 2)
+        turn_back(0, 0, 3, 1)
+        copy_back(0, 0, 3)
+        finish_in_two(0, 384, 640)
+        finish_in_two(1, 0, 384)
+        store_back(0, 0, 3)
+        scatter_last()
         finish(1, 384, 640)
         finish(2, 0, 320)
         finish(2, 320, 640)

@@ -315,6 +315,19 @@ def tile_moe_res_mlp_relu2_kernel(tc, xT, xr, w1_words, w1_scales, w2_words, w2_
             for a, b in ((c0, mid), (mid, c1)):
                 nc.sync.dma_start(out=out[n * P : (n + 1) * P, a:b], in_=residual[n][:, a:b])
 
+        def warm_up(count, bank_no):
+            spare = psum.tile([P, 512], F32, name="spare", tag=f"bank{bank_no}")
+            for repeat in range(count):
+                nc.tensor.matmul_mx(
+                    out=spare[:],
+                    lhsT=codes[ST - 1][0][:, 0, :].bitcast(E4M3),
+                    lhsT_scale=codes[ST - 1][1][:, 0, :],
+                    rhs=w1w[1][0][:, 0:1024].bitcast(E2M1),
+                    rhs_scale=w1_planes[1][0][:, 0:512],
+                    start=True,
+                    stop=True,
+                )
+
         group_tokens(0, 0)
         group_tokens(0, 1)
         quantize_tokens(0)
@@ -413,11 +426,14 @@ def tile_moe_res_mlp_relu2_kernel(tc, xT, xr, w1_words, w1_scales, w2_words, w2_
         leave_bank(0, 0)
         leave_bank(0, 1)
         leave_bank(0, 2)
-        turn_back(0, 0, 3, 1)
-        copy_back(0, 0, 3)
+        turn_back(0, 0, 2, 1)
+        turn_back(0, 2, 3, 4)
+        copy_back(0, 0, 2)
+        copy_back(0, 2, 3)
         finish_in_two(0, 384, 640)
         finish_in_two(1, 0, 384)
-        store_back(0, 0, 3)
+        store_back(0, 0, 2)
+        store_back(0, 2, 3)
         scatter_last()
         finish(1, 384, 640)
         finish(2, 0, 320)

@@ -26,9 +26,6 @@ NT = N // P
 
 PIECES = ((0, 256), (256, 384), (384, 640))
 SCALAR_FROM = ((384, 384), (192, 384))
-SUM_BANK = ((0, 1), (2, 3), (0, 1), (1, 2))
-TURN_BANK = ((4, 5), (6, 7), (2, 4), (0, 5))
-OUT_BANK = (((2, 0, 1), (3, 1, 3)), ((3, 0, 3),), ((2, 0, 3),), ((6, 0, 1), (7, 1, 2), (3, 2, 3)))
 SLOT = 4096
 PLACE = {
     "grouped1_1": 0 * SLOT,
@@ -39,21 +36,20 @@ PLACE = {
     "g_words0_3": 2 * SLOT + 64,
     "g_words1_3": 2 * SLOT + 960,
     "g_scales1_1": 3 * SLOT + 64,
-    "g_scales1_2": 3 * SLOT,
     "g_scales0_3": 3 * SLOT + 128,
-    "relu1_1": 4 * SLOT,
-    "g_scales1_3": 4 * SLOT,
+    "g_scales1_3": 3 * SLOT,
     "g_words1_2": 5 * SLOT,
-    "h_words1": 5 * SLOT,
-    "h_words0": 6 * SLOT,
+    "h_words1_0": 5 * SLOT,
     "relu2_1": 6 * SLOT,
     "y1_1": 6 * SLOT,
     "y1_2": 6 * SLOT + 512,
-    "y3_0": 8 * SLOT,
-    "y_last": 8 * SLOT,
+    "h_words0_0": 6 * SLOT,
+    "residual0": 9 * SLOT,
+    "total1_128": 9 * SLOT - 960,
+    "total1_384": 9 * SLOT + 64,
+    "total2_0": 9 * SLOT + 1088,
+    "total2_320": 9 * SLOT + 2368,
 }
-BLOCK1_CUT = 448
-BLOCK2_CUT = 320
 
 
 def tile_moe_res_mlp_relu2_kernel(tc, xT, xr, w1_words, w1_scales, w2_words, w2_scales, gate, offs, out):
@@ -67,6 +63,9 @@ def tile_moe_res_mlp_relu2_kernel(tc, xT, xr, w1_words, w1_scales, w2_words, w2_
             if name in PLACE:
                 return shared.tile(shape, dtype, name=name, align_bytes=64, offset=PLACE[name])
             return keep.tile(shape, dtype, name=name, align_bytes=64)
+
+        def new_bank(shape, name, bank_no):
+            return psum.tile(shape, F32, name=name, tag=f"bank{bank_no}")
 
         offsets = keep.tile([P, S // 16], U16, name="offsets")
 
@@ -84,14 +83,11 @@ def tile_moe_res_mlp_relu2_kernel(tc, xT, xr, w1_words, w1_scales, w2_words, w2_
         for n in range(NT):
             nc.vector.memset(windows[n][:], 0.0)
 
-        def load_tokens(s):
+        def load_rows(s, u):
             rows = xT[s * 512 : (s + 1) * 512, :].rearrange("(q u j) w -> u q j w", u=2, j=2)
-            halves = []
-            for u in range(2):
-                t = keep.tile([P, 2, T], F32, name=f"raw{s}_{u}")
-                nc.sync.dma_start(out=t[:], in_=rows[u])
-                halves.append(t)
-            return halves
+            t = keep.tile([P, 2, T], F32, name=f"raw{s}_{u}")
+            nc.sync.dma_start(out=t[:], in_=rows[u])
+            return t
 
         def load_scales(plane, rows):
             for r in range(4):
@@ -107,9 +103,9 @@ def tile_moe_res_mlp_relu2_kernel(tc, xT, xr, w1_words, w1_scales, w2_words, w2_
             nc.sync.dma_start(out=t[:].bitcast(I32), in_=w1_rows[e, :, s0:s1, :])
             w1w[e].extend(t[:, s, :] for s in range(s1 - s0))
 
-        raw = [load_tokens(0)]
+        raw = [[load_rows(0, 0), load_rows(0, 1)], [load_rows(1, 0)]]
         nc.sync.dma_start(offsets[:], offs)
-        raw.append(load_tokens(1))
+        raw[1].append(load_rows(1, 1))
         load_scales(w1s[0], w1s_rows[0, :, :, 0:1, :])
         halves = []
         for g in range(HP):
@@ -128,9 +124,12 @@ def tile_moe_res_mlp_relu2_kernel(tc, xT, xr, w1_words, w1_scales, w2_words, w2_
         gates = keep.tile([P, S], F32, name="gates")
         nc.sync.dma_start(out=gates[:], in_=gate[0:P, :])
         nc.sync.dma_start(out=w2w[1][:].bitcast(I32), in_=w2_rows[1])
-        residual = [keep.tile([P, T], F32, name=f"residual{n}") for n in range(NT)]
+        residual = [new_tile([P, T], F32, f"residual{n}") for n in range(NT)]
         for n in range(NT):
             nc.sync.dma_start(out=residual[n][:], in_=xr[n * P : (n + 1) * P, :])
+        gate_col = keep.tile([P, ST], F32, name="gate_col")
+        with nc.allow_non_contiguous_dma(reason="one gate value a slot, slots on the partitions"):
+            nc.sync.dma_start(out=gate_col[:], in_=gate[0:1, :].rearrange("o (t p) -> p (o t)", p=P))
 
         x_words = [new_tile([P, T], U32, f"x_words{s}") for s in range(KP)]
 
@@ -175,9 +174,9 @@ def tile_moe_res_mlp_relu2_kernel(tc, xT, xr, w1_words, w1_scales, w2_words, w2_
 
         sums = {}
 
-        def first_pass(st, s, g):
+        def first_pass(st, s, g, bank_no=None):
             if s == 0:
-                sums[st, g] = psum.tile([P, 512], F32, name="sums", tag=f"bank{SUM_BANK[st][g]}")
+                sums[st, g] = new_bank([P, 512], f"sums{st}{g}", bank_no)
             e = st * P // C
             nc.tensor.matmul_mx(
                 out=sums[st, g][:],
@@ -188,10 +187,6 @@ def tile_moe_res_mlp_relu2_kernel(tc, xT, xr, w1_words, w1_scales, w2_words, w2_
                 start=(s == 0),
                 stop=(s == KP - 1),
             )
-
-        def first_product(st, g):
-            for s in range(KP):
-                first_pass(st, s, g)
 
         relus = {}
 
@@ -208,8 +203,8 @@ def tile_moe_res_mlp_relu2_kernel(tc, xT, xr, w1_words, w1_scales, w2_words, w2_
 
         turned = {}
 
-        def turn(st, g):
-            bank = psum.tile([P, 4, P], F32, name="turned", tag=f"bank{TURN_BANK[st][g]}")
+        def turn(st, g, bank_no):
+            bank = new_bank([P, 4, P], f"turned{st}{g}", bank_no)
             for t in range(4):
                 nc.tensor.transpose(bank[:, t, :], relus[st, g][:, t, :], ident[:])
             turned[st, g] = bank
@@ -221,35 +216,45 @@ def tile_moe_res_mlp_relu2_kernel(tc, xT, xr, w1_words, w1_scales, w2_words, w2_
 
         codes = {}
 
-        def quantize_hidden(st):
-            h_words = new_tile([P, HP, P], U32, f"h_words{st}")
-            h_scales = new_tile([P, HP, P], U8, f"h_scales{st}")
+        def quantize_hidden(st, g0=0, g1=HP):
+            h_words = new_tile([P, g1 - g0, P], U32, f"h_words{st}_{g0}")
+            h_scales = new_tile([P, g1 - g0, P], U8, f"h_scales{st}_{g0}")
             nc.vector.quantize_mx(
                 out=h_words[:].rearrange("p g c -> p (g c)").bitcast(E4M3),
                 scales=h_scales[:].rearrange("p g c -> p (g c)"),
-                in_=hidden[st][:].rearrange("p g c t -> p (g c t)"),
+                in_=hidden[st][:, g0:g1, :, :].rearrange("p g c t -> p (g c t)"),
             )
-            codes[st] = (h_words, h_scales)
+            for g in range(g0, g1):
+                codes[st, g] = (h_words[:, g - g0, :].bitcast(E4M3), h_scales[:, g - g0, :])
 
         y_banks = {}
 
-        def second_product(st):
+        def y_bank(st, n0, n1, bank_no):
+            bank = new_bank([P, n1 - n0, P], f"ybank{st}{n0}", bank_no)
+            for n in range(n0, n1):
+                y_banks[st, n] = (bank, n0)
+
+        def second_pass(st, n, g, by_slot=False):
             e = st * P // C
-            h_words, h_scales = codes[st]
-            for bank_no, n0, n1 in OUT_BANK[st]:
-                bank = psum.tile([P, n1 - n0, P], F32, name="y_bank", tag=f"bank{bank_no}")
-                for n in range(n0, n1):
-                    for g in range(HP):
-                        nc.tensor.matmul_mx(
-                            out=bank[:, n - n0, :],
-                            lhsT=w2w[e][:, g, 256 * n : 256 * (n + 1)].bitcast(E2M1),
-                            lhsT_scale=w2s[:, e * HP + g, P * n : P * (n + 1)],
-                            rhs=h_words[:, g, :].bitcast(E4M3),
-                            rhs_scale=h_scales[:, g, :],
-                            start=(g == 0),
-                            stop=(g == HP - 1),
-                        )
-                    y_banks[st, n] = (bank, n0)
+            bank, n0 = y_banks[st, n]
+            h = codes[st, g]
+            w = (w2w[e][:, g, 256 * n : 256 * (n + 1)].bitcast(E2M1), w2s[:, e * HP + g, P * n : P * (n + 1)])
+            still, moving = (h, w) if by_slot else (w, h)
+            nc.tensor.matmul_mx(
+                out=bank[:, n - n0, :],
+                lhsT=still[0],
+                lhsT_scale=still[1],
+                rhs=moving[0],
+                rhs_scale=moving[1],
+                start=(g == 0),
+                stop=(g == HP - 1),
+            )
+
+        def second_product(st, n0, n1, bank_no, by_slot=False):
+            y_bank(st, n0, n1, bank_no)
+            for n in range(n0, n1):
+                for g in range(HP):
+                    second_pass(st, n, g, by_slot)
 
         y_rows = {}
 
@@ -263,15 +268,20 @@ def tile_moe_res_mlp_relu2_kernel(tc, xT, xr, w1_words, w1_scales, w2_words, w2_
         def scatter(st, n):
             nc.vector.tensor_tensor(windows[n][:].indirect(slots(st, st + 1)), y_rows[st, n], gates[:, st * P : (st + 1) * P], ALU.mult)
 
-        def finish(n, c0, c1):
-            nc.vector.tensor_add(out=residual[n][:, c0:c1], in0=windows[n][:, c0:c1], in1=residual[n][:, c0:c1])
-            nc.sync.dma_start(out=out[n * P : (n + 1) * P, c0:c1], in_=residual[n][:, c0:c1])
+        totals = {}
+
+        def store(n, c0, c1):
+            nc.sync.dma_start(out=out[n * P : (n + 1) * P, c0:c1], in_=totals[n, c0][:])
+
+        def add(engine, n, c0, c1):
+            totals[n, c0] = new_tile([P, c1 - c0], F32, f"total{n}_{c0}")
+            engine.tensor_tensor(totals[n, c0][:], windows[n][:, c0:c1], residual[n][:, c0:c1], ALU.add)
 
         there = {}
         summed = {}
 
         def open_sum(n, b, bank_no):
-            there[n, b] = psum.tile([P, P], F32, name="there", tag=f"bank{bank_no}")
+            there[n, b] = new_bank([P, P], f"there{b}", bank_no)
             nc.tensor.matmul(there[n, b][:], residual[n][:, b * P : (b + 1) * P], ident[:], start=True, stop=False, is_transpose=True)
 
         def close_sum(n, b):
@@ -284,7 +294,7 @@ def tile_moe_res_mlp_relu2_kernel(tc, xT, xr, w1_words, w1_scales, w2_words, w2_
         backs = {}
 
         def turn_back(n, b0, b1, bank_no):
-            backs[n, b0] = psum.tile([P, b1 - b0, P], F32, name="back", tag=f"bank{bank_no}")
+            backs[n, b0] = new_bank([P, b1 - b0, P], f"back{b0}", bank_no)
             for b in range(b0, b1):
                 nc.tensor.transpose(backs[n, b0][:, b - b0, :], summed[n, b][:], ident[:])
 
@@ -297,48 +307,53 @@ def tile_moe_res_mlp_relu2_kernel(tc, xT, xr, w1_words, w1_scales, w2_words, w2_
         def store_back(n, b0, b1):
             nc.sync.dma_start(out=out[n * P : (n + 1) * P, b0 * P : b1 * P], in_=results[n, b0][:])
 
-        last = {}
+        lists = {}
 
-        def empty_last(st):
-            if not last:
-                last["y"] = new_tile([P, 2, P], F32, "y_last")
-            y_last = last["y"]
-            bank, first = y_banks[st, NT - 1]
-            nc.scalar.activation(y_last[:, st - 2, :], bank[:, NT - 1 - first, :], ACT.Copy)
+        def list_tile(name, tiles):
+            lists[name] = new_tile([P, tiles, P], F32, name)
 
-        def scatter_last():
-            nc.vector.tensor_tensor(windows[NT - 1][:].indirect(slots(2, ST)), last["y"][:].rearrange("p a c -> p (a c)"), gates[:, 2 * P : S], ALU.mult)
+        def empty_into(name, a, st, n):
+            bank, first = y_banks[st, n]
+            nc.scalar.activation(lists[name][:, a, :], bank[:, n - first, :], ACT.Copy)
 
-        def finish_in_two(n, c0, c1):
-            nc.vector.tensor_add(out=residual[n][:, c0:c1], in0=windows[n][:, c0:c1], in1=residual[n][:, c0:c1])
-            mid = (c0 + c1) // 2
-            for a, b in ((c0, mid), (mid, c1)):
-                nc.sync.dma_start(out=out[n * P : (n + 1) * P, a:b], in_=residual[n][:, a:b])
+        def scatter_list(name, n, st0, st1):
+            nc.vector.tensor_tensor(windows[n][:].indirect(slots(st0, st1)), lists[name][:].rearrange("p a c -> p (a c)"), gates[:, st0 * P : st1 * P], ALU.mult)
 
-        def warm_up(count, bank_no):
-            spare = psum.tile([P, 512], F32, name="spare", tag=f"bank{bank_no}")
-            for repeat in range(count):
-                nc.tensor.matmul_mx(
-                    out=spare[:],
-                    lhsT=codes[ST - 1][0][:, 0, :].bitcast(E4M3),
-                    lhsT_scale=codes[ST - 1][1][:, 0, :],
-                    rhs=w1w[1][0][:, 0:1024].bitcast(E2M1),
-                    rhs_scale=w1_planes[1][0][:, 0:512],
-                    start=True,
-                    stop=True,
-                )
+        def gate_into(name, a, st, n):
+            bank, first = y_banks[st, n]
+            nc.vector.tensor_tensor(lists[name][:, a, :], bank[:, n - first, :], gates[:, st * P : (st + 1) * P], ALU.mult)
+
+        def scatter_gated(name, n, st0, st1):
+            nc.vector.tensor_copy(out=windows[n][:].indirect(slots(st0, st1)), in_=lists[name][:].rearrange("p a c -> p (a c)"))
+
+        by_slot = {}
+
+        def gate_by_slot(st, n):
+            bank, first = y_banks[st, n]
+            by_slot[st, n] = new_tile([P, P], F32, f"by_slot{st}_{n}")
+            nc.scalar.activation(by_slot[st, n][:], bank[:, n - first, :], ACT.Copy, scale=gate_col[:, st : st + 1])
+
+        upright = {}
+
+        def turn_gated(n, st0, st1, bank_no):
+            upright[n, st0] = new_bank([P, st1 - st0, P], f"upright{st0}", bank_no)
+            for st in range(st0, st1):
+                nc.tensor.transpose(upright[n, st0][:, st - st0, :], by_slot[st, n][:], ident[:])
+
+        def empty_gated(name, a, n, st0, st1):
+            nc.scalar.activation(lists[name][:, a : a + st1 - st0, :], upright[n, st0][:], ACT.Copy)
 
         group_tokens(0, 0)
         group_tokens(0, 1)
         quantize_tokens(0)
+        group_tokens(1, 0)
         gather_words(0, 0, 2)
         gather_scales(0, 0, 2)
-        group_tokens(1, 0)
         group_tokens(1, 1)
-        first_pass(0, 0, 0)
-        first_pass(1, 0, 0)
-        first_pass(0, 0, 1)
-        first_pass(1, 0, 1)
+        first_pass(0, 0, 0, 0)
+        first_pass(1, 0, 0, 2)
+        first_pass(0, 0, 1, 1)
+        first_pass(1, 0, 1, 3)
         quantize_tokens(1)
         gather_words(0, 2)
         gather_words(1, 0)
@@ -349,50 +364,52 @@ def tile_moe_res_mlp_relu2_kernel(tc, xT, xr, w1_words, w1_scales, w2_words, w2_
         gather_scales(1, 1)
         first_pass(1, 1, 0)
         first_pass(1, 1, 1)
+
         gather_scales(0, 2)
         gather_words(1, 2)
+        gather_scales(1, 2)
         relu(0, 0, parts=2)
         relu(0, 1, on_vector=True)
         relu(1, 0)
         relu(1, 1, on_vector=True)
-        gather_scales(1, 2)
         gather_words(0, 3)
         gather_scales(0, 3)
         gather_words(1, 3)
-        turn(0, 0)
-        turn(0, 1)
-        turn(1, 0)
-        turn(1, 1)
+        turn(0, 0, 4)
+        turn(0, 1, 5)
+        turn(1, 0, 6)
+        turn(1, 1, 7)
         square(0, 0)
         square(0, 1)
-        quantize_hidden(0)
         gather_scales(1, 3)
-        first_pass(2, 0, 0)
+        quantize_hidden(0)
+        first_pass(2, 0, 0, 0)
         first_pass(2, 1, 0)
         square(1, 0)
-        first_pass(2, 0, 1)
+        first_pass(2, 0, 1, 1)
         first_pass(2, 1, 1)
         square(1, 1)
         relu(2, 0, on_vector=True)
         quantize_hidden(1)
-        second_product(0)
+        second_product(0, 0, 1, 2)
+        second_product(0, 1, 3, 3)
         empty(0, 0, 1)
         empty(0, 1, 3)
         relu(2, 1)
         scatter(0, 0)
         scatter(0, 1)
         scatter(0, 2)
-        turn(2, 0)
-        second_product(1)
-        turn(2, 1)
+        turn(2, 0, 2)
+        second_product(1, 0, 3, 3)
+        turn(2, 1, 4)
         square(2, 0)
         empty(1, 0, 1)
         square(2, 1)
         empty(1, 1, 2)
-        first_pass(3, 0, 0)
+        first_pass(3, 0, 0, 1)
         first_pass(3, 1, 0)
         relu(3, 0, parts=2)
-        first_pass(3, 0, 1)
+        first_pass(3, 0, 1, 2)
         first_pass(3, 1, 1)
         relu(3, 1, parts=2)
         empty(1, 2, 3)
@@ -400,41 +417,48 @@ def tile_moe_res_mlp_relu2_kernel(tc, xT, xr, w1_words, w1_scales, w2_words, w2_
         quantize_hidden(2)
         scatter(1, 1)
         scatter(1, 2)
-        turn(3, 0)
-        turn(3, 1)
-        second_product(2)
+        turn(3, 0, 0)
+        turn(3, 1, 5)
+        y_bank(2, 0, 3, 2)
+        second_pass(2, 0, 0)
+        second_pass(2, 0, 1)
+        second_pass(2, 1, 0)
+        second_pass(2, 1, 1)
+        second_pass(2, 2, 0, True)
+        second_pass(2, 2, 1, True)
         square(3, 0)
         square(3, 1)
         empty(2, 0, 1)
         empty(2, 1, 2)
+        gate_by_slot(2, 2)
         quantize_hidden(3)
         scatter(2, 0)
         scatter(2, 1)
-        second_product(3)
+
+        second_product(3, 1, 2, 7, by_slot=True)
+        second_product(3, 0, 1, 6)
+        second_product(3, 2, 3, 3, by_slot=True)
+        gate_by_slot(3, 1)
         empty(3, 0, 1)
-        empty(3, 1, 2)
-        open_sum(0, 0, 0)
-        open_sum(0, 1, 5)
-        open_sum(0, 2, 6)
+        gate_by_slot(3, 2)
+        turn_gated(1, 3, 4, 0)
+        list_tile("y3_1", 1)
+        empty_gated("y3_1", 0, 1, 3, 4)
+        turn_gated(2, 2, 4, 6)
+        list_tile("y_last", 2)
+        empty_gated("y_last", 0, 2, 2, 4)
         scatter(3, 0)
-        empty_last(2)
-        empty_last(3)
-        scatter(3, 1)
-        close_sum(0, 0)
-        close_sum(0, 1)
-        close_sum(0, 2)
-        leave_bank(0, 0)
-        leave_bank(0, 1)
-        leave_bank(0, 2)
-        turn_back(0, 0, 2, 1)
-        turn_back(0, 2, 3, 4)
-        copy_back(0, 0, 2)
-        copy_back(0, 2, 3)
-        finish_in_two(0, 384, 640)
-        finish_in_two(1, 0, 384)
-        store_back(0, 0, 2)
-        store_back(0, 2, 3)
-        scatter_last()
-        finish(1, 384, 640)
-        finish(2, 0, 320)
-        finish(2, 320, 640)
+        scatter_gated("y3_1", 1, 3, 4)
+        add(nc.gpsimd, 0, 0, 640)
+        store(0, 0, 640)
+        add(nc.gpsimd, 1, 0, 128)
+        scatter_gated("y_last", 2, 2, 4)
+        store(1, 0, 128)
+        add(nc.vector, 1, 128, 384)
+        store(1, 128, 384)
+        add(nc.vector, 1, 384, 640)
+        store(1, 384, 640)
+        add(nc.vector, 2, 0, 320)
+        store(2, 0, 320)
+        add(nc.vector, 2, 320, 640)
+        store(2, 320, 640)

@@ -39,11 +39,10 @@ PLACE = {
     "g_scales0_3": 3 * SLOT + 128,
     "g_scales1_3": 3 * SLOT,
     "g_words1_2": 5 * SLOT,
-    "h_words1_0": 5 * SLOT,
     "relu2_1": 6 * SLOT,
     "y1_1": 6 * SLOT,
     "y1_2": 6 * SLOT + 512,
-    "h_words0_0": 6 * SLOT,
+    "h_words0_1": 6 * SLOT,
     "residual0": 9 * SLOT,
     "total1_128": 9 * SLOT - 960,
     "total1_384": 9 * SLOT + 64,
@@ -115,12 +114,15 @@ def tile_moe_res_mlp_relu2_kernel(tc, xT, xr, w1_words, w1_scales, w2_words, w2_
         w1w[0].append(halves)
         load_words(0, 1, 2)
         load_scales(w1s[1], w1s_rows[0, :, :, 1:2, :])
-        load_words(1, 0, KP)
+        late = [new_tile([P, KP, H], U8, f"w1w1_{g}") for g in range(HP)]
+        w1w[1].extend([late[g][:, s, :] for g in range(HP)] for s in range(KP))
+        nc.sync.dma_start(out=late[0][:].bitcast(I32), in_=w1_rows[1, :, :, 0:256])
         load_scales(w1s[2], w1s_rows[1])
         w2w = [new_tile([P, HP, 2 * N], U8, f"w2w{e}") for e in range(E)]
         w2_rows = w2_words.bitcast(I32).rearrange("e s p w -> e p s w")
         nc.sync.dma_start(out=w2w[0][:].bitcast(I32), in_=w2_rows[0])
         load_scales(w2s, w2s_rows)
+        nc.sync.dma_start(out=late[1][:].bitcast(I32), in_=w1_rows[1, :, :, 256:512])
         gates = keep.tile([P, S], F32, name="gates")
         nc.sync.dma_start(out=gates[:], in_=gate[0:P, :])
         nc.sync.dma_start(out=w2w[1][:].bitcast(I32), in_=w2_rows[1])
@@ -182,7 +184,7 @@ def tile_moe_res_mlp_relu2_kernel(tc, xT, xr, w1_words, w1_scales, w2_words, w2_
                 out=sums[st, g][:],
                 lhsT=g_words[s, st].bitcast(E4M3),
                 lhsT_scale=g_scales[s, st],
-                rhs=(w1w[e][s][g][:] if (e, s) == (0, 0) else w1w[e][s][:, g * 1024 : (g + 1) * 1024]).bitcast(E2M1),
+                rhs=(w1w[e][s][:, g * 1024 : (g + 1) * 1024] if (e, s) == (0, 1) else w1w[e][s][g][:]).bitcast(E2M1),
                 rhs_scale=w1_planes[e][s][:, g * 512 : (g + 1) * 512],
                 start=(s == 0),
                 stop=(s == KP - 1),
@@ -273,9 +275,14 @@ def tile_moe_res_mlp_relu2_kernel(tc, xT, xr, w1_words, w1_scales, w2_words, w2_
         def store(n, c0, c1):
             nc.sync.dma_start(out=out[n * P : (n + 1) * P, c0:c1], in_=totals[n, c0][:])
 
-        def add(engine, n, c0, c1):
+        def total(n, c0, c1):
             totals[n, c0] = new_tile([P, c1 - c0], F32, f"total{n}_{c0}")
-            engine.tensor_tensor(totals[n, c0][:], windows[n][:, c0:c1], residual[n][:, c0:c1], ALU.add)
+
+        def add(engine, n, c0, c1, first=None):
+            if first is None:
+                first = c0
+                total(n, c0, c1)
+            engine.tensor_tensor(totals[n, first][:, c0 - first : c1 - first], windows[n][:, c0:c1], residual[n][:, c0:c1], ALU.add)
 
         there = {}
         summed = {}
@@ -381,18 +388,19 @@ def tile_moe_res_mlp_relu2_kernel(tc, xT, xr, w1_words, w1_scales, w2_words, w2_
         turn(1, 1, 7)
         square(0, 0)
         square(0, 1)
+        quantize_hidden(0, 0, 1)
         gather_scales(1, 3)
-        quantize_hidden(0)
+        quantize_hidden(0, 1, 2)
         first_pass(2, 0, 0, 0)
         first_pass(2, 1, 0)
         square(1, 0)
-        first_pass(2, 0, 1, 1)
-        first_pass(2, 1, 1)
         square(1, 1)
         relu(2, 0, on_vector=True)
         quantize_hidden(1)
         second_product(0, 0, 1, 2)
         second_product(0, 1, 3, 3)
+        first_pass(2, 0, 1, 1)
+        first_pass(2, 1, 1)
         empty(0, 0, 1)
         empty(0, 1, 3)
         relu(2, 1)
@@ -431,13 +439,14 @@ def tile_moe_res_mlp_relu2_kernel(tc, xT, xr, w1_words, w1_scales, w2_words, w2_
         empty(2, 0, 1)
         empty(2, 1, 2)
         gate_by_slot(2, 2)
-        quantize_hidden(3)
+        quantize_hidden(3, 0, 1)
+        quantize_hidden(3, 1, 2)
         scatter(2, 0)
         scatter(2, 1)
 
         second_product(3, 1, 2, 7, by_slot=True)
         second_product(3, 0, 1, 6)
-        second_product(3, 2, 3, 3, by_slot=True)
+        second_product(3, 2, 3, 2, by_slot=True)
         gate_by_slot(3, 1)
         empty(3, 0, 1)
         gate_by_slot(3, 2)

@@ -34,15 +34,15 @@ PLACE = {
     "g_scales0_2": 1 * SLOT,
     "g_words1_1": 2 * SLOT + 512,
     "g_words0_3": 2 * SLOT + 64,
-    "g_words1_3": 2 * SLOT + 960,
     "g_scales1_1": 3 * SLOT + 64,
+    "g_scales1_2": 3 * SLOT,
     "g_scales0_3": 3 * SLOT + 128,
-    "g_scales1_3": 3 * SLOT,
-    "g_words1_2": 5 * SLOT,
-    "relu2_1": 6 * SLOT,
-    "y1_1": 6 * SLOT,
-    "y1_2": 6 * SLOT + 512,
+    "relu1_1": 4 * SLOT,
+    "g_words1_3": 4 * SLOT,
+    "hidden0_1": 5 * SLOT,
+    "g_scales1_3": 5 * SLOT,
     "h_words0_1": 6 * SLOT,
+    "relu2_0": 6 * SLOT,
     "residual0": 9 * SLOT,
     "total1_128": 9 * SLOT - 960,
     "total1_384": 9 * SLOT + 64,
@@ -192,10 +192,10 @@ def tile_moe_res_mlp_relu2_kernel(tc, xT, xr, w1_words, w1_scales, w2_words, w2_
 
         relus = {}
 
-        def relu(st, g, on_vector=False, parts=1):
-            r = new_tile([P, 4, P], F32, f"relu{st}_{g}")
+        def relu(st, g, on_vector=False, parts=1, only=None):
+            r = relus[st, g] if (st, g) in relus else new_tile([P, 4, P], F32, f"relu{st}_{g}")
             src = sums[st, g][:].rearrange("p (m t) -> p t m", t=4)
-            for a in range(parts):
+            for a in range(parts) if only is None else (only,):
                 blocks = slice(4 * a // parts, 4 * (a + 1) // parts)
                 if on_vector:
                     nc.vector.tensor_scalar_max(r[:, blocks, :], src[:, blocks, :], 0.0)
@@ -211,10 +211,16 @@ def tile_moe_res_mlp_relu2_kernel(tc, xT, xr, w1_words, w1_scales, w2_words, w2_
                 nc.tensor.transpose(bank[:, t, :], relus[st, g][:, t, :], ident[:])
             turned[st, g] = bank
 
-        hidden = [new_tile([P, HP, P, 4], BF16, f"hidden{st}") for st in range(ST)]
+        hidden = {}
 
         def square(st, g):
-            nc.scalar.activation(hidden[st][:, g, :, :], turned[st, g][:].rearrange("p t c -> p c t"), ACT.Square)
+            if st != 2:
+                hidden[st, g] = new_tile([P, 1, P, 4], BF16, f"hidden{st}_{g}")[:]
+            elif g == 0:
+                both = new_tile([P, HP, P, 4], BF16, f"hidden{st}")
+                hidden[st, 0] = both[:]
+                hidden[st, 1] = both[:, 1:2, :, :]
+            nc.scalar.activation(hidden[st, g][:, 0, :, :], turned[st, g][:].rearrange("p t c -> p c t"), ACT.Square)
 
         codes = {}
 
@@ -224,7 +230,7 @@ def tile_moe_res_mlp_relu2_kernel(tc, xT, xr, w1_words, w1_scales, w2_words, w2_
             nc.vector.quantize_mx(
                 out=h_words[:].rearrange("p g c -> p (g c)").bitcast(E4M3),
                 scales=h_scales[:].rearrange("p g c -> p (g c)"),
-                in_=hidden[st][:, g0:g1, :, :].rearrange("p g c t -> p (g c t)"),
+                in_=hidden[st, g0].rearrange("p g c t -> p (g c t)"),
             )
             for g in range(g0, g1):
                 codes[st, g] = (h_words[:, g - g0, :].bitcast(E4M3), h_scales[:, g - g0, :])
@@ -374,14 +380,13 @@ def tile_moe_res_mlp_relu2_kernel(tc, xT, xr, w1_words, w1_scales, w2_words, w2_
 
         gather_scales(0, 2)
         gather_words(1, 2)
-        gather_scales(1, 2)
         relu(0, 0, parts=2)
         relu(0, 1, on_vector=True)
         relu(1, 0)
         relu(1, 1, on_vector=True)
+        gather_scales(1, 2)
         gather_words(0, 3)
         gather_scales(0, 3)
-        gather_words(1, 3)
         turn(0, 0, 4)
         turn(0, 1, 5)
         turn(1, 0, 6)
@@ -389,45 +394,51 @@ def tile_moe_res_mlp_relu2_kernel(tc, xT, xr, w1_words, w1_scales, w2_words, w2_
         square(0, 0)
         square(0, 1)
         quantize_hidden(0, 0, 1)
-        gather_scales(1, 3)
+        gather_words(1, 3)
         quantize_hidden(0, 1, 2)
+        gather_scales(1, 3)
         first_pass(2, 0, 0, 0)
         first_pass(2, 1, 0)
         square(1, 0)
         square(1, 1)
-        relu(2, 0, on_vector=True)
-        quantize_hidden(1)
+        quantize_hidden(1, 0, 1)
+        quantize_hidden(1, 1, 2)
         second_product(0, 0, 1, 2)
-        second_product(0, 1, 3, 3)
+        second_product(0, 1, 2, 4)
+        second_product(0, 2, 3, 3)
         first_pass(2, 0, 1, 1)
         first_pass(2, 1, 1)
         empty(0, 0, 1)
-        empty(0, 1, 3)
+        empty(0, 1, 2)
+        relu(2, 0)
+        empty(0, 2, 3)
         relu(2, 1)
         scatter(0, 0)
         scatter(0, 1)
         scatter(0, 2)
-        turn(2, 0, 2)
-        second_product(1, 0, 3, 3)
-        turn(2, 1, 4)
-        square(2, 0)
-        empty(1, 0, 1)
-        square(2, 1)
-        empty(1, 1, 2)
-        first_pass(3, 0, 0, 1)
+        first_pass(3, 0, 0, 2)
         first_pass(3, 1, 0)
-        relu(3, 0, parts=2)
-        first_pass(3, 0, 1, 2)
+        turn(2, 0, 5)
+        second_product(1, 0, 1, 0)
+        turn(2, 1, 4)
+        first_pass(3, 0, 1, 1)
         first_pass(3, 1, 1)
-        relu(3, 1, parts=2)
+        relu(3, 0)
+        second_product(1, 1, 3, 2)
+        empty(1, 0, 1)
+        square(2, 0)
+        square(2, 1)
+        relu(3, 1, parts=2, only=0)
+        empty(1, 1, 2)
+        relu(3, 1, parts=2, only=1)
         empty(1, 2, 3)
         scatter(1, 0)
         quantize_hidden(2)
         scatter(1, 1)
         scatter(1, 2)
-        turn(3, 0, 0)
-        turn(3, 1, 5)
-        y_bank(2, 0, 3, 2)
+        turn(3, 0, 6)
+        turn(3, 1, 3)
+        y_bank(2, 0, 3, 1)
         second_pass(2, 0, 0)
         second_pass(2, 0, 1)
         second_pass(2, 1, 0)
@@ -445,15 +456,15 @@ def tile_moe_res_mlp_relu2_kernel(tc, xT, xr, w1_words, w1_scales, w2_words, w2_
         scatter(2, 1)
 
         second_product(3, 1, 2, 7, by_slot=True)
-        second_product(3, 0, 1, 6)
-        second_product(3, 2, 3, 2, by_slot=True)
+        second_product(3, 0, 1, 0)
+        second_product(3, 2, 3, 1, by_slot=True)
         gate_by_slot(3, 1)
         empty(3, 0, 1)
         gate_by_slot(3, 2)
-        turn_gated(1, 3, 4, 0)
+        turn_gated(1, 3, 4, 2)
         list_tile("y3_1", 1)
         empty_gated("y3_1", 0, 1, 3, 4)
-        turn_gated(2, 2, 4, 6)
+        turn_gated(2, 2, 4, 0)
         list_tile("y_last", 2)
         empty_gated("y_last", 0, 2, 2, 4)
         scatter(3, 0)

@@ -19,24 +19,31 @@ ACT = mybir.ActivationFunctionType
 ALU = mybir.AluOpType
 
 P = 128
-KP = K // 512
-HP = H // 512
-ST = S // P
+PASS = 4 * P
+KP = K // PASS
+HP = H // PASS
 NT = N // P
+PER_COLUMN = 16
+HALF_BYTES = 2 * PASS
+HALF_INTS = HALF_BYTES // 4
 
 PIECES = ((0, 256), (256, 384), (384, 640))
 SCALAR_FROM = ((384, 384), (192, 384))
+GPSIMD_COLUMNS = 128
+VECTOR_PIECES = ((1, 128, 384), (1, 384, 640), (2, 0, 320), (2, 320, 640))
+
 SLOT = 4096
+ALIGN = 64
 PLACE = {
     "grouped1_1": 0 * SLOT,
     "g_words0_2": 0 * SLOT,
     "grouped1_2": 1 * SLOT,
     "g_scales0_2": 1 * SLOT,
-    "g_words1_1": 2 * SLOT + 512,
-    "g_words0_3": 2 * SLOT + 64,
-    "g_scales1_1": 3 * SLOT + 64,
+    "g_words1_1": 2 * SLOT + 8 * ALIGN,
+    "g_words0_3": 2 * SLOT + ALIGN,
+    "g_scales1_1": 3 * SLOT + ALIGN,
     "g_scales1_2": 3 * SLOT,
-    "g_scales0_3": 3 * SLOT + 128,
+    "g_scales0_3": 3 * SLOT + 2 * ALIGN,
     "relu1_1": 4 * SLOT,
     "g_words1_3": 4 * SLOT,
     "hidden0_1": 5 * SLOT,
@@ -44,10 +51,10 @@ PLACE = {
     "h_words0_1": 6 * SLOT,
     "relu2_0": 6 * SLOT,
     "residual0": 9 * SLOT,
-    "total1_128": 9 * SLOT - 960,
-    "total1_384": 9 * SLOT + 64,
-    "total2_0": 9 * SLOT + 1088,
-    "total2_320": 9 * SLOT + 2368,
+    "total1_128": 9 * SLOT + ALIGN - 4 * 256,
+    "total1_384": 9 * SLOT + ALIGN,
+    "total2_0": 9 * SLOT + ALIGN + 4 * 256,
+    "total2_320": 9 * SLOT + ALIGN + 4 * (256 + 320),
 }
 
 
@@ -60,13 +67,13 @@ def tile_moe_res_mlp_relu2_kernel(tc, xT, xr, w1_words, w1_scales, w2_words, w2_
 
         def new_tile(shape, dtype, name):
             if name in PLACE:
-                return shared.tile(shape, dtype, name=name, align_bytes=64, offset=PLACE[name])
-            return keep.tile(shape, dtype, name=name, align_bytes=64)
+                return shared.tile(shape, dtype, name=name, align_bytes=ALIGN, offset=PLACE[name])
+            return keep.tile(shape, dtype, name=name, align_bytes=ALIGN)
 
         def new_bank(shape, name, bank_no):
             return psum.tile(shape, F32, name=name, tag=f"bank{bank_no}")
 
-        offsets = keep.tile([P, S // 16], U16, name="offsets")
+        offsets = keep.tile([P, S // PER_COLUMN], U16, name="offsets")
 
         w1s = [new_tile([P, 1, H], U8, "w1s0_0"), new_tile([P, 1, H], U8, "w1s0_1"), new_tile([P, KP, H], U8, "w1s1")]
         w1_planes = [[w1s[0][:, 0, :], w1s[1][:, 0, :]], [w1s[2][:, s, :] for s in range(KP)]]
@@ -83,7 +90,7 @@ def tile_moe_res_mlp_relu2_kernel(tc, xT, xr, w1_words, w1_scales, w2_words, w2_
             nc.vector.memset(windows[n][:], 0.0)
 
         def load_rows(s, u):
-            rows = xT[s * 512 : (s + 1) * 512, :].rearrange("(q u j) w -> u q j w", u=2, j=2)
+            rows = xT[s * PASS : (s + 1) * PASS, :].rearrange("(q u j) w -> u q j w", u=2, j=2)
             t = keep.tile([P, 2, T], F32, name=f"raw{s}_{u}")
             nc.sync.dma_start(out=t[:], in_=rows[u])
             return t
@@ -95,46 +102,43 @@ def tile_moe_res_mlp_relu2_kernel(tc, xT, xr, w1_words, w1_scales, w2_words, w2_
         w1s_rows = w1_scales.bitcast(I32).rearrange("e s (a r) i -> e r a s i", r=4)
         w2s_rows = w2_scales.bitcast(I32).rearrange("e s (a r) i -> r a (e s) i", r=4)
         w1_rows = w1_words.bitcast(I32).rearrange("e s p w -> e p s w")
-        w1w = [[], []]
-
-        def load_words(e, s0, s1):
-            t = new_tile([P, s1 - s0, 2 * H], U8, f"w1w{e}_{s0}")
-            nc.sync.dma_start(out=t[:].bitcast(I32), in_=w1_rows[e, :, s0:s1, :])
-            w1w[e].extend(t[:, s, :] for s in range(s1 - s0))
+        w2_rows = w2_words.bitcast(I32).rearrange("e s p w -> e p s w")
+        w1w = {}
 
         raw = [[load_rows(0, 0), load_rows(0, 1)], [load_rows(1, 0)]]
         nc.sync.dma_start(offsets[:], offs)
         raw[1].append(load_rows(1, 1))
         load_scales(w1s[0], w1s_rows[0, :, :, 0:1, :])
-        halves = []
         for g in range(HP):
-            t = new_tile([P, H], U8, f"w1w0_0_{g}")
-            nc.sync.dma_start(out=t[:].bitcast(I32), in_=w1_rows[0, :, 0, g * 256 : (g + 1) * 256])
-            halves.append(t)
-        w1w[0].append(halves)
-        load_words(0, 1, 2)
+            t = new_tile([P, HALF_BYTES], U8, f"w1w0_0_{g}")
+            nc.sync.dma_start(out=t[:].bitcast(I32), in_=w1_rows[0, :, 0, g * HALF_INTS : (g + 1) * HALF_INTS])
+            w1w[0, 0, g] = t[:]
+        t = new_tile([P, 1, HP * HALF_BYTES], U8, "w1w0_1")
+        nc.sync.dma_start(out=t[:].bitcast(I32), in_=w1_rows[0, :, 1:2, :])
+        for g in range(HP):
+            w1w[0, 1, g] = t[:, 0, g * HALF_BYTES : (g + 1) * HALF_BYTES]
         load_scales(w1s[1], w1s_rows[0, :, :, 1:2, :])
-        late = [new_tile([P, KP, H], U8, f"w1w1_{g}") for g in range(HP)]
-        w1w[1].extend([late[g][:, s, :] for g in range(HP)] for s in range(KP))
-        nc.sync.dma_start(out=late[0][:].bitcast(I32), in_=w1_rows[1, :, :, 0:256])
+        halves1 = [new_tile([P, KP, HALF_BYTES], U8, f"w1w1_{g}") for g in range(HP)]
+        for g in range(HP):
+            for s in range(KP):
+                w1w[1, s, g] = halves1[g][:, s, :]
+        nc.sync.dma_start(out=halves1[0][:].bitcast(I32), in_=w1_rows[1, :, :, 0:HALF_INTS])
         load_scales(w1s[2], w1s_rows[1])
         w2w = [new_tile([P, HP, 2 * N], U8, f"w2w{e}") for e in range(E)]
-        w2_rows = w2_words.bitcast(I32).rearrange("e s p w -> e p s w")
         nc.sync.dma_start(out=w2w[0][:].bitcast(I32), in_=w2_rows[0])
         load_scales(w2s, w2s_rows)
-        nc.sync.dma_start(out=late[1][:].bitcast(I32), in_=w1_rows[1, :, :, 256:512])
+        nc.sync.dma_start(out=halves1[1][:].bitcast(I32), in_=w1_rows[1, :, :, HALF_INTS : 2 * HALF_INTS])
         gates = keep.tile([P, S], F32, name="gates")
         nc.sync.dma_start(out=gates[:], in_=gate[0:P, :])
         nc.sync.dma_start(out=w2w[1][:].bitcast(I32), in_=w2_rows[1])
         residual = [new_tile([P, T], F32, f"residual{n}") for n in range(NT)]
         for n in range(NT):
             nc.sync.dma_start(out=residual[n][:], in_=xr[n * P : (n + 1) * P, :])
-        gate_col = keep.tile([P, ST], F32, name="gate_col")
+        gate_col = keep.tile([P, C // P], F32, name="gate_col")
         with nc.allow_non_contiguous_dma(reason="one gate value a slot, slots on the partitions"):
-            nc.sync.dma_start(out=gate_col[:], in_=gate[0:1, :].rearrange("o (t p) -> p (o t)", p=P))
+            nc.sync.dma_start(out=gate_col[:], in_=gate[0:1, C:S].rearrange("o (t p) -> p (o t)", p=P))
 
         x_words = [new_tile([P, T], U32, f"x_words{s}") for s in range(KP)]
-
         grouped = [[new_tile([P, c1 - c0, 2, 2], BF16, f"grouped{s}_{piece}") for piece, (c0, c1) in enumerate(PIECES)] for s in range(KP)]
 
         def group_tokens(s, u):
@@ -157,7 +161,7 @@ def tile_moe_res_mlp_relu2_kernel(tc, xT, xr, w1_words, w1_scales, w2_words, w2_
                 )
 
         def slots(st0, st1):
-            return offsets[:, st0 * P // 16 : st1 * P // 16]
+            return offsets[:, st0 * P // PER_COLUMN : st1 * P // PER_COLUMN]
 
         g_words = {}
         g_scales = {}
@@ -178,307 +182,224 @@ def tile_moe_res_mlp_relu2_kernel(tc, xT, xr, w1_words, w1_scales, w2_words, w2_
 
         def first_pass(st, s, g, bank_no=None):
             if s == 0:
-                sums[st, g] = new_bank([P, 512], f"sums{st}{g}", bank_no)
+                sums[st, g] = new_bank([P, PASS], f"sums{st}{g}", bank_no)
             e = st * P // C
             nc.tensor.matmul_mx(
                 out=sums[st, g][:],
                 lhsT=g_words[s, st].bitcast(E4M3),
                 lhsT_scale=g_scales[s, st],
-                rhs=(w1w[e][s][:, g * 1024 : (g + 1) * 1024] if (e, s) == (0, 1) else w1w[e][s][g][:]).bitcast(E2M1),
-                rhs_scale=w1_planes[e][s][:, g * 512 : (g + 1) * 512],
+                rhs=w1w[e, s, g].bitcast(E2M1),
+                rhs_scale=w1_planes[e][s][:, g * PASS : (g + 1) * PASS],
                 start=(s == 0),
                 stop=(s == KP - 1),
             )
 
         relus = {}
 
-        def relu(st, g, on_vector=False, parts=1, only=None):
-            r = relus[st, g] if (st, g) in relus else new_tile([P, 4, P], F32, f"relu{st}_{g}")
-            src = sums[st, g][:].rearrange("p (m t) -> p t m", t=4)
-            for a in range(parts) if only is None else (only,):
-                blocks = slice(4 * a // parts, 4 * (a + 1) // parts)
-                if on_vector:
-                    nc.vector.tensor_scalar_max(r[:, blocks, :], src[:, blocks, :], 0.0)
-                else:
-                    nc.scalar.activation(r[:, blocks, :], src[:, blocks, :], ACT.Relu)
-            relus[st, g] = r
+        def relu_operands(st, g, t0, t1):
+            if t0 == 0:
+                relus[st, g] = new_tile([P, 4, P], F32, f"relu{st}_{g}")
+            return relus[st, g][:, t0:t1, :], sums[st, g][:].rearrange("p (m t) -> p t m", t=4)[:, t0:t1, :]
+
+        def relu_on_vector(st, g):
+            nc.vector.tensor_scalar_max(*relu_operands(st, g, 0, 4), 0.0)
+
+        def relu_on_scalar(st, g, t0=0, t1=4):
+            nc.scalar.activation(*relu_operands(st, g, t0, t1), ACT.Relu)
 
         turned = {}
 
         def turn(st, g, bank_no):
-            bank = new_bank([P, 4, P], f"turned{st}{g}", bank_no)
+            turned[st, g] = new_bank([P, 4, P], f"turned{st}{g}", bank_no)
             for t in range(4):
-                nc.tensor.transpose(bank[:, t, :], relus[st, g][:, t, :], ident[:])
-            turned[st, g] = bank
+                nc.tensor.transpose(turned[st, g][:, t, :], relus[st, g][:, t, :], ident[:])
+
+        def hidden_tile(st, g0, halves):
+            return new_tile([P, halves, P, 4], BF16, f"hidden{st}_{g0}")
+
+        def square(st, g, into):
+            nc.scalar.activation(into, turned[st, g][:].rearrange("p t c -> p c t"), ACT.Square)
 
         hidden = {}
 
-        def square(st, g):
-            if st != 2:
-                hidden[st, g] = new_tile([P, 1, P, 4], BF16, f"hidden{st}_{g}")[:]
-            elif g == 0:
-                both = new_tile([P, HP, P, 4], BF16, f"hidden{st}")
-                hidden[st, 0] = both[:]
-                hidden[st, 1] = both[:, 1:2, :, :]
-            nc.scalar.activation(hidden[st, g][:, 0, :, :], turned[st, g][:].rearrange("p t c -> p c t"), ACT.Square)
+        def square_half(st, g):
+            hidden[st, g] = hidden_tile(st, g, 1)
+            square(st, g, hidden[st, g][:, 0, :, :])
 
         codes = {}
 
-        def quantize_hidden(st, g0=0, g1=HP):
-            h_words = new_tile([P, g1 - g0, P], U32, f"h_words{st}_{g0}")
-            h_scales = new_tile([P, g1 - g0, P], U8, f"h_scales{st}_{g0}")
+        def quantize_hidden(st, g0, halves=1):
+            h_words = new_tile([P, halves, P], U32, f"h_words{st}_{g0}")
+            h_scales = new_tile([P, halves, P], U8, f"h_scales{st}_{g0}")
             nc.vector.quantize_mx(
                 out=h_words[:].rearrange("p g c -> p (g c)").bitcast(E4M3),
                 scales=h_scales[:].rearrange("p g c -> p (g c)"),
-                in_=hidden[st, g0].rearrange("p g c t -> p (g c t)"),
+                in_=hidden[st, g0][:].rearrange("p g c t -> p (g c t)"),
             )
-            for g in range(g0, g1):
-                codes[st, g] = (h_words[:, g - g0, :].bitcast(E4M3), h_scales[:, g - g0, :])
+            for a in range(halves):
+                codes[st, g0 + a] = (h_words[:, a, :].bitcast(E4M3), h_scales[:, a, :])
 
-        y_banks = {}
+        y_sums = {}
 
-        def y_bank(st, n0, n1, bank_no):
-            bank = new_bank([P, n1 - n0, P], f"ybank{st}{n0}", bank_no)
-            for n in range(n0, n1):
-                y_banks[st, n] = (bank, n0)
-
-        def second_pass(st, n, g, by_slot=False):
+        def second_product(st, blocks, bank_no, by_slot=()):
             e = st * P // C
-            bank, n0 = y_banks[st, n]
-            h = codes[st, g]
-            w = (w2w[e][:, g, 256 * n : 256 * (n + 1)].bitcast(E2M1), w2s[:, e * HP + g, P * n : P * (n + 1)])
-            still, moving = (h, w) if by_slot else (w, h)
-            nc.tensor.matmul_mx(
-                out=bank[:, n - n0, :],
-                lhsT=still[0],
-                lhsT_scale=still[1],
-                rhs=moving[0],
-                rhs_scale=moving[1],
-                start=(g == 0),
-                stop=(g == HP - 1),
-            )
-
-        def second_product(st, n0, n1, bank_no, by_slot=False):
-            y_bank(st, n0, n1, bank_no)
-            for n in range(n0, n1):
+            bank = new_bank([P, len(blocks), P], f"ybank{st}{blocks[0]}", bank_no)
+            for a, n in enumerate(blocks):
+                y_sums[st, n] = bank[:, a, :]
                 for g in range(HP):
-                    second_pass(st, n, g, by_slot)
+                    h = codes[st, g]
+                    w = (w2w[e][:, g, 2 * P * n : 2 * P * (n + 1)].bitcast(E2M1), w2s[:, e * HP + g, P * n : P * (n + 1)])
+                    still, moving = (h, w) if n in by_slot else (w, h)
+                    nc.tensor.matmul_mx(
+                        out=y_sums[st, n],
+                        lhsT=still[0],
+                        lhsT_scale=still[1],
+                        rhs=moving[0],
+                        rhs_scale=moving[1],
+                        start=(g == 0),
+                        stop=(g == HP - 1),
+                    )
 
         y_rows = {}
 
-        def empty(st, n0, n1):
-            bank, first = y_banks[st, n0]
-            y = new_tile([P, n1 - n0, P], F32, f"y{st}_{n0}")
-            nc.scalar.activation(y[:], bank[:, n0 - first : n1 - first, :], ACT.Copy)
-            for n in range(n0, n1):
-                y_rows[st, n] = y[:, n - n0, :]
+        def empty(st, n):
+            y_rows[st, n] = new_tile([P, P], F32, f"y{st}_{n}")
+            nc.scalar.activation(y_rows[st, n][:], y_sums[st, n], ACT.Copy)
 
         def scatter(st, n):
-            nc.vector.tensor_tensor(windows[n][:].indirect(slots(st, st + 1)), y_rows[st, n], gates[:, st * P : (st + 1) * P], ALU.mult)
+            nc.vector.tensor_tensor(windows[n][:].indirect(slots(st, st + 1)), y_rows[st, n][:], gates[:, st * P : (st + 1) * P], ALU.mult)
 
-        totals = {}
-
-        def store(n, c0, c1):
-            nc.sync.dma_start(out=out[n * P : (n + 1) * P, c0:c1], in_=totals[n, c0][:])
-
-        def total(n, c0, c1):
-            totals[n, c0] = new_tile([P, c1 - c0], F32, f"total{n}_{c0}")
-
-        def add(engine, n, c0, c1, first=None):
-            if first is None:
-                first = c0
-                total(n, c0, c1)
-            engine.tensor_tensor(totals[n, first][:, c0 - first : c1 - first], windows[n][:, c0:c1], residual[n][:, c0:c1], ALU.add)
-
-        there = {}
-        summed = {}
-
-        def open_sum(n, b, bank_no):
-            there[n, b] = new_bank([P, P], f"there{b}", bank_no)
-            nc.tensor.matmul(there[n, b][:], residual[n][:, b * P : (b + 1) * P], ident[:], start=True, stop=False, is_transpose=True)
-
-        def close_sum(n, b):
-            nc.tensor.matmul(there[n, b][:], windows[n][:, b * P : (b + 1) * P], ident[:], start=False, stop=True, is_transpose=True)
-
-        def leave_bank(n, b):
-            summed[n, b] = new_tile([P, P], F32, f"summed{n}_{b}")
-            nc.scalar.activation(summed[n, b][:], there[n, b][:], ACT.Copy)
-
-        backs = {}
-
-        def turn_back(n, b0, b1, bank_no):
-            backs[n, b0] = new_bank([P, b1 - b0, P], f"back{b0}", bank_no)
-            for b in range(b0, b1):
-                nc.tensor.transpose(backs[n, b0][:, b - b0, :], summed[n, b][:], ident[:])
-
-        results = {}
-
-        def copy_back(n, b0, b1):
-            results[n, b0] = new_tile([P, (b1 - b0) * P], F32, f"result{n}_{b0}")
-            nc.scalar.activation(results[n, b0][:], backs[n, b0][:].rearrange("p b c -> p (b c)"), ACT.Copy)
-
-        def store_back(n, b0, b1):
-            nc.sync.dma_start(out=out[n * P : (n + 1) * P, b0 * P : b1 * P], in_=results[n, b0][:])
-
-        lists = {}
-
-        def list_tile(name, tiles):
-            lists[name] = new_tile([P, tiles, P], F32, name)
-
-        def empty_into(name, a, st, n):
-            bank, first = y_banks[st, n]
-            nc.scalar.activation(lists[name][:, a, :], bank[:, n - first, :], ACT.Copy)
-
-        def scatter_list(name, n, st0, st1):
-            nc.vector.tensor_tensor(windows[n][:].indirect(slots(st0, st1)), lists[name][:].rearrange("p a c -> p (a c)"), gates[:, st0 * P : st1 * P], ALU.mult)
-
-        def gate_into(name, a, st, n):
-            bank, first = y_banks[st, n]
-            nc.vector.tensor_tensor(lists[name][:, a, :], bank[:, n - first, :], gates[:, st * P : (st + 1) * P], ALU.mult)
-
-        def scatter_gated(name, n, st0, st1):
-            nc.vector.tensor_copy(out=windows[n][:].indirect(slots(st0, st1)), in_=lists[name][:].rearrange("p a c -> p (a c)"))
-
-        by_slot = {}
+        gated = {}
 
         def gate_by_slot(st, n):
-            bank, first = y_banks[st, n]
-            by_slot[st, n] = new_tile([P, P], F32, f"by_slot{st}_{n}")
-            nc.scalar.activation(by_slot[st, n][:], bank[:, n - first, :], ACT.Copy, scale=gate_col[:, st : st + 1])
-
-        upright = {}
+            gated[st, n] = new_tile([P, P], F32, f"gated{st}_{n}")
+            nc.scalar.activation(gated[st, n][:], y_sums[st, n], ACT.Copy, scale=gate_col[:, st - C // P : st - C // P + 1])
 
         def turn_gated(n, st0, st1, bank_no):
-            upright[n, st0] = new_bank([P, st1 - st0, P], f"upright{st0}", bank_no)
+            bank = new_bank([P, st1 - st0, P], f"upright{n}", bank_no)
             for st in range(st0, st1):
-                nc.tensor.transpose(upright[n, st0][:, st - st0, :], by_slot[st, n][:], ident[:])
+                nc.tensor.transpose(bank[:, st - st0, :], gated[st, n][:], ident[:])
+            values = new_tile([P, st1 - st0, P], F32, f"values{n}")
+            nc.scalar.activation(values[:], bank[:], ACT.Copy)
+            return values
 
-        def empty_gated(name, a, n, st0, st1):
-            nc.scalar.activation(lists[name][:, a : a + st1 - st0, :], upright[n, st0][:], ACT.Copy)
+        def scatter_gated(values, n, st0, st1):
+            nc.vector.tensor_copy(out=windows[n][:].indirect(slots(st0, st1)), in_=values[:].rearrange("p a c -> p (a c)"))
+
+        def add(engine, n, c0, c1):
+            total = new_tile([P, c1 - c0], F32, f"total{n}_{c0}")
+            engine.tensor_tensor(total[:], windows[n][:, c0:c1], residual[n][:, c0:c1], ALU.add)
+            return total
+
+        def store(total, n, c0, c1):
+            nc.sync.dma_start(out=out[n * P : (n + 1) * P, c0:c1], in_=total[:])
 
         group_tokens(0, 0)
         group_tokens(0, 1)
         quantize_tokens(0)
         group_tokens(1, 0)
-        gather_words(0, 0, 2)
-        gather_scales(0, 0, 2)
+        gather_words(0, 0, tiles=2)
+        gather_scales(0, 0, tiles=2)
         group_tokens(1, 1)
-        first_pass(0, 0, 0, 0)
-        first_pass(1, 0, 0, 2)
-        first_pass(0, 0, 1, 1)
-        first_pass(1, 0, 1, 3)
+        for g in range(HP):
+            for st in range(2):
+                first_pass(st, 0, g, bank_no=2 * st + g)
         quantize_tokens(1)
         gather_words(0, 2)
-        gather_words(1, 0)
-        gather_scales(1, 0)
-        first_pass(0, 1, 0)
-        first_pass(0, 1, 1)
-        gather_words(1, 1)
-        gather_scales(1, 1)
-        first_pass(1, 1, 0)
-        first_pass(1, 1, 1)
+        for st in range(2):
+            gather_words(1, st)
+            gather_scales(1, st)
+            for g in range(HP):
+                first_pass(st, 1, g)
 
         gather_scales(0, 2)
         gather_words(1, 2)
-        relu(0, 0, parts=2)
-        relu(0, 1, on_vector=True)
-        relu(1, 0)
-        relu(1, 1, on_vector=True)
+        relu_on_scalar(0, 0, 0, 2)
+        relu_on_scalar(0, 0, 2, 4)
+        relu_on_vector(0, 1)
+        relu_on_scalar(1, 0)
+        relu_on_vector(1, 1)
         gather_scales(1, 2)
         gather_words(0, 3)
         gather_scales(0, 3)
-        turn(0, 0, 4)
-        turn(0, 1, 5)
-        turn(1, 0, 6)
-        turn(1, 1, 7)
-        square(0, 0)
-        square(0, 1)
-        quantize_hidden(0, 0, 1)
+        for st in range(2):
+            for g in range(HP):
+                turn(st, g, bank_no=4 + 2 * st + g)
+        square_half(0, 0)
+        square_half(0, 1)
+        quantize_hidden(0, 0)
         gather_words(1, 3)
-        quantize_hidden(0, 1, 2)
+        quantize_hidden(0, 1)
         gather_scales(1, 3)
-        first_pass(2, 0, 0, 0)
+        first_pass(2, 0, 0, bank_no=0)
         first_pass(2, 1, 0)
-        square(1, 0)
-        square(1, 1)
-        quantize_hidden(1, 0, 1)
-        quantize_hidden(1, 1, 2)
-        second_product(0, 0, 1, 2)
-        second_product(0, 1, 2, 4)
-        second_product(0, 2, 3, 3)
-        first_pass(2, 0, 1, 1)
+        square_half(1, 0)
+        square_half(1, 1)
+        quantize_hidden(1, 0)
+        quantize_hidden(1, 1)
+
+        second_product(0, (0,), bank_no=2)
+        second_product(0, (1,), bank_no=4)
+        second_product(0, (2,), bank_no=3)
+        first_pass(2, 0, 1, bank_no=1)
         first_pass(2, 1, 1)
-        empty(0, 0, 1)
-        empty(0, 1, 2)
-        relu(2, 0)
-        empty(0, 2, 3)
-        relu(2, 1)
-        scatter(0, 0)
-        scatter(0, 1)
-        scatter(0, 2)
-        first_pass(3, 0, 0, 2)
+        empty(0, 0)
+        empty(0, 1)
+        relu_on_scalar(2, 0)
+        empty(0, 2)
+        relu_on_scalar(2, 1)
+        for n in range(NT):
+            scatter(0, n)
+
+        first_pass(3, 0, 0, bank_no=2)
         first_pass(3, 1, 0)
-        turn(2, 0, 5)
-        second_product(1, 0, 1, 0)
-        turn(2, 1, 4)
-        first_pass(3, 0, 1, 1)
+        turn(2, 0, bank_no=5)
+        second_product(1, (0,), bank_no=0)
+        turn(2, 1, bank_no=4)
+        first_pass(3, 0, 1, bank_no=1)
         first_pass(3, 1, 1)
-        relu(3, 0)
-        second_product(1, 1, 3, 2)
-        empty(1, 0, 1)
-        square(2, 0)
-        square(2, 1)
-        relu(3, 1, parts=2, only=0)
-        empty(1, 1, 2)
-        relu(3, 1, parts=2, only=1)
-        empty(1, 2, 3)
+        relu_on_scalar(3, 0)
+        second_product(1, (1, 2), bank_no=2)
+        empty(1, 0)
+        hidden[2, 0] = hidden_tile(2, 0, HP)
+        for g in range(HP):
+            square(2, g, hidden[2, 0][:, g, :, :])
+        relu_on_scalar(3, 1, 0, 2)
+        empty(1, 1)
+        relu_on_scalar(3, 1, 2, 4)
+        empty(1, 2)
         scatter(1, 0)
-        quantize_hidden(2)
+        quantize_hidden(2, 0, halves=HP)
         scatter(1, 1)
         scatter(1, 2)
-        turn(3, 0, 6)
-        turn(3, 1, 3)
-        y_bank(2, 0, 3, 1)
-        second_pass(2, 0, 0)
-        second_pass(2, 0, 1)
-        second_pass(2, 1, 0)
-        second_pass(2, 1, 1)
-        second_pass(2, 2, 0, True)
-        second_pass(2, 2, 1, True)
-        square(3, 0)
-        square(3, 1)
-        empty(2, 0, 1)
-        empty(2, 1, 2)
+
+        turn(3, 0, bank_no=6)
+        turn(3, 1, bank_no=3)
+        second_product(2, (0, 1, 2), bank_no=1, by_slot=(2,))
+        square_half(3, 0)
+        square_half(3, 1)
+        empty(2, 0)
+        empty(2, 1)
         gate_by_slot(2, 2)
-        quantize_hidden(3, 0, 1)
-        quantize_hidden(3, 1, 2)
+        quantize_hidden(3, 0)
+        quantize_hidden(3, 1)
         scatter(2, 0)
         scatter(2, 1)
 
-        second_product(3, 1, 2, 7, by_slot=True)
-        second_product(3, 0, 1, 0)
-        second_product(3, 2, 3, 1, by_slot=True)
+        second_product(3, (1,), bank_no=7, by_slot=(1,))
+        second_product(3, (0,), bank_no=0)
+        second_product(3, (2,), bank_no=1, by_slot=(2,))
         gate_by_slot(3, 1)
-        empty(3, 0, 1)
+        empty(3, 0)
         gate_by_slot(3, 2)
-        turn_gated(1, 3, 4, 2)
-        list_tile("y3_1", 1)
-        empty_gated("y3_1", 0, 1, 3, 4)
-        turn_gated(2, 2, 4, 0)
-        list_tile("y_last", 2)
-        empty_gated("y_last", 0, 2, 2, 4)
+        values1 = turn_gated(1, 3, 4, bank_no=2)
+        values2 = turn_gated(2, 2, 4, bank_no=0)
+
         scatter(3, 0)
-        scatter_gated("y3_1", 1, 3, 4)
-        add(nc.gpsimd, 0, 0, 640)
-        store(0, 0, 640)
-        add(nc.gpsimd, 1, 0, 128)
-        scatter_gated("y_last", 2, 2, 4)
-        store(1, 0, 128)
-        add(nc.vector, 1, 128, 384)
-        store(1, 128, 384)
-        add(nc.vector, 1, 384, 640)
-        store(1, 384, 640)
-        add(nc.vector, 2, 0, 320)
-        store(2, 0, 320)
-        add(nc.vector, 2, 320, 640)
-        store(2, 320, 640)
+        scatter_gated(values1, 1, 3, 4)
+        store(add(nc.gpsimd, 0, 0, T), 0, 0, T)
+        head1 = add(nc.gpsimd, 1, 0, GPSIMD_COLUMNS)
+        scatter_gated(values2, 2, 2, 4)
+        store(head1, 1, 0, GPSIMD_COLUMNS)
+        for n, c0, c1 in VECTOR_PIECES:
+            store(add(nc.vector, n, c0, c1), n, c0, c1)

@@ -214,30 +214,19 @@ def tile_moe_res_mlp_relu2_kernel(tc, xT, xr, w1_words, w1_scales, w2_words, w2_
             for t in range(4):
                 nc.tensor.transpose(turned[st, g][:, t, :], relus[st, g][:, t, :], ident[:])
 
-        def hidden_tile(st, g0, halves):
-            return new_tile([P, halves, P, 4], BF16, f"hidden{st}_{g0}")
-
-        def square(st, g, into):
-            nc.scalar.activation(into, turned[st, g][:].rearrange("p t c -> p c t"), ACT.Square)
-
         hidden = {}
 
-        def square_half(st, g):
-            hidden[st, g] = hidden_tile(st, g, 1)
-            square(st, g, hidden[st, g][:, 0, :, :])
+        def square(st, g):
+            hidden[st, g] = new_tile([P, P, 4], BF16, f"hidden{st}_{g}")
+            nc.scalar.activation(hidden[st, g][:], turned[st, g][:].rearrange("p t c -> p c t"), ACT.Square)
 
         codes = {}
 
-        def quantize_hidden(st, g0, halves=1):
-            h_words = new_tile([P, halves, P], U32, f"h_words{st}_{g0}")
-            h_scales = new_tile([P, halves, P], U8, f"h_scales{st}_{g0}")
-            nc.vector.quantize_mx(
-                out=h_words[:].rearrange("p g c -> p (g c)").bitcast(E4M3),
-                scales=h_scales[:].rearrange("p g c -> p (g c)"),
-                in_=hidden[st, g0][:].rearrange("p g c t -> p (g c t)"),
-            )
-            for a in range(halves):
-                codes[st, g0 + a] = (h_words[:, a, :].bitcast(E4M3), h_scales[:, a, :])
+        def quantize_hidden(st, g):
+            h_words = new_tile([P, P], U32, f"h_words{st}_{g}")
+            h_scales = new_tile([P, P], U8, f"h_scales{st}_{g}")
+            nc.vector.quantize_mx(out=h_words[:].bitcast(E4M3), scales=h_scales[:], in_=hidden[st, g][:].rearrange("p c t -> p (c t)"))
+            codes[st, g] = (h_words[:].bitcast(E4M3), h_scales[:])
 
         y_sums = {}
 
@@ -325,16 +314,16 @@ def tile_moe_res_mlp_relu2_kernel(tc, xT, xr, w1_words, w1_scales, w2_words, w2_
         for st in range(2):
             for g in range(HP):
                 turn(st, g, bank_no=4 + 2 * st + g)
-        square_half(0, 0)
-        square_half(0, 1)
+        square(0, 0)
+        square(0, 1)
         quantize_hidden(0, 0)
         gather_words(1, 3)
         quantize_hidden(0, 1)
         gather_scales(1, 3)
         first_pass(2, 0, 0, bank_no=0)
         first_pass(2, 1, 0)
-        square_half(1, 0)
-        square_half(1, 1)
+        square(1, 0)
+        square(1, 1)
         quantize_hidden(1, 0)
         quantize_hidden(1, 1)
 
@@ -359,25 +348,26 @@ def tile_moe_res_mlp_relu2_kernel(tc, xT, xr, w1_words, w1_scales, w2_words, w2_
         first_pass(3, 0, 1, bank_no=1)
         first_pass(3, 1, 1)
         relu_on_scalar(3, 0)
-        second_product(1, (1, 2), bank_no=2)
+        second_product(1, (1,), bank_no=2)
         empty(1, 0)
-        hidden[2, 0] = hidden_tile(2, 0, HP)
-        for g in range(HP):
-            square(2, g, hidden[2, 0][:, g, :, :])
-        relu_on_scalar(3, 1, 0, 2)
+        second_product(1, (2,), bank_no=0)
+        square(2, 0)
+        square(2, 1)
         empty(1, 1)
+        relu_on_scalar(3, 1, 0, 2)
         relu_on_scalar(3, 1, 2, 4)
         empty(1, 2)
         scatter(1, 0)
-        quantize_hidden(2, 0, halves=HP)
+        quantize_hidden(2, 0)
+        quantize_hidden(2, 1)
         scatter(1, 1)
         scatter(1, 2)
 
         turn(3, 0, bank_no=6)
         turn(3, 1, bank_no=3)
         second_product(2, (0, 1, 2), bank_no=1, by_slot=(2,))
-        square_half(3, 0)
-        square_half(3, 1)
+        square(3, 0)
+        square(3, 1)
         empty(2, 0)
         empty(2, 1)
         gate_by_slot(2, 2)

@@ -26,35 +26,26 @@ NT = N // P
 PER_COLUMN = 16
 HALF_BYTES = 2 * PASS
 HALF_INTS = HALF_BYTES // 4
-
-PIECES = ((0, 256), (256, 384), (384, 640))
-SCALAR_FROM = ((384, 384), (192, 384))
-GPSIMD_COLUMNS = 128
-VECTOR_PIECES = ((1, 128, 384), (1, 384, 640), (2, 0, 320), (2, 320, 640))
-
-SLOT = 4096
 ALIGN = 64
+SLOT = 4096
+
+GROUPS = (((0, 2), (2, 2)), ((1, 1), (2, 2)))
+SCALE_GROUPS = ((0, 0, 1), (0, 1, 2), (1, 0, 2))
+LISTS = (((0, 1), (1, 2), (2, 3), (3, 4)), ((0, 1), (1, 2), (2, 3), (3, 4)), ((0, 1), (1, 2), (2, 4)))
 PLACE = {
-    "grouped1_1": 0 * SLOT,
-    "g_words0_2": 0 * SLOT,
-    "grouped1_2": 1 * SLOT,
-    "g_scales0_2": 1 * SLOT,
-    "g_words1_1": 2 * SLOT + 8 * ALIGN,
-    "g_words0_3": 2 * SLOT + ALIGN,
-    "g_scales1_1": 3 * SLOT + ALIGN,
-    "g_scales1_2": 3 * SLOT,
-    "g_scales0_3": 3 * SLOT + 2 * ALIGN,
-    "relu1_1": 4 * SLOT,
-    "g_words1_3": 4 * SLOT,
-    "hidden0_1": 5 * SLOT,
-    "g_scales1_3": 5 * SLOT,
-    "h_words0_1": 6 * SLOT,
+    "x1_0_words": 0 * SLOT,
+    "woven1_2": 0 * SLOT,
+    "x1_1_words": 1 * SLOT,
+    "woven0_3": 1 * SLOT,
+    "x1_1_scales": 2 * SLOT,
+    "woven1_3": 2 * SLOT,
+    "relu3_0": 3 * SLOT,
+    "values1_1": 3 * SLOT,
+    "values1_2": 3 * SLOT + 512,
+    "w1w1_0_0": 5 * SLOT,
+    "values1_0": 5 * SLOT,
+    "hidden0_1": 6 * SLOT,
     "relu2_0": 6 * SLOT,
-    "residual0": 9 * SLOT,
-    "total1_128": 9 * SLOT + ALIGN - 4 * 256,
-    "total1_384": 9 * SLOT + ALIGN,
-    "total2_0": 9 * SLOT + ALIGN + 4 * 256,
-    "total2_320": 9 * SLOT + ALIGN + 4 * (256 + 320),
 }
 
 
@@ -75,108 +66,108 @@ def tile_moe_res_mlp_relu2_kernel(tc, xT, xr, w1_words, w1_scales, w2_words, w2_
 
         offsets = keep.tile([P, S // PER_COLUMN], U16, name="offsets")
 
-        w1s = [new_tile([P, 1, H], U8, "w1s0_0"), new_tile([P, 1, H], U8, "w1s0_1"), new_tile([P, KP, H], U8, "w1s1")]
-        w1_planes = [[w1s[0][:, 0, :], w1s[1][:, 0, :]], [w1s[2][:, s, :] for s in range(KP)]]
+        w1s = {(e, s0): new_tile([P, s1 - s0, H], U8, f"w1s{e}_{s0}") for e, s0, s1 in SCALE_GROUPS}
         w2s = new_tile([P, E * HP, N], U8, "w2s")
-        for plane in (*w1s, w2s):
+        for plane in (*w1s.values(), w2s):
             nc.vector.memset(plane[:].rearrange("p g i -> p (g i)").bitcast(I32), 0)
-        x_scales = [new_tile([P, T], U8, f"x_scales{s}") for s in range(KP)]
-        for s in range(KP):
-            nc.vector.memset(x_scales[s][:].bitcast(I32), 0)
         ident = keep.tile([P, P], F32, name="ident")
         make_identity(nc, ident[:])
         windows = [keep.tile([P, T], F32, name=f"window{n}") for n in range(NT)]
         for n in range(NT):
             nc.vector.memset(windows[n][:], 0.0)
 
-        def load_rows(s, u):
-            rows = xT[s * PASS : (s + 1) * PASS, :].rearrange("(q u j) w -> u q j w", u=2, j=2)
-            t = keep.tile([P, 2, T], F32, name=f"raw{s}_{u}")
-            nc.sync.dma_start(out=t[:], in_=rows[u])
-            return t
+        def w1_plane(e, s, g):
+            s0 = max(c[1] for c in SCALE_GROUPS if c[0] == e and c[1] <= s)
+            return w1s[e, s0][:, s - s0, g * PASS : (g + 1) * PASS]
 
-        def load_scales(plane, rows):
+        rows = {}
+
+        def load_row(s, j):
+            rows[s, j] = keep.tile([P, T], F32, name=f"row{s}_{j}")
+            nc.sync.dma_start(out=rows[s, j][:], in_=xT[s * PASS : (s + 1) * PASS, :].rearrange("(q j) w -> j q w", j=4)[j])
+
+        def load_scales(plane, src):
             for r in range(4):
-                nc.sync.dma_start(out=plane[r:P:32, :, :].bitcast(I32), in_=rows[r])
+                nc.sync.dma_start(out=plane[r:P:32, :, :].bitcast(I32), in_=src[r])
 
-        w1s_rows = w1_scales.bitcast(I32).rearrange("e s (a r) i -> e r a s i", r=4)
+        w1s_rows = w1_scales.bitcast(I32).rearrange("e s (a r) i -> r a (e s) i", r=4)
         w2s_rows = w2_scales.bitcast(I32).rearrange("e s (a r) i -> r a (e s) i", r=4)
         w1_rows = w1_words.bitcast(I32).rearrange("e s p w -> e p s w")
         w2_rows = w2_words.bitcast(I32).rearrange("e s p w -> e p s w")
         w1w = {}
 
-        raw = [[load_rows(0, 0), load_rows(0, 1)], [load_rows(1, 0)]]
-        nc.sync.dma_start(offsets[:], offs)
-        raw[1].append(load_rows(1, 1))
-        load_scales(w1s[0], w1s_rows[0, :, :, 0:1, :])
-        for g in range(HP):
-            t = new_tile([P, HALF_BYTES], U8, f"w1w0_0_{g}")
-            nc.sync.dma_start(out=t[:].bitcast(I32), in_=w1_rows[0, :, 0, g * HALF_INTS : (g + 1) * HALF_INTS])
-            w1w[0, 0, g] = t[:]
-        t = new_tile([P, 1, HP * HALF_BYTES], U8, "w1w0_1")
-        nc.sync.dma_start(out=t[:].bitcast(I32), in_=w1_rows[0, :, 1:2, :])
-        for g in range(HP):
-            w1w[0, 1, g] = t[:, 0, g * HALF_BYTES : (g + 1) * HALF_BYTES]
-        load_scales(w1s[1], w1s_rows[0, :, :, 1:2, :])
-        halves1 = [new_tile([P, KP, HALF_BYTES], U8, f"w1w1_{g}") for g in range(HP)]
-        for g in range(HP):
-            for s in range(KP):
-                w1w[1, s, g] = halves1[g][:, s, :]
-        nc.sync.dma_start(out=halves1[0][:].bitcast(I32), in_=w1_rows[1, :, :, 0:HALF_INTS])
-        load_scales(w1s[2], w1s_rows[1])
+        def load_w1(e, s0, s1, g0, g1):
+            t = new_tile([P, s1 - s0, (g1 - g0) * HALF_BYTES], U8, f"w1w{e}_{s0}_{g0}")
+            nc.sync.dma_start(out=t[:].bitcast(I32), in_=w1_rows[e, :, s0:s1, g0 * HALF_INTS : g1 * HALF_INTS])
+            for s in range(s0, s1):
+                for g in range(g0, g1):
+                    w1w[e, s, g] = t[:, s - s0, (g - g0) * HALF_BYTES : (g - g0 + 1) * HALF_BYTES]
+
+        def load_w1_scales(group):
+            e, s0, s1 = SCALE_GROUPS[group]
+            load_scales(w1s[e, s0], w1s_rows[:, :, e * KP + s0 : e * KP + s1, :])
+
         w2w = [new_tile([P, HP, 2 * N], U8, f"w2w{e}") for e in range(E)]
-        nc.sync.dma_start(out=w2w[0][:].bitcast(I32), in_=w2_rows[0])
-        load_scales(w2s, w2s_rows)
-        nc.sync.dma_start(out=halves1[1][:].bitcast(I32), in_=w1_rows[1, :, :, HALF_INTS : 2 * HALF_INTS])
         gates = keep.tile([P, S], F32, name="gates")
-        nc.sync.dma_start(out=gates[:], in_=gate[0:P, :])
-        nc.sync.dma_start(out=w2w[1][:].bitcast(I32), in_=w2_rows[1])
         residual = [new_tile([P, T], F32, f"residual{n}") for n in range(NT)]
+
+        nc.sync.dma_start(offsets[:], offs)
+        for j in range(4):
+            load_row(0, j)
+        load_row(1, 0)
+        load_w1_scales(0)
+        load_w1(0, 0, 1, 0, 2)
+        for j in range(1, 4):
+            load_row(1, j)
+        load_w1(0, 1, 2, 0, 2)
+        load_w1_scales(1)
+        load_w1(1, 0, 2, 0, 1)
+        load_w1_scales(2)
+        load_w1(1, 0, 2, 1, 2)
+        nc.sync.dma_start(out=w2w[0][:].bitcast(I32), in_=w2_rows[0])
+        nc.sync.dma_start(out=gates[:], in_=gate[0:P, :])
+        load_scales(w2s, w2s_rows)
+        nc.sync.dma_start(out=w2w[1][:].bitcast(I32), in_=w2_rows[1])
         for n in range(NT):
             nc.sync.dma_start(out=residual[n][:], in_=xr[n * P : (n + 1) * P, :])
-        gate_col = keep.tile([P, C // P], F32, name="gate_col")
-        with nc.allow_non_contiguous_dma(reason="one gate value a slot, slots on the partitions"):
-            nc.sync.dma_start(out=gate_col[:], in_=gate[0:1, C:S].rearrange("o (t p) -> p (o t)", p=P))
-
-        x_words = [new_tile([P, T], U32, f"x_words{s}") for s in range(KP)]
-        grouped = [[new_tile([P, c1 - c0, 2, 2], BF16, f"grouped{s}_{piece}") for piece, (c0, c1) in enumerate(PIECES)] for s in range(KP)]
-
-        def group_tokens(s, u):
-            cut = SCALAR_FROM[s][u]
-            for t, (c0, c1) in zip(grouped[s], PIECES):
-                for a, b in ((c0, min(c1, cut)), (max(c0, cut), c1)):
-                    if a < b:
-                        src = raw[s][u][:, :, a:b].rearrange("p j c -> p c j")
-                        if a >= cut:
-                            nc.scalar.activation(t[:, a - c0 : b - c0, u, :], src, ACT.Copy)
-                        else:
-                            nc.vector.tensor_copy(out=t[:, a - c0 : b - c0, u, :], in_=src)
-
-        def quantize_tokens(s):
-            for t, (c0, c1) in zip(grouped[s], PIECES):
-                nc.vector.quantize_mx(
-                    out=x_words[s][:, c0:c1].bitcast(E4M3),
-                    scales=x_scales[s][:, c0:c1],
-                    in_=t[:].rearrange("p w u j -> p (w u j)"),
-                )
 
         def slots(st0, st1):
             return offsets[:, st0 * P // PER_COLUMN : st1 * P // PER_COLUMN]
 
-        g_words = {}
-        g_scales = {}
+        picked = {(s, st): new_tile([P, 4, n * P], BF16, f"picked{s}_{st}") for s in range(KP) for st, n in GROUPS[s]}
+        woven = {}
 
-        def gather_words(s, st0, tiles=1):
-            t = new_tile([P, tiles, P], U32, f"g_words{s}_{st0}")
-            nc.vector.tensor_copy(out=t[:].rearrange("p a c -> p (a c)"), in_=x_words[s][:].indirect(slots(st0, st0 + tiles)))
-            for a in range(tiles):
-                g_words[s, st0 + a] = t[:, a, :]
+        def pick(on_scalar, s, j, st0):
+            src = rows[s, j][:].indirect(slots(st0, st0 + dict(GROUPS[s])[st0]))
+            if on_scalar:
+                nc.scalar.activation(picked[s, st0][:, j, :], src, ACT.Copy)
+            else:
+                nc.vector.tensor_copy(out=picked[s, st0][:, j, :], in_=src)
 
-        def gather_scales(s, st0, tiles=1):
-            t = new_tile([P, tiles, P], U8, f"g_scales{s}_{st0}")
-            nc.vector.tensor_copy(out=t[:].rearrange("p a c -> p (a c)"), in_=x_scales[s][:].indirect(slots(st0, st0 + tiles)))
-            for a in range(tiles):
-                g_scales[s, st0 + a] = t[:, a, :]
+        def weave(on_scalar, s, st):
+            st0 = max(a for a, n in GROUPS[s] if a <= st)
+            woven[s, st] = new_tile([P, P, 4], BF16, f"woven{s}_{st}")
+            src = picked[s, st0][:, :, (st - st0) * P : (st - st0 + 1) * P].rearrange("p j c -> p c j")
+            if on_scalar:
+                nc.scalar.activation(woven[s, st][:], src, ACT.Copy)
+            else:
+                nc.vector.tensor_copy(out=woven[s, st][:], in_=src)
+
+        def pick_woven(s, j, st):
+            if j == 0:
+                woven[s, st] = new_tile([P, P, 4], BF16, f"woven{s}_{st}")
+            nc.vector.tensor_copy(out=woven[s, st][:, :, j], in_=rows[s, j][:].indirect(slots(st, st + 1)))
+
+        x_codes = {}
+
+        def quantize(src, name):
+            words = new_tile([P, P], U32, f"{name}_words")
+            scales = new_tile([P, P], U8, f"{name}_scales")
+            nc.vector.quantize_mx(out=words[:].bitcast(E4M3), scales=scales[:], in_=src[:].rearrange("p c t -> p (c t)"))
+            return words[:].bitcast(E4M3), scales[:]
+
+        def quantize_slots(s, st):
+            x_codes[s, st] = quantize(woven[s, st], f"x{s}_{st}")
 
         sums = {}
 
@@ -186,26 +177,25 @@ def tile_moe_res_mlp_relu2_kernel(tc, xT, xr, w1_words, w1_scales, w2_words, w2_
             e = st * P // C
             nc.tensor.matmul_mx(
                 out=sums[st, g][:],
-                lhsT=g_words[s, st].bitcast(E4M3),
-                lhsT_scale=g_scales[s, st],
+                lhsT=x_codes[s, st][0],
+                lhsT_scale=x_codes[s, st][1],
                 rhs=w1w[e, s, g].bitcast(E2M1),
-                rhs_scale=w1_planes[e][s][:, g * PASS : (g + 1) * PASS],
+                rhs_scale=w1_plane(e, s, g),
                 start=(s == 0),
                 stop=(s == KP - 1),
             )
 
         relus = {}
 
-        def relu_operands(st, g, t0, t1):
+        def relu(on_scalar, st, g, t0=0, t1=4):
             if t0 == 0:
                 relus[st, g] = new_tile([P, 4, P], F32, f"relu{st}_{g}")
-            return relus[st, g][:, t0:t1, :], sums[st, g][:].rearrange("p (m t) -> p t m", t=4)[:, t0:t1, :]
-
-        def relu_on_vector(st, g):
-            nc.vector.tensor_scalar_max(*relu_operands(st, g, 0, 4), 0.0)
-
-        def relu_on_scalar(st, g, t0=0, t1=4):
-            nc.scalar.activation(*relu_operands(st, g, t0, t1), ACT.Relu)
+            dst = relus[st, g][:, t0:t1, :]
+            src = sums[st, g][:].rearrange("p (m t) -> p t m", t=4)[:, t0:t1, :]
+            if on_scalar:
+                nc.scalar.activation(dst, src, ACT.Relu)
+            else:
+                nc.vector.tensor_scalar_max(dst, src, 0.0)
 
         turned = {}
 
@@ -220,176 +210,179 @@ def tile_moe_res_mlp_relu2_kernel(tc, xT, xr, w1_words, w1_scales, w2_words, w2_
             hidden[st, g] = new_tile([P, P, 4], BF16, f"hidden{st}_{g}")
             nc.scalar.activation(hidden[st, g][:], turned[st, g][:].rearrange("p t c -> p c t"), ACT.Square)
 
-        codes = {}
+        h_codes = {}
 
         def quantize_hidden(st, g):
-            h_words = new_tile([P, P], U32, f"h_words{st}_{g}")
-            h_scales = new_tile([P, P], U8, f"h_scales{st}_{g}")
-            nc.vector.quantize_mx(out=h_words[:].bitcast(E4M3), scales=h_scales[:], in_=hidden[st, g][:].rearrange("p c t -> p (c t)"))
-            codes[st, g] = (h_words[:].bitcast(E4M3), h_scales[:])
+            h_codes[st, g] = quantize(hidden[st, g], f"h{st}_{g}")
 
         y_sums = {}
 
-        def second_product(st, blocks, bank_no, by_slot=()):
+        def second_pass(st, blocks, g, bank_no=None):
             e = st * P // C
-            bank = new_bank([P, len(blocks), P], f"ybank{st}{blocks[0]}", bank_no)
-            for a, n in enumerate(blocks):
-                y_sums[st, n] = bank[:, a, :]
-                for g in range(HP):
-                    h = codes[st, g]
-                    w = (w2w[e][:, g, 2 * P * n : 2 * P * (n + 1)].bitcast(E2M1), w2s[:, e * HP + g, P * n : P * (n + 1)])
-                    still, moving = (h, w) if n in by_slot else (w, h)
+            if bank_no is not None:
+                bank = new_bank([P, len(blocks), P], f"y{st}_{blocks[0]}", bank_no)
+                for a, n in enumerate(blocks):
+                    y_sums[st, n] = bank[:, a, :]
+            for n in blocks:
+                for gg in g:
                     nc.tensor.matmul_mx(
                         out=y_sums[st, n],
-                        lhsT=still[0],
-                        lhsT_scale=still[1],
-                        rhs=moving[0],
-                        rhs_scale=moving[1],
-                        start=(g == 0),
-                        stop=(g == HP - 1),
+                        lhsT=w2w[e][:, gg, 2 * P * n : 2 * P * (n + 1)].bitcast(E2M1),
+                        lhsT_scale=w2s[:, e * HP + gg, P * n : P * (n + 1)],
+                        rhs=h_codes[st, gg][0],
+                        rhs_scale=h_codes[st, gg][1],
+                        start=(gg == 0),
+                        stop=(gg == HP - 1),
                     )
 
-        y_rows = {}
+        def second_product(st, blocks, bank_no):
+            second_pass(st, blocks, (0, 1), bank_no)
 
-        def empty(st, n):
-            y_rows[st, n] = new_tile([P, P], F32, f"y{st}_{n}")
-            nc.scalar.activation(y_rows[st, n][:], y_sums[st, n], ACT.Copy)
+        lists = {}
 
-        def scatter(st, n):
-            nc.vector.tensor_tensor(windows[n][:].indirect(slots(st, st + 1)), y_rows[st, n][:], gates[:, st * P : (st + 1) * P], ALU.mult)
+        def list_of(st, n):
+            st0, st1 = [c for c in LISTS[n] if c[0] <= st < c[1]][0]
+            if st == st0:
+                lists[st0, n] = new_tile([P, st1 - st0, P], F32, f"values{st0}_{n}")
+            return lists[st0, n][:, st - st0, :]
 
-        gated = {}
+        def apply_gate(st, n):
+            nc.vector.tensor_tensor(list_of(st, n), y_sums[st, n], gates[:, st * P : (st + 1) * P], ALU.mult)
 
-        def gate_by_slot(st, n):
-            gated[st, n] = new_tile([P, P], F32, f"gated{st}_{n}")
-            nc.scalar.activation(gated[st, n][:], y_sums[st, n], ACT.Copy, scale=gate_col[:, st - C // P : st - C // P + 1])
+        def scatter(on_scalar, st0, n):
+            dst = windows[n][:].indirect(slots(st0, dict(LISTS[n])[st0]))
+            src = lists[st0, n][:].rearrange("p a c -> p (a c)")
+            if on_scalar:
+                nc.scalar.activation(dst, src, ACT.Copy)
+            else:
+                nc.vector.tensor_copy(out=dst, in_=src)
 
-        def turn_gated(n, st0, st1, bank_no):
-            bank = new_bank([P, st1 - st0, P], f"upright{n}", bank_no)
-            for st in range(st0, st1):
-                nc.tensor.transpose(bank[:, st - st0, :], gated[st, n][:], ident[:])
-            values = new_tile([P, st1 - st0, P], F32, f"values{n}")
-            nc.scalar.activation(values[:], bank[:], ACT.Copy)
-            return values
-
-        def scatter_gated(values, n, st0, st1):
-            nc.vector.tensor_copy(out=windows[n][:].indirect(slots(st0, st1)), in_=values[:].rearrange("p a c -> p (a c)"))
-
-        def add(engine, n, c0, c1):
+        def add_and_store(engine, n, c0, c1):
             total = new_tile([P, c1 - c0], F32, f"total{n}_{c0}")
             engine.tensor_tensor(total[:], windows[n][:, c0:c1], residual[n][:, c0:c1], ALU.add)
-            return total
-
-        def store(total, n, c0, c1):
             nc.sync.dma_start(out=out[n * P : (n + 1) * P, c0:c1], in_=total[:])
 
-        group_tokens(0, 0)
-        group_tokens(0, 1)
-        quantize_tokens(0)
-        group_tokens(1, 0)
-        gather_words(0, 0, tiles=2)
-        gather_scales(0, 0, tiles=2)
-        group_tokens(1, 1)
-        for g in range(HP):
-            for st in range(2):
-                first_pass(st, 0, g, bank_no=2 * st + g)
-        quantize_tokens(1)
-        gather_words(0, 2)
-        for st in range(2):
-            gather_words(1, st)
-            gather_scales(1, st)
-            for g in range(HP):
-                first_pass(st, 1, g)
-
-        gather_scales(0, 2)
-        gather_words(1, 2)
-        relu_on_scalar(0, 0, 0, 2)
-        relu_on_scalar(0, 0, 2, 4)
-        relu_on_vector(0, 1)
-        relu_on_scalar(1, 0)
-        relu_on_vector(1, 1)
-        gather_scales(1, 2)
-        gather_words(0, 3)
-        gather_scales(0, 3)
-        for st in range(2):
-            for g in range(HP):
-                turn(st, g, bank_no=4 + 2 * st + g)
+        VEC, SCA = False, True
+        pick(SCA, 0, 0, 2)
+        pick(VEC, 0, 0, 0)
+        pick(SCA, 0, 1, 2)
+        pick(VEC, 0, 1, 0)
+        pick(SCA, 0, 2, 2)
+        pick(VEC, 0, 2, 0)
+        pick(SCA, 0, 3, 2)
+        pick(VEC, 0, 3, 0)
+        pick(SCA, 1, 0, 1)
+        weave(VEC, 0, 0)
+        pick(SCA, 1, 0, 2)
+        weave(VEC, 0, 1)
+        pick(SCA, 1, 1, 1)
+        quantize_slots(0, 0)
+        first_pass(0, 0, 0, 0)
+        pick(SCA, 1, 1, 2)
+        pick_woven(1, 0, 0)
+        pick(SCA, 1, 2, 1)
+        quantize_slots(0, 1)
+        first_pass(1, 0, 0, 2)
+        pick(SCA, 1, 3, 1)
+        weave(VEC, 0, 2)
+        first_pass(0, 0, 1, 1)
+        pick(SCA, 1, 2, 2)
+        pick_woven(1, 1, 0)
+        first_pass(1, 0, 1, 3)
+        pick(SCA, 1, 3, 2)
+        quantize_slots(0, 2)
+        pick_woven(1, 2, 0)
+        pick_woven(1, 3, 0)
+        quantize_slots(1, 0)
+        first_pass(0, 1, 0)
+        weave(VEC, 1, 1)
+        first_pass(0, 1, 1)
+        relu(SCA, 0, 1)
+        quantize_slots(1, 1)
+        first_pass(1, 1, 0)
+        relu(SCA, 1, 0)
+        relu(VEC, 0, 0)
+        first_pass(1, 1, 1)
+        weave(VEC, 1, 2)
+        turn(0, 0, 4)
         square(0, 0)
+        relu(VEC, 1, 1)
+        turn(0, 1, 5)
         square(0, 1)
-        quantize_hidden(0, 0)
-        gather_words(1, 3)
-        quantize_hidden(0, 1)
-        gather_scales(1, 3)
-        first_pass(2, 0, 0, bank_no=0)
-        first_pass(2, 1, 0)
+        quantize_slots(1, 2)
+        turn(1, 0, 6)
         square(1, 0)
+        weave(VEC, 0, 3)
+        turn(1, 1, 7)
         square(1, 1)
-        quantize_hidden(1, 0)
-        quantize_hidden(1, 1)
-
-        second_product(0, (0,), bank_no=2)
-        second_product(0, (1,), bank_no=4)
-        second_product(0, (2,), bank_no=3)
-        first_pass(2, 0, 1, bank_no=1)
+        weave(VEC, 1, 3)
+        first_pass(2, 0, 0, 0)
+        quantize_hidden(0, 0)
+        first_pass(2, 1, 0)
+        quantize_slots(0, 3)
+        first_pass(2, 0, 1, 1)
+        quantize_hidden(0, 1)
         first_pass(2, 1, 1)
-        empty(0, 0)
-        empty(0, 1)
-        relu_on_scalar(2, 0)
-        empty(0, 2)
-        relu_on_scalar(2, 1)
-        for n in range(NT):
-            scatter(0, n)
-
-        first_pass(3, 0, 0, bank_no=2)
+        relu(SCA, 2, 1)
+        quantize_slots(1, 3)
+        second_product(0, (0,), 2)
+        relu(VEC, 2, 0)
+        second_product(0, (1,), 3)
+        quantize_hidden(1, 0)
+        second_product(0, (2,), 6)
+        quantize_hidden(1, 1)
+        second_product(1, (0,), 4)
+        apply_gate(0, 0)
+        second_product(1, (1, 2), 5)
+        scatter(SCA, 0, 0)
+        apply_gate(0, 1)
+        first_pass(3, 0, 0, 2)
+        apply_gate(0, 2)
         first_pass(3, 1, 0)
-        turn(2, 0, bank_no=5)
-        second_product(1, (0,), bank_no=0)
-        turn(2, 1, bank_no=4)
-        first_pass(3, 0, 1, bank_no=1)
+        scatter(SCA, 0, 2)
+        scatter(VEC, 0, 1)
+        first_pass(3, 0, 1, 3)
+        relu(VEC, 3, 0)
         first_pass(3, 1, 1)
-        relu_on_scalar(3, 0)
-        second_product(1, (1,), bank_no=2)
-        empty(1, 0)
-        second_product(1, (2,), bank_no=0)
+        apply_gate(1, 0)
+        turn(2, 0, 6)
         square(2, 0)
+        relu(VEC, 3, 1)
+        turn(2, 1, 2)
         square(2, 1)
-        empty(1, 1)
-        relu_on_scalar(3, 1, 0, 2)
-        relu_on_scalar(3, 1, 2, 4)
-        empty(1, 2)
-        scatter(1, 0)
-        quantize_hidden(2, 0)
-        quantize_hidden(2, 1)
-        scatter(1, 1)
-        scatter(1, 2)
-
-        turn(3, 0, bank_no=6)
-        turn(3, 1, bank_no=3)
-        second_product(2, (0, 1, 2), bank_no=1, by_slot=(2,))
+        scatter(VEC, 1, 0)
+        turn(3, 0, 7)
         square(3, 0)
+        quantize_hidden(2, 0)
+        turn(3, 1, 3)
         square(3, 1)
-        empty(2, 0)
-        empty(2, 1)
-        gate_by_slot(2, 2)
+        apply_gate(1, 1)
+        scatter(SCA, 1, 1)
+        quantize_hidden(2, 1)
+        second_product(2, (0, 1, 2), 7)
+        apply_gate(1, 2)
+        scatter(SCA, 1, 2)
         quantize_hidden(3, 0)
+        second_pass(3, (0,), (0,), 5)
         quantize_hidden(3, 1)
-        scatter(2, 0)
-        scatter(2, 1)
-
-        second_product(3, (1,), bank_no=7, by_slot=(1,))
-        second_product(3, (0,), bank_no=0)
-        second_product(3, (2,), bank_no=1, by_slot=(2,))
-        gate_by_slot(3, 1)
-        empty(3, 0)
-        gate_by_slot(3, 2)
-        values1 = turn_gated(1, 3, 4, bank_no=2)
-        values2 = turn_gated(2, 2, 4, bank_no=0)
-
-        scatter(3, 0)
-        scatter_gated(values1, 1, 3, 4)
-        store(add(nc.gpsimd, 0, 0, T), 0, 0, T)
-        head1 = add(nc.gpsimd, 1, 0, GPSIMD_COLUMNS)
-        scatter_gated(values2, 2, 2, 4)
-        store(head1, 1, 0, GPSIMD_COLUMNS)
-        for n, c0, c1 in VECTOR_PIECES:
-            store(add(nc.vector, n, c0, c1), n, c0, c1)
+        second_pass(3, (1,), (0,), 4)
+        apply_gate(2, 0)
+        second_pass(3, (2,), (0,), 6)
+        apply_gate(2, 1)
+        second_pass(3, (0,), (1,))
+        scatter(SCA, 2, 1)
+        apply_gate(2, 2)
+        second_pass(3, (2,), (1,))
+        scatter(VEC, 2, 0)
+        second_pass(3, (1,), (1,))
+        apply_gate(3, 0)
+        apply_gate(3, 2)
+        scatter(SCA, 2, 2)
+        apply_gate(3, 1)
+        scatter(VEC, 3, 0)
+        add_and_store(nc.gpsimd, 0, 0, 384)
+        scatter(VEC, 3, 1)
+        add_and_store(nc.vector, 0, 384, T)
+        add_and_store(nc.vector, 1, 0, T)
+        add_and_store(nc.vector, 2, 0, 384)
+        add_and_store(nc.vector, 2, 384, T)

@@ -134,7 +134,7 @@ def tile_moe_res_mlp_relu2_kernel(tc, xT, xr, w1_words, w1_scales, w2_words, w2_
         def slots(st0, st1):
             return offsets[:, st0 * P // PER_COLUMN : st1 * P // PER_COLUMN]
 
-        picked = {(s, st): new_tile([P, 4, n * P], BF16, f"picked{s}_{st}") for s in range(KP) for st, n in GROUPS[s]}
+        picked = {(s, st): new_tile([P, 4, n * P], F32, f"picked{s}_{st}") for s in range(KP) for st, n in GROUPS[s]}
         woven = {}
 
         def pick(on_scalar, s, j, st0):

@@ -39,13 +39,10 @@ PLACE = {
     "woven0_3": 1 * SLOT,
     "x1_1_scales": 2 * SLOT,
     "woven1_3": 2 * SLOT,
-    "relu3_0": 3 * SLOT,
-    "values1_1": 3 * SLOT,
-    "values1_2": 3 * SLOT + 512,
-    "w1w1_0_0": 5 * SLOT,
-    "values1_0": 5 * SLOT,
-    "hidden0_1": 6 * SLOT,
-    "relu2_0": 6 * SLOT,
+    "hidden0_1": 3 * SLOT,
+    "relu2_0": 3 * SLOT,
+    "relu3_1": 4 * SLOT,
+    "values1_2": 4 * SLOT,
 }
 
 
@@ -123,10 +120,11 @@ def tile_moe_res_mlp_relu2_kernel(tc, xT, xr, w1_words, w1_scales, w2_words, w2_
         load_w1_scales(1)
         load_w1(1, 0, 2, 0, 1)
         load_w1_scales(2)
-        load_w1(1, 0, 2, 1, 2)
+        load_w1(1, 0, 1, 1, 2)
         nc.sync.dma_start(out=w2w[0][:].bitcast(I32), in_=w2_rows[0])
         nc.sync.dma_start(out=gates[:], in_=gate[0:P, :])
         load_scales(w2s, w2s_rows)
+        load_w1(1, 1, 2, 1, 2)
         nc.sync.dma_start(out=w2w[1][:].bitcast(I32), in_=w2_rows[1])
         for n in range(NT):
             nc.sync.dma_start(out=residual[n][:], in_=xr[n * P : (n + 1) * P, :])
@@ -246,6 +244,14 @@ def tile_moe_res_mlp_relu2_kernel(tc, xT, xr, w1_words, w1_scales, w2_words, w2_
                 lists[st0, n] = new_tile([P, st1 - st0, P], F32, f"values{st0}_{n}")
             return lists[st0, n][:, st - st0, :]
 
+        def empty(st, n):
+            nc.scalar.activation(list_of(st, n), y_sums[st, n], ACT.Copy)
+
+        def scatter_times_gate(st0, n):
+            st1 = dict(LISTS[n])[st0]
+            src = lists[st0, n][:].rearrange("p a c -> p (a c)")
+            nc.vector.tensor_tensor(windows[n][:].indirect(slots(st0, st1)), src, gates[:, st0 * P : st1 * P], ALU.mult)
+
         def apply_gate(st, n):
             nc.vector.tensor_tensor(list_of(st, n), y_sums[st, n], gates[:, st * P : (st + 1) * P], ALU.mult)
 
@@ -315,74 +321,77 @@ def tile_moe_res_mlp_relu2_kernel(tc, xT, xr, w1_words, w1_scales, w2_words, w2_
         weave(VEC, 0, 3)
         turn(1, 1, 7)
         square(1, 1)
-        weave(VEC, 1, 3)
-        first_pass(2, 0, 0, 0)
         quantize_hidden(0, 0)
+        first_pass(2, 0, 0, 0)
+        weave(VEC, 1, 3)
         first_pass(2, 1, 0)
-        quantize_slots(0, 3)
-        first_pass(2, 0, 1, 1)
         quantize_hidden(0, 1)
+        first_pass(2, 0, 1, 1)
+        quantize_slots(0, 3)
+        second_product(0, (0,), 2)
+        empty(0, 0)
+        quantize_slots(1, 3)
+        second_product(0, (1,), 3)
+        empty(0, 1)
+        relu(VEC, 2, 0)
+        second_product(0, (2,), 4)
+        empty(0, 2)
+        quantize_hidden(1, 0)
         first_pass(2, 1, 1)
         relu(SCA, 2, 1)
-        quantize_slots(1, 3)
-        second_product(0, (0,), 2)
-        relu(VEC, 2, 0)
-        second_product(0, (1,), 3)
-        quantize_hidden(1, 0)
-        second_product(0, (2,), 6)
         quantize_hidden(1, 1)
-        second_product(1, (0,), 4)
-        apply_gate(0, 0)
-        second_product(1, (1, 2), 5)
-        scatter(SCA, 0, 0)
-        apply_gate(0, 1)
         first_pass(3, 0, 0, 2)
-        apply_gate(0, 2)
+        scatter_times_gate(0, 0)
         first_pass(3, 1, 0)
-        scatter(SCA, 0, 2)
-        scatter(VEC, 0, 1)
-        first_pass(3, 0, 1, 3)
-        relu(VEC, 3, 0)
-        first_pass(3, 1, 1)
-        apply_gate(1, 0)
-        turn(2, 0, 6)
+        relu(SCA, 3, 0)
+        scatter_times_gate(0, 1)
+        turn(2, 0, 3)
         square(2, 0)
-        relu(VEC, 3, 1)
-        turn(2, 1, 2)
-        square(2, 1)
-        scatter(VEC, 1, 0)
-        turn(3, 0, 7)
-        square(3, 0)
+        scatter_times_gate(0, 2)
+        first_pass(3, 0, 1, 4)
+        first_pass(3, 1, 1)
+        second_product(1, (0,), 1)
+        empty(1, 0)
+        scatter_times_gate(1, 0)
+        turn(2, 1, 5)
+        relu(SCA, 3, 1)
         quantize_hidden(2, 0)
-        turn(3, 1, 3)
-        square(3, 1)
-        apply_gate(1, 1)
-        scatter(SCA, 1, 1)
+        second_product(1, (1,), 2)
+        square(2, 1)
         quantize_hidden(2, 1)
-        second_product(2, (0, 1, 2), 7)
+        second_product(1, (2,), 3)
+        empty(1, 1)
         apply_gate(1, 2)
-        scatter(SCA, 1, 2)
+        turn(3, 0, 6)
+        square(3, 0)
+        scatter_times_gate(1, 1)
+        turn(3, 1, 7)
+        square(3, 1)
         quantize_hidden(3, 0)
-        second_pass(3, (0,), (0,), 5)
-        quantize_hidden(3, 1)
-        second_pass(3, (1,), (0,), 4)
+        second_product(2, (0,), 2)
+        scatter(SCA, 1, 2)
         apply_gate(2, 0)
-        second_pass(3, (2,), (0,), 6)
+        second_product(2, (1, 2), 6)
+        scatter(SCA, 2, 0)
+        quantize_hidden(3, 1)
+        second_pass(3, (0,), (0,), 0)
         apply_gate(2, 1)
-        second_pass(3, (0,), (1,))
+        second_pass(3, (1,), (0,), 1)
         scatter(SCA, 2, 1)
         apply_gate(2, 2)
-        second_pass(3, (2,), (1,))
-        scatter(VEC, 2, 0)
-        second_pass(3, (1,), (1,))
+        second_pass(3, (2,), (0,), 5)
+        second_pass(3, (0,), (1,))
         apply_gate(3, 0)
+        second_pass(3, (1,), (1,))
+        scatter(SCA, 3, 0)
+        apply_gate(3, 1)
+        second_pass(3, (2,), (1,))
+        scatter(SCA, 3, 1)
         apply_gate(3, 2)
         scatter(SCA, 2, 2)
-        apply_gate(3, 1)
-        scatter(VEC, 3, 0)
-        add_and_store(nc.gpsimd, 0, 0, 384)
-        scatter(VEC, 3, 1)
-        add_and_store(nc.vector, 0, 384, T)
-        add_and_store(nc.vector, 1, 0, T)
-        add_and_store(nc.vector, 2, 0, 384)
-        add_and_store(nc.vector, 2, 384, T)
+        add_and_store(nc.vector, 0, 0, 320)
+        add_and_store(nc.vector, 0, 320, T)
+        add_and_store(nc.vector, 1, 0, 320)
+        add_and_store(nc.vector, 1, 320, T)
+        add_and_store(nc.vector, 2, 0, 320)
+        add_and_store(nc.vector, 2, 320, T)

@@ -31,15 +31,20 @@ SLOT = 4096
 
 GROUPS = (((0, 2), (2, 2)), ((1, 1), (2, 2)))
 SCALE_GROUPS = ((0, 0, 1), (0, 1, 2), (1, 0, 2))
-LISTS = (((0, 1), (1, 2), (2, 3), (3, 4)), ((0, 1), (1, 2), (2, 3), (3, 4)), ((0, 1), (1, 2), (2, 4)))
+LISTS = (((0, 1), (1, 2), (2, 3), (3, 4)), ((0, 1), (1, 2), (2, 3), (3, 4)), ((0, 1), (1, 2), (2, 3), (3, 4)))
+BY_SLOT = ()
 PLACE = {
     "x1_0_words": 0 * SLOT,
-    "woven1_2": 0 * SLOT,
+    "woven0_2": 0 * SLOT,
+    "x1_0_scales": 5 * SLOT,
+    "woven1_2": 5 * SLOT,
     "x1_1_words": 1 * SLOT,
     "woven0_3": 1 * SLOT,
-    "x1_1_scales": 2 * SLOT,
+    "hidden0_1": 2 * SLOT,
     "woven1_3": 2 * SLOT,
-    "hidden0_1": 3 * SLOT,
+    "hidden0_0": 6 * SLOT,
+    "x0_3_words": 6 * SLOT,
+    "h0_0_words": 3 * SLOT,
     "relu2_0": 3 * SLOT,
     "relu3_1": 4 * SLOT,
     "values1_2": 4 * SLOT,
@@ -79,9 +84,11 @@ def tile_moe_res_mlp_relu2_kernel(tc, xT, xr, w1_words, w1_scales, w2_words, w2_
 
         rows = {}
 
-        def load_row(s, j):
-            rows[s, j] = keep.tile([P, T], F32, name=f"row{s}_{j}")
-            nc.sync.dma_start(out=rows[s, j][:], in_=xT[s * PASS : (s + 1) * PASS, :].rearrange("(q j) w -> j q w", j=4)[j])
+        def load_rows(s, j0, j1):
+            t = keep.tile([P, j1 - j0, T], F32, name=f"rows{s}_{j0}")
+            nc.sync.dma_start(out=t[:], in_=xT[s * PASS : (s + 1) * PASS, :].rearrange("(q j) w -> q j w", j=4)[:, j0:j1, :])
+            for j in range(j0, j1):
+                rows[s, j] = t[:, j - j0, :]
 
         def load_scales(plane, src):
             for r in range(4):
@@ -106,16 +113,18 @@ def tile_moe_res_mlp_relu2_kernel(tc, xT, xr, w1_words, w1_scales, w2_words, w2_
 
         w2w = [new_tile([P, HP, 2 * N], U8, f"w2w{e}") for e in range(E)]
         gates = keep.tile([P, S], F32, name="gates")
+        gate_col = keep.tile([P, S // P], F32, name="gate_col")
         residual = [new_tile([P, T], F32, f"residual{n}") for n in range(NT)]
 
+        load_rows(0, 0, 1)
         nc.sync.dma_start(offsets[:], offs)
-        for j in range(4):
-            load_row(0, j)
-        load_row(1, 0)
+        for j in range(1, 4):
+            load_rows(0, j, j + 1)
+        load_rows(1, 0, 1)
         load_w1_scales(0)
         load_w1(0, 0, 1, 0, 2)
         for j in range(1, 4):
-            load_row(1, j)
+            load_rows(1, j, j + 1)
         load_w1(0, 1, 2, 0, 2)
         load_w1_scales(1)
         load_w1(1, 0, 2, 0, 1)
@@ -135,12 +144,14 @@ def tile_moe_res_mlp_relu2_kernel(tc, xT, xr, w1_words, w1_scales, w2_words, w2_
         picked = {(s, st): new_tile([P, 4, n * P], F32, f"picked{s}_{st}") for s in range(KP) for st, n in GROUPS[s]}
         woven = {}
 
-        def pick(on_scalar, s, j, st0):
-            src = rows[s, j][:].indirect(slots(st0, st0 + dict(GROUPS[s])[st0]))
+        def pick(on_scalar, s, j, a, b):
+            st0 = max(c for c, n in GROUPS[s] if c * P <= a)
+            src = rows[s, j].indirect(offsets[:, a // PER_COLUMN : b // PER_COLUMN])
+            dst = picked[s, st0][:, j, a - st0 * P : b - st0 * P]
             if on_scalar:
-                nc.scalar.activation(picked[s, st0][:, j, :], src, ACT.Copy)
+                nc.scalar.activation(dst, src, ACT.Copy)
             else:
-                nc.vector.tensor_copy(out=picked[s, st0][:, j, :], in_=src)
+                nc.vector.tensor_copy(out=dst, in_=src)
 
         def weave(on_scalar, s, st):
             st0 = max(a for a, n in GROUPS[s] if a <= st)
@@ -154,7 +165,7 @@ def tile_moe_res_mlp_relu2_kernel(tc, xT, xr, w1_words, w1_scales, w2_words, w2_
         def pick_woven(s, j, st):
             if j == 0:
                 woven[s, st] = new_tile([P, P, 4], BF16, f"woven{s}_{st}")
-            nc.vector.tensor_copy(out=woven[s, st][:, :, j], in_=rows[s, j][:].indirect(slots(st, st + 1)))
+            nc.vector.tensor_copy(out=woven[s, st][:, :, j], in_=rows[s, j].indirect(slots(st, st + 1)))
 
         x_codes = {}
 
@@ -169,27 +180,29 @@ def tile_moe_res_mlp_relu2_kernel(tc, xT, xr, w1_words, w1_scales, w2_words, w2_
 
         sums = {}
 
-        def first_pass(st, s, g, bank_no=None):
+        def first_pass(st, s, g, bank_no=None, part=0, parts=1):
+            w = PASS // parts
             if s == 0:
-                sums[st, g] = new_bank([P, PASS], f"sums{st}{g}", bank_no)
+                sums[st, g, part] = new_bank([P, w], f"sums{st}{g}{part}", bank_no)
             e = st * P // C
             nc.tensor.matmul_mx(
-                out=sums[st, g][:],
+                out=sums[st, g, part][:],
                 lhsT=x_codes[s, st][0],
                 lhsT_scale=x_codes[s, st][1],
-                rhs=w1w[e, s, g].bitcast(E2M1),
-                rhs_scale=w1_plane(e, s, g),
+                rhs=w1w[e, s, g][:, 2 * w * part : 2 * w * (part + 1)].bitcast(E2M1),
+                rhs_scale=w1_plane(e, s, g)[:, w * part : w * (part + 1)],
                 start=(s == 0),
                 stop=(s == KP - 1),
             )
 
         relus = {}
 
-        def relu(on_scalar, st, g, t0=0, t1=4):
-            if t0 == 0:
+        def relu(on_scalar, st, g, part=0, parts=1):
+            if (st, g) not in relus:
                 relus[st, g] = new_tile([P, 4, P], F32, f"relu{st}_{g}")
-            dst = relus[st, g][:, t0:t1, :]
-            src = sums[st, g][:].rearrange("p (m t) -> p t m", t=4)[:, t0:t1, :]
+            m = P // parts
+            dst = relus[st, g][:, :, m * part : m * (part + 1)]
+            src = sums[st, g, part][:].rearrange("p (m t) -> p t m", t=4)
             if on_scalar:
                 nc.scalar.activation(dst, src, ACT.Relu)
             else:
@@ -223,12 +236,14 @@ def tile_moe_res_mlp_relu2_kernel(tc, xT, xr, w1_words, w1_scales, w2_words, w2_
                     y_sums[st, n] = bank[:, a, :]
             for n in blocks:
                 for gg in g:
+                    weights = (w2w[e][:, gg, 2 * P * n : 2 * P * (n + 1)].bitcast(E2M1), w2s[:, e * HP + gg, P * n : P * (n + 1)])
+                    left, right = (h_codes[st, gg], weights) if (st, n) in BY_SLOT else (weights, h_codes[st, gg])
                     nc.tensor.matmul_mx(
                         out=y_sums[st, n],
-                        lhsT=w2w[e][:, gg, 2 * P * n : 2 * P * (n + 1)].bitcast(E2M1),
-                        lhsT_scale=w2s[:, e * HP + gg, P * n : P * (n + 1)],
-                        rhs=h_codes[st, gg][0],
-                        rhs_scale=h_codes[st, gg][1],
+                        lhsT=left[0],
+                        lhsT_scale=left[1],
+                        rhs=right[0],
+                        rhs_scale=right[1],
                         start=(gg == 0),
                         stop=(gg == HP - 1),
                     )
@@ -252,6 +267,20 @@ def tile_moe_res_mlp_relu2_kernel(tc, xT, xr, w1_words, w1_scales, w2_words, w2_
             src = lists[st0, n][:].rearrange("p a c -> p (a c)")
             nc.vector.tensor_tensor(windows[n][:].indirect(slots(st0, st1)), src, gates[:, st0 * P : st1 * P], ALU.mult)
 
+        gated = {}
+        upright = {}
+
+        def gate_by_slot(st, n):
+            gated[st, n] = new_tile([P, P], F32, f"gated{st}_{n}")
+            nc.scalar.activation(gated[st, n][:], y_sums[st, n], ACT.Copy, scale=gate_col[:, st : st + 1])
+
+        def turn_gated(st, n, bank_no):
+            upright[st, n] = new_bank([P, P], f"upright{st}_{n}", bank_no)
+            nc.tensor.transpose(upright[st, n][:], gated[st, n][:], ident[:])
+
+        def empty_gated(st, n):
+            nc.scalar.activation(list_of(st, n), upright[st, n][:], ACT.Copy)
+
         def apply_gate(st, n):
             nc.vector.tensor_tensor(list_of(st, n), y_sums[st, n], gates[:, st * P : (st + 1) * P], ALU.mult)
 
@@ -263,51 +292,64 @@ def tile_moe_res_mlp_relu2_kernel(tc, xT, xr, w1_words, w1_scales, w2_words, w2_
             else:
                 nc.vector.tensor_copy(out=dst, in_=src)
 
+        def scatter_part(on_scalar, st0, n, a, b):
+            dst = windows[n][:].indirect(offsets[:, (st0 * P + a) // PER_COLUMN : (st0 * P + b) // PER_COLUMN])
+            src = lists[st0, n][:].rearrange("p a c -> p (a c)")[:, a:b]
+            if on_scalar:
+                nc.scalar.activation(dst, src, ACT.Copy)
+            else:
+                nc.vector.tensor_copy(out=dst, in_=src)
+
         def add_and_store(engine, n, c0, c1):
             total = new_tile([P, c1 - c0], F32, f"total{n}_{c0}")
             engine.tensor_tensor(total[:], windows[n][:, c0:c1], residual[n][:, c0:c1], ALU.add)
             nc.sync.dma_start(out=out[n * P : (n + 1) * P, c0:c1], in_=total[:])
 
         VEC, SCA = False, True
-        pick(SCA, 0, 0, 2)
-        pick(VEC, 0, 0, 0)
-        pick(SCA, 0, 1, 2)
-        pick(VEC, 0, 1, 0)
-        pick(SCA, 0, 2, 2)
-        pick(VEC, 0, 2, 0)
-        pick(SCA, 0, 3, 2)
-        pick(VEC, 0, 3, 0)
-        pick(SCA, 1, 0, 1)
+        pick(SCA, 0, 0, 256, 512)
+        pick(VEC, 0, 0, 0, 256)
+        pick(SCA, 0, 1, 256, 512)
+        pick(VEC, 0, 1, 0, 256)
+        pick(SCA, 0, 2, 256, 512)
+        pick(VEC, 0, 2, 0, 256)
+        pick(SCA, 0, 3, 256, 512)
+        pick(VEC, 0, 3, 0, 256)
+        pick(SCA, 1, 0, 128, 256)
         weave(VEC, 0, 0)
-        pick(SCA, 1, 0, 2)
+        pick(SCA, 1, 0, 256, 512)
         weave(VEC, 0, 1)
-        pick(SCA, 1, 1, 1)
+        pick(SCA, 1, 1, 128, 256)
         quantize_slots(0, 0)
-        first_pass(0, 0, 0, 0)
-        pick(SCA, 1, 1, 2)
+        first_pass(0, 0, 0, 0, 0, 2)
+        pick(SCA, 1, 1, 384, 512)
         pick_woven(1, 0, 0)
-        pick(SCA, 1, 2, 1)
+        first_pass(0, 0, 0, 7, 1, 2)
+        pick(SCA, 1, 2, 128, 256)
         quantize_slots(0, 1)
         first_pass(1, 0, 0, 2)
-        pick(SCA, 1, 3, 1)
-        weave(VEC, 0, 2)
-        first_pass(0, 0, 1, 1)
-        pick(SCA, 1, 2, 2)
+        pick(SCA, 1, 2, 384, 512)
         pick_woven(1, 1, 0)
+        first_pass(0, 0, 1, 1)
+        pick(SCA, 1, 3, 128, 256)
+        pick(VEC, 1, 1, 256, 384)
         first_pass(1, 0, 1, 3)
-        pick(SCA, 1, 3, 2)
-        quantize_slots(0, 2)
+        pick(SCA, 1, 3, 384, 512)
         pick_woven(1, 2, 0)
+        pick(SCA, 1, 3, 256, 384)
+        pick(VEC, 1, 2, 256, 384)
         pick_woven(1, 3, 0)
         quantize_slots(1, 0)
-        first_pass(0, 1, 0)
+        first_pass(0, 1, 0, None, 0, 2)
         weave(VEC, 1, 1)
+        first_pass(0, 1, 0, None, 1, 2)
+        relu(SCA, 0, 0, 1, 2)
+        quantize_slots(1, 1)
         first_pass(0, 1, 1)
         relu(SCA, 0, 1)
-        quantize_slots(1, 1)
+        relu(VEC, 0, 0, 0, 2)
         first_pass(1, 1, 0)
         relu(SCA, 1, 0)
-        relu(VEC, 0, 0)
+        weave(VEC, 0, 2)
         first_pass(1, 1, 1)
         weave(VEC, 1, 2)
         turn(0, 0, 4)
@@ -315,32 +357,33 @@ def tile_moe_res_mlp_relu2_kernel(tc, xT, xr, w1_words, w1_scales, w2_words, w2_
         relu(VEC, 1, 1)
         turn(0, 1, 5)
         square(0, 1)
-        quantize_slots(1, 2)
+        quantize_slots(0, 2)
         turn(1, 0, 6)
         square(1, 0)
-        weave(VEC, 0, 3)
+        quantize_slots(1, 2)
         turn(1, 1, 7)
         square(1, 1)
-        quantize_hidden(0, 0)
+        weave(VEC, 0, 3)
         first_pass(2, 0, 0, 0)
-        weave(VEC, 1, 3)
+        quantize_hidden(0, 0)
         first_pass(2, 1, 0)
-        quantize_hidden(0, 1)
-        first_pass(2, 0, 1, 1)
         quantize_slots(0, 3)
+        first_pass(2, 0, 1, 1)
+        quantize_hidden(0, 1)
         second_product(0, (0,), 2)
         empty(0, 0)
-        quantize_slots(1, 3)
+        weave(VEC, 1, 3)
         second_product(0, (1,), 3)
         empty(0, 1)
-        relu(VEC, 2, 0)
-        second_product(0, (2,), 4)
-        empty(0, 2)
         quantize_hidden(1, 0)
+        second_product(0, (2,), 4)
+        relu(SCA, 2, 0)
+        quantize_slots(1, 3)
         first_pass(2, 1, 1)
-        relu(SCA, 2, 1)
+        empty(0, 2)
         quantize_hidden(1, 1)
         first_pass(3, 0, 0, 2)
+        relu(SCA, 2, 1)
         scatter_times_gate(0, 0)
         first_pass(3, 1, 0)
         relu(SCA, 3, 0)
@@ -348,19 +391,19 @@ def tile_moe_res_mlp_relu2_kernel(tc, xT, xr, w1_words, w1_scales, w2_words, w2_
         turn(2, 0, 3)
         square(2, 0)
         scatter_times_gate(0, 2)
-        first_pass(3, 0, 1, 4)
-        first_pass(3, 1, 1)
-        second_product(1, (0,), 1)
+        second_product(1, (0,), 0)
         empty(1, 0)
         scatter_times_gate(1, 0)
-        turn(2, 1, 5)
-        relu(SCA, 3, 1)
+        first_pass(3, 0, 1, 4)
         quantize_hidden(2, 0)
-        second_product(1, (1,), 2)
+        first_pass(3, 1, 1)
+        relu(SCA, 3, 1)
+        turn(2, 1, 5)
         square(2, 1)
         quantize_hidden(2, 1)
-        second_product(1, (2,), 3)
+        second_product(1, (1,), 2)
         empty(1, 1)
+        second_product(1, (2,), 3)
         apply_gate(1, 2)
         turn(3, 0, 6)
         square(3, 0)
@@ -371,15 +414,16 @@ def tile_moe_res_mlp_relu2_kernel(tc, xT, xr, w1_words, w1_scales, w2_words, w2_
         second_product(2, (0,), 2)
         scatter(SCA, 1, 2)
         apply_gate(2, 0)
-        second_product(2, (1, 2), 6)
+        second_product(2, (2, 1), 6)
         scatter(SCA, 2, 0)
         quantize_hidden(3, 1)
         second_pass(3, (0,), (0,), 0)
-        apply_gate(2, 1)
-        second_pass(3, (1,), (0,), 1)
-        scatter(SCA, 2, 1)
         apply_gate(2, 2)
+        second_pass(3, (1,), (0,), 1)
+        scatter(SCA, 2, 2)
+        apply_gate(2, 1)
         second_pass(3, (2,), (0,), 5)
+        scatter(VEC, 2, 1)
         second_pass(3, (0,), (1,))
         apply_gate(3, 0)
         second_pass(3, (1,), (1,))
@@ -388,7 +432,7 @@ def tile_moe_res_mlp_relu2_kernel(tc, xT, xr, w1_words, w1_scales, w2_words, w2_
         second_pass(3, (2,), (1,))
         scatter(SCA, 3, 1)
         apply_gate(3, 2)
-        scatter(SCA, 2, 2)
+        scatter(SCA, 3, 2)
         add_and_store(nc.vector, 0, 0, 320)
         add_and_store(nc.vector, 0, 320, T)
         add_and_store(nc.vector, 1, 0, 320)

@@ -48,6 +48,9 @@ PLACE = {
     "relu2_0": 3 * SLOT,
     "relu3_1": 4 * SLOT,
     "values1_2": 4 * SLOT,
+    "values3_1": 7 * SLOT,
+    "total0_0": 7 * SLOT - 1024,
+    "total0_320": 7 * SLOT + 256,
 }
 
 
@@ -424,18 +427,18 @@ def tile_moe_res_mlp_relu2_kernel(tc, xT, xr, w1_words, w1_scales, w2_words, w2_
         apply_gate(2, 1)
         second_pass(3, (2,), (0,), 5)
         scatter(VEC, 2, 1)
+        second_pass(3, (1,), (1,))
+        apply_gate(3, 1)
         second_pass(3, (0,), (1,))
         apply_gate(3, 0)
-        second_pass(3, (1,), (1,))
-        scatter(SCA, 3, 0)
-        apply_gate(3, 1)
         second_pass(3, (2,), (1,))
-        scatter(SCA, 3, 1)
+        scatter(SCA, 3, 0)
         apply_gate(3, 2)
         scatter(SCA, 3, 2)
-        add_and_store(nc.vector, 0, 0, 320)
-        add_and_store(nc.vector, 0, 320, T)
+        scatter(VEC, 3, 1)
         add_and_store(nc.vector, 1, 0, 320)
         add_and_store(nc.vector, 1, 320, T)
+        add_and_store(nc.vector, 0, 0, 320)
+        add_and_store(nc.vector, 0, 320, T)
         add_and_store(nc.vector, 2, 0, 320)
         add_and_store(nc.vector, 2, 320, T)

@@ -23,34 +23,37 @@ PASS = 4 * P
 KP = K // PASS
 HP = H // PASS
 NT = N // P
+ST = S // P
 PER_COLUMN = 16
 HALF_BYTES = 2 * PASS
 HALF_INTS = HALF_BYTES // 4
 ALIGN = 64
-SLOT = 4096
+SLOT = 2048
 
-GROUPS = (((0, 2), (2, 2)), ((1, 1), (2, 2)))
 SCALE_GROUPS = ((0, 0, 1), (0, 1, 2), (1, 0, 2))
-LISTS = (((0, 1), (1, 2), (2, 3), (3, 4)), ((0, 1), (1, 2), (2, 3), (3, 4)), ((0, 1), (1, 2), (2, 3), (3, 4)))
-BY_SLOT = ()
+GROUPS = (((0, 2), (2, 4)), ((1, 2), (2, 4)))
 PLACE = {
-    "x1_0_words": 0 * SLOT,
-    "woven0_2": 0 * SLOT,
-    "x1_0_scales": 5 * SLOT,
-    "woven1_2": 5 * SLOT,
-    "x1_1_words": 1 * SLOT,
-    "woven0_3": 1 * SLOT,
-    "hidden0_1": 2 * SLOT,
-    "woven1_3": 2 * SLOT,
-    "hidden0_0": 6 * SLOT,
-    "x0_3_words": 6 * SLOT,
-    "h0_0_words": 3 * SLOT,
-    "relu2_0": 3 * SLOT,
-    "relu3_1": 4 * SLOT,
-    "values1_2": 4 * SLOT,
-    "values3_1": 7 * SLOT,
-    "total0_0": 7 * SLOT - 1024,
-    "total0_320": 7 * SLOT + 256,
+    "woven0_2": 0,
+    "woven0_1": 0.25,
+    "woven0_3": 0.5,
+    "woven1_2": 2,
+    "woven1_1": 2.25,
+    "woven1_3": 2.5,
+    "woven1_0": 4,
+    "x0_2_words": 4,
+    "x0_3_words": 4.25,
+    "x1_1_words": 5,
+    "x1_2_words": 5,
+    "x1_1_scales": 6,
+    "x1_3_words": 6,
+    "x0_2_scales": 7,
+    "h1_0_words": 7,
+    "h1_1_words": 4,
+    "relu3_1": 8,
+    "values1_2": 8,
+    "values3_1": 14,
+    "total0_0": 13.5,
+    "total0_320": 14.125,
 }
 
 
@@ -63,7 +66,7 @@ def tile_moe_res_mlp_relu2_kernel(tc, xT, xr, w1_words, w1_scales, w2_words, w2_
 
         def new_tile(shape, dtype, name):
             if name in PLACE:
-                return shared.tile(shape, dtype, name=name, align_bytes=ALIGN, offset=PLACE[name])
+                return shared.tile(shape, dtype, name=name, align_bytes=ALIGN, offset=int(PLACE[name] * SLOT))
             return keep.tile(shape, dtype, name=name, align_bytes=ALIGN)
 
         def new_bank(shape, name, bank_no):
@@ -81,14 +84,10 @@ def tile_moe_res_mlp_relu2_kernel(tc, xT, xr, w1_words, w1_scales, w2_words, w2_
         for n in range(NT):
             nc.vector.memset(windows[n][:], 0.0)
 
-        def w1_plane(e, s, g):
-            s0 = max(c[1] for c in SCALE_GROUPS if c[0] == e and c[1] <= s)
-            return w1s[e, s0][:, s - s0, g * PASS : (g + 1) * PASS]
-
         rows = {}
 
         def load_rows(s, j0, j1):
-            t = keep.tile([P, j1 - j0, T], F32, name=f"rows{s}_{j0}")
+            t = new_tile([P, j1 - j0, T], F32, f"rows{s}_{j0}")
             nc.sync.dma_start(out=t[:], in_=xT[s * PASS : (s + 1) * PASS, :].rearrange("(q j) w -> q j w", j=4)[:, j0:j1, :])
             for j in range(j0, j1):
                 rows[s, j] = t[:, j - j0, :]
@@ -97,7 +96,7 @@ def tile_moe_res_mlp_relu2_kernel(tc, xT, xr, w1_words, w1_scales, w2_words, w2_
             for r in range(4):
                 nc.sync.dma_start(out=plane[r:P:32, :, :].bitcast(I32), in_=src[r])
 
-        w1s_rows = w1_scales.bitcast(I32).rearrange("e s (a r) i -> r a (e s) i", r=4)
+        w1s_rows = w1_scales.bitcast(I32).rearrange("e s (a r) i -> e r a s i", r=4)
         w2s_rows = w2_scales.bitcast(I32).rearrange("e s (a r) i -> r a (e s) i", r=4)
         w1_rows = w1_words.bitcast(I32).rearrange("e s p w -> e p s w")
         w2_rows = w2_words.bitcast(I32).rearrange("e s p w -> e p s w")
@@ -112,12 +111,18 @@ def tile_moe_res_mlp_relu2_kernel(tc, xT, xr, w1_words, w1_scales, w2_words, w2_
 
         def load_w1_scales(group):
             e, s0, s1 = SCALE_GROUPS[group]
-            load_scales(w1s[e, s0], w1s_rows[:, :, e * KP + s0 : e * KP + s1, :])
+            load_scales(w1s[e, s0], w1s_rows[e][:, :, s0:s1, :])
+
+        def w1_plane(e, s, g):
+            s0 = max(c[1] for c in SCALE_GROUPS if c[0] == e and c[1] <= s)
+            return w1s[e, s0][:, s - s0, g * PASS : (g + 1) * PASS]
 
         w2w = [new_tile([P, HP, 2 * N], U8, f"w2w{e}") for e in range(E)]
         gates = keep.tile([P, S], F32, name="gates")
-        gate_col = keep.tile([P, S // P], F32, name="gate_col")
         residual = [new_tile([P, T], F32, f"residual{n}") for n in range(NT)]
+
+        def load_w2(e):
+            nc.sync.dma_start(out=w2w[e][:].bitcast(I32), in_=w2_rows[e])
 
         load_rows(0, 0, 1)
         nc.sync.dma_start(offsets[:], offs)
@@ -133,42 +138,45 @@ def tile_moe_res_mlp_relu2_kernel(tc, xT, xr, w1_words, w1_scales, w2_words, w2_
         load_w1(1, 0, 2, 0, 1)
         load_w1_scales(2)
         load_w1(1, 0, 1, 1, 2)
-        nc.sync.dma_start(out=w2w[0][:].bitcast(I32), in_=w2_rows[0])
+        load_w2(0)
         nc.sync.dma_start(out=gates[:], in_=gate[0:P, :])
         load_scales(w2s, w2s_rows)
         load_w1(1, 1, 2, 1, 2)
-        nc.sync.dma_start(out=w2w[1][:].bitcast(I32), in_=w2_rows[1])
+        load_w2(1)
         for n in range(NT):
             nc.sync.dma_start(out=residual[n][:], in_=xr[n * P : (n + 1) * P, :])
 
         def slots(st0, st1):
             return offsets[:, st0 * P // PER_COLUMN : st1 * P // PER_COLUMN]
 
-        picked = {(s, st): new_tile([P, 4, n * P], F32, f"picked{s}_{st}") for s in range(KP) for st, n in GROUPS[s]}
-        woven = {}
-
-        def pick(on_scalar, s, j, a, b):
-            st0 = max(c for c, n in GROUPS[s] if c * P <= a)
-            src = rows[s, j].indirect(offsets[:, a // PER_COLUMN : b // PER_COLUMN])
-            dst = picked[s, st0][:, j, a - st0 * P : b - st0 * P]
+        def move(on_scalar, dst, src):
             if on_scalar:
                 nc.scalar.activation(dst, src, ACT.Copy)
             else:
                 nc.vector.tensor_copy(out=dst, in_=src)
 
-        def weave(on_scalar, s, st):
-            st0 = max(a for a, n in GROUPS[s] if a <= st)
-            woven[s, st] = new_tile([P, P, 4], BF16, f"woven{s}_{st}")
-            src = picked[s, st0][:, :, (st - st0) * P : (st - st0 + 1) * P].rearrange("p j c -> p c j")
-            if on_scalar:
-                nc.scalar.activation(woven[s, st][:], src, ACT.Copy)
-            else:
-                nc.vector.tensor_copy(out=woven[s, st][:], in_=src)
+        picked = {}
+        woven = {}
 
-        def pick_woven(s, j, st):
-            if j == 0:
+        def pick(on_scalar, s, j, st0, st1):
+            for group in GROUPS[s]:
+                if group[0] <= st0 < group[1]:
+                    if (s, group[0]) not in picked:
+                        planes = new_tile([P, 4, (group[1] - group[0]) * P], F32, f"picked{s}_{group[0]}")
+                        for st in range(*group):
+                            picked[s, st] = planes[:, :, (st - group[0]) * P : (st - group[0] + 1) * P]
+                        picked[s, group] = planes
+                    dst = picked[s, group][:, j, (st0 - group[0]) * P : (st1 - group[0]) * P]
+                    move(on_scalar, dst, rows[s, j].indirect(slots(st0, st1)))
+
+        def weave(on_scalar, s, st):
+            woven[s, st] = new_tile([P, P, 4], BF16, f"woven{s}_{st}")
+            move(on_scalar, woven[s, st][:], picked[s, st].rearrange("p j c -> p c j"))
+
+        def pick_woven(on_scalar, s, j, st):
+            if (s, st) not in woven:
                 woven[s, st] = new_tile([P, P, 4], BF16, f"woven{s}_{st}")
-            nc.vector.tensor_copy(out=woven[s, st][:, :, j], in_=rows[s, j].indirect(slots(st, st + 1)))
+            move(on_scalar, woven[s, st][:, :, j], rows[s, j].indirect(slots(st, st + 1)))
 
         x_codes = {}
 
@@ -183,13 +191,13 @@ def tile_moe_res_mlp_relu2_kernel(tc, xT, xr, w1_words, w1_scales, w2_words, w2_
 
         sums = {}
 
-        def first_pass(st, s, g, bank_no=None, part=0, parts=1):
+        def first_pass(st, g, s, bank_no=None, part=0, parts=1):
             w = PASS // parts
-            if s == 0:
-                sums[st, g, part] = new_bank([P, w], f"sums{st}{g}{part}", bank_no)
+            if bank_no is not None:
+                sums[st, g, part] = new_bank([P, w], f"sums{st}{g}{part}", bank_no)[:]
             e = st * P // C
             nc.tensor.matmul_mx(
-                out=sums[st, g, part][:],
+                out=sums[st, g, part],
                 lhsT=x_codes[s, st][0],
                 lhsT_scale=x_codes[s, st][1],
                 rhs=w1w[e, s, g][:, 2 * w * part : 2 * w * (part + 1)].bitcast(E2M1),
@@ -198,23 +206,32 @@ def tile_moe_res_mlp_relu2_kernel(tc, xT, xr, w1_words, w1_scales, w2_words, w2_
                 stop=(s == KP - 1),
             )
 
+        def two_banks(name):
+            return psum.tile([P, HP, PASS], F32, name=name, tag="two_banks")
+
+        def first_product(st, g, bank_no):
+            first_pass(st, g, 0, bank_no)
+            first_pass(st, g, 1)
+
         relus = {}
 
-        def relu(on_scalar, st, g, part=0, parts=1):
-            if (st, g) not in relus:
-                relus[st, g] = new_tile([P, 4, P], F32, f"relu{st}_{g}")
-            m = P // parts
-            dst = relus[st, g][:, :, m * part : m * (part + 1)]
-            src = sums[st, g, part][:].rearrange("p (m t) -> p t m", t=4)
+        def leave_bank(on_scalar, dst, src):
             if on_scalar:
                 nc.scalar.activation(dst, src, ACT.Relu)
             else:
                 nc.vector.tensor_scalar_max(dst, src, 0.0)
 
+        def relu(on_scalar, st, g, part=0, parts=1):
+            if (st, g) not in relus:
+                relus[st, g] = new_tile([P, 4, P], F32, f"relu{st}_{g}")
+            m = P // parts
+            leave_bank(on_scalar, relus[st, g][:, :, m * part : m * (part + 1)], sums[st, g, part].rearrange("p (m t) -> p t m", t=4))
+
         turned = {}
 
-        def turn(st, g, bank_no):
-            turned[st, g] = new_bank([P, 4, P], f"turned{st}{g}", bank_no)
+        def turn(st, g, bank_no=None):
+            if bank_no is not None:
+                turned[st, g] = new_bank([P, 4, P], f"turned{st}{g}", bank_no)[:]
             for t in range(4):
                 nc.tensor.transpose(turned[st, g][:, t, :], relus[st, g][:, t, :], ident[:])
 
@@ -222,7 +239,11 @@ def tile_moe_res_mlp_relu2_kernel(tc, xT, xr, w1_words, w1_scales, w2_words, w2_
 
         def square(st, g):
             hidden[st, g] = new_tile([P, P, 4], BF16, f"hidden{st}_{g}")
-            nc.scalar.activation(hidden[st, g][:], turned[st, g][:].rearrange("p t c -> p c t"), ACT.Square)
+            nc.scalar.activation(hidden[st, g][:], turned[st, g].rearrange("p t c -> p c t"), ACT.Square)
+
+        def weave_on_gpsimd(s, st):
+            woven[s, st] = new_tile([P, P, 4], BF16, f"woven{s}_{st}")
+            nc.gpsimd.tensor_scalar(woven[s, st][:], picked[s, st].rearrange("p j c -> p c j"), 1.0, 0.0, ALU.mult, ALU.add)
 
         h_codes = {}
 
@@ -231,77 +252,52 @@ def tile_moe_res_mlp_relu2_kernel(tc, xT, xr, w1_words, w1_scales, w2_words, w2_
 
         y_sums = {}
 
-        def second_pass(st, blocks, g, bank_no=None):
+        def second_pass(st, n, g, bank_no=None):
             e = st * P // C
             if bank_no is not None:
-                bank = new_bank([P, len(blocks), P], f"y{st}_{blocks[0]}", bank_no)
-                for a, n in enumerate(blocks):
-                    y_sums[st, n] = bank[:, a, :]
-            for n in blocks:
-                for gg in g:
-                    weights = (w2w[e][:, gg, 2 * P * n : 2 * P * (n + 1)].bitcast(E2M1), w2s[:, e * HP + gg, P * n : P * (n + 1)])
-                    left, right = (h_codes[st, gg], weights) if (st, n) in BY_SLOT else (weights, h_codes[st, gg])
-                    nc.tensor.matmul_mx(
-                        out=y_sums[st, n],
-                        lhsT=left[0],
-                        lhsT_scale=left[1],
-                        rhs=right[0],
-                        rhs_scale=right[1],
-                        start=(gg == 0),
-                        stop=(gg == HP - 1),
-                    )
+                y_sums[st, n] = new_bank([P, P], f"y{st}_{n}", bank_no)[:]
+            nc.tensor.matmul_mx(
+                out=y_sums[st, n],
+                lhsT=w2w[e][:, g, 2 * P * n : 2 * P * (n + 1)].bitcast(E2M1),
+                lhsT_scale=w2s[:, e * HP + g, P * n : P * (n + 1)],
+                rhs=h_codes[st, g][0],
+                rhs_scale=h_codes[st, g][1],
+                start=(g == 0),
+                stop=(g == HP - 1),
+            )
 
-        def second_product(st, blocks, bank_no):
-            second_pass(st, blocks, (0, 1), bank_no)
+        def second_product(st, n, bank_no=None):
+            second_pass(st, n, 0, bank_no)
+            second_pass(st, n, 1)
 
-        lists = {}
+        def second_product_beside(st, n, bank_no, key):
+            bank = new_bank([P, 3, P], f"y{st}_{n}", bank_no)
+            y_sums[st, n] = bank[:, 0, :]
+            turned[key] = bank[:, 1:, :]
+            second_pass(st, n, 0)
+            second_pass(st, n, 1)
 
-        def list_of(st, n):
-            st0, st1 = [c for c in LISTS[n] if c[0] <= st < c[1]][0]
-            if st == st0:
-                lists[st0, n] = new_tile([P, st1 - st0, P], F32, f"values{st0}_{n}")
-            return lists[st0, n][:, st - st0, :]
+        def second_products(st, blocks, bank_no):
+            bank = new_bank([P, len(blocks), P], f"y{st}_{blocks[0]}", bank_no)
+            for a, n in enumerate(blocks):
+                y_sums[st, n] = bank[:, a, :]
+                second_product(st, n)
+
+        values = {}
 
         def empty(st, n):
-            nc.scalar.activation(list_of(st, n), y_sums[st, n], ACT.Copy)
+            values[st, n] = new_tile([P, P], F32, f"values{st}_{n}")[:]
+            nc.scalar.activation(values[st, n], y_sums[st, n], ACT.Copy)
 
-        def scatter_times_gate(st0, n):
-            st1 = dict(LISTS[n])[st0]
-            src = lists[st0, n][:].rearrange("p a c -> p (a c)")
-            nc.vector.tensor_tensor(windows[n][:].indirect(slots(st0, st1)), src, gates[:, st0 * P : st1 * P], ALU.mult)
-
-        gated = {}
-        upright = {}
-
-        def gate_by_slot(st, n):
-            gated[st, n] = new_tile([P, P], F32, f"gated{st}_{n}")
-            nc.scalar.activation(gated[st, n][:], y_sums[st, n], ACT.Copy, scale=gate_col[:, st : st + 1])
-
-        def turn_gated(st, n, bank_no):
-            upright[st, n] = new_bank([P, P], f"upright{st}_{n}", bank_no)
-            nc.tensor.transpose(upright[st, n][:], gated[st, n][:], ident[:])
-
-        def empty_gated(st, n):
-            nc.scalar.activation(list_of(st, n), upright[st, n][:], ACT.Copy)
+        def scatter_times_gate(st, n):
+            nc.vector.tensor_tensor(windows[n][:].indirect(slots(st, st + 1)), values[st, n], gates[:, st * P : (st + 1) * P], ALU.mult)
 
         def apply_gate(st, n):
-            nc.vector.tensor_tensor(list_of(st, n), y_sums[st, n], gates[:, st * P : (st + 1) * P], ALU.mult)
+            values[st, n] = new_tile([P, P], F32, f"values{st}_{n}")[:]
+            nc.vector.tensor_tensor(values[st, n], y_sums[st, n], gates[:, st * P : (st + 1) * P], ALU.mult)
 
-        def scatter(on_scalar, st0, n):
-            dst = windows[n][:].indirect(slots(st0, dict(LISTS[n])[st0]))
-            src = lists[st0, n][:].rearrange("p a c -> p (a c)")
-            if on_scalar:
-                nc.scalar.activation(dst, src, ACT.Copy)
-            else:
-                nc.vector.tensor_copy(out=dst, in_=src)
-
-        def scatter_part(on_scalar, st0, n, a, b):
-            dst = windows[n][:].indirect(offsets[:, (st0 * P + a) // PER_COLUMN : (st0 * P + b) // PER_COLUMN])
-            src = lists[st0, n][:].rearrange("p a c -> p (a c)")[:, a:b]
-            if on_scalar:
-                nc.scalar.activation(dst, src, ACT.Copy)
-            else:
-                nc.vector.tensor_copy(out=dst, in_=src)
+        def scatter(on_scalar, st, n):
+            move(on_scalar, windows[n][:].indirect(slots(st, st + 1)), values[st, n])
 
         def add_and_store(engine, n, c0, c1):
             total = new_tile([P, c1 - c0], F32, f"total{n}_{c0}")
@@ -309,104 +305,104 @@ def tile_moe_res_mlp_relu2_kernel(tc, xT, xr, w1_words, w1_scales, w2_words, w2_
             nc.sync.dma_start(out=out[n * P : (n + 1) * P, c0:c1], in_=total[:])
 
         VEC, SCA = False, True
-        pick(SCA, 0, 0, 256, 512)
-        pick(VEC, 0, 0, 0, 256)
-        pick(SCA, 0, 1, 256, 512)
-        pick(VEC, 0, 1, 0, 256)
-        pick(SCA, 0, 2, 256, 512)
-        pick(VEC, 0, 2, 0, 256)
-        pick(SCA, 0, 3, 256, 512)
-        pick(VEC, 0, 3, 0, 256)
-        pick(SCA, 1, 0, 128, 256)
+        pick(SCA, 0, 0, 2, 4)
+        pick(VEC, 0, 0, 0, 2)
+        pick(SCA, 0, 1, 2, 4)
+        pick(VEC, 0, 1, 0, 2)
+        pick(SCA, 0, 2, 2, 4)
+        pick(VEC, 0, 2, 0, 2)
+        pick(SCA, 0, 3, 2, 4)
+        pick(VEC, 0, 3, 0, 2)
+        pick(SCA, 1, 0, 1, 2)
         weave(VEC, 0, 0)
-        pick(SCA, 1, 0, 256, 512)
+        pick(SCA, 1, 0, 2, 4)
         weave(VEC, 0, 1)
-        pick(SCA, 1, 1, 128, 256)
+        pick(SCA, 1, 1, 1, 2)
         quantize_slots(0, 0)
         first_pass(0, 0, 0, 0, 0, 2)
-        pick(SCA, 1, 1, 384, 512)
-        pick_woven(1, 0, 0)
+        pick(SCA, 1, 1, 3, 4)
+        pick_woven(VEC, 1, 0, 0)
         first_pass(0, 0, 0, 7, 1, 2)
-        pick(SCA, 1, 2, 128, 256)
+        pick(SCA, 1, 2, 1, 2)
         quantize_slots(0, 1)
         first_pass(1, 0, 0, 2)
-        pick(SCA, 1, 2, 384, 512)
-        pick_woven(1, 1, 0)
-        first_pass(0, 0, 1, 1)
-        pick(SCA, 1, 3, 128, 256)
-        pick(VEC, 1, 1, 256, 384)
-        first_pass(1, 0, 1, 3)
-        pick(SCA, 1, 3, 384, 512)
-        pick_woven(1, 2, 0)
-        pick(SCA, 1, 3, 256, 384)
-        pick(VEC, 1, 2, 256, 384)
-        pick_woven(1, 3, 0)
+        weave_on_gpsimd(0, 2)
+        weave_on_gpsimd(0, 3)
+        pick(SCA, 1, 2, 3, 4)
+        pick_woven(VEC, 1, 1, 0)
+        first_pass(0, 1, 0, 1)
+        pick(SCA, 1, 3, 1, 2)
+        pick(VEC, 1, 1, 2, 3)
+        first_pass(1, 1, 0, 3)
+        pick(SCA, 1, 3, 3, 4)
+        pick_woven(VEC, 1, 2, 0)
+        pick(SCA, 1, 3, 2, 3)
+        pick(VEC, 1, 2, 2, 3)
+        pick_woven(VEC, 1, 3, 0)
         quantize_slots(1, 0)
-        first_pass(0, 1, 0, None, 0, 2)
-        weave(VEC, 1, 1)
-        first_pass(0, 1, 0, None, 1, 2)
-        relu(SCA, 0, 0, 1, 2)
-        quantize_slots(1, 1)
+        first_pass(0, 0, 1, None, 0, 2)
+        first_pass(0, 0, 1, None, 1, 2)
         first_pass(0, 1, 1)
-        relu(SCA, 0, 1)
-        relu(VEC, 0, 0, 0, 2)
-        first_pass(1, 1, 0)
-        relu(SCA, 1, 0)
-        weave(VEC, 0, 2)
-        first_pass(1, 1, 1)
-        weave(VEC, 1, 2)
-        turn(0, 0, 4)
-        square(0, 0)
-        relu(VEC, 1, 1)
-        turn(0, 1, 5)
-        square(0, 1)
+        weave(VEC, 1, 1)
         quantize_slots(0, 2)
+        quantize_slots(0, 3)
+        quantize_slots(1, 1)
+        first_pass(1, 0, 1)
+        first_pass(1, 1, 1)
+        weave_on_gpsimd(1, 2)
+        weave_on_gpsimd(1, 3)
+        relu(SCA, 0, 0, 1, 2)
+        relu(VEC, 0, 0, 0, 2)
+        relu(SCA, 0, 1)
+        relu(SCA, 1, 0)
+        relu(VEC, 1, 1)
+        turn(0, 0, 4)
+        turn(0, 1, 5)
         turn(1, 0, 6)
-        square(1, 0)
-        quantize_slots(1, 2)
         turn(1, 1, 7)
+        square(0, 0)
+        square(0, 1)
+        quantize_slots(1, 2)
+        quantize_slots(1, 3)
+        square(1, 0)
         square(1, 1)
-        weave(VEC, 0, 3)
         first_pass(2, 0, 0, 0)
         quantize_hidden(0, 0)
-        first_pass(2, 1, 0)
-        quantize_slots(0, 3)
-        first_pass(2, 0, 1, 1)
+        first_pass(2, 0, 1)
+        first_pass(2, 1, 0, 1)
         quantize_hidden(0, 1)
-        second_product(0, (0,), 2)
+        second_product(0, 0, 2)
         empty(0, 0)
-        weave(VEC, 1, 3)
-        second_product(0, (1,), 3)
+        relu(VEC, 2, 0)
+        second_product(0, 1, 3)
         empty(0, 1)
         quantize_hidden(1, 0)
-        second_product(0, (2,), 4)
-        relu(SCA, 2, 0)
-        quantize_slots(1, 3)
+        second_product(0, 2, 4)
         first_pass(2, 1, 1)
         empty(0, 2)
         quantize_hidden(1, 1)
         first_pass(3, 0, 0, 2)
         relu(SCA, 2, 1)
         scatter_times_gate(0, 0)
-        first_pass(3, 1, 0)
+        first_pass(3, 0, 1)
         relu(SCA, 3, 0)
         scatter_times_gate(0, 1)
         turn(2, 0, 3)
         square(2, 0)
         scatter_times_gate(0, 2)
-        second_product(1, (0,), 0)
+        second_product(1, 0, 1)
         empty(1, 0)
         scatter_times_gate(1, 0)
-        first_pass(3, 0, 1, 4)
+        first_pass(3, 1, 0, 4)
         quantize_hidden(2, 0)
         first_pass(3, 1, 1)
         relu(SCA, 3, 1)
         turn(2, 1, 5)
         square(2, 1)
         quantize_hidden(2, 1)
-        second_product(1, (1,), 2)
+        second_product(1, 1, 2)
         empty(1, 1)
-        second_product(1, (2,), 3)
+        second_product(1, 2, 3)
         apply_gate(1, 2)
         turn(3, 0, 6)
         square(3, 0)
@@ -414,24 +410,24 @@ def tile_moe_res_mlp_relu2_kernel(tc, xT, xr, w1_words, w1_scales, w2_words, w2_
         turn(3, 1, 7)
         square(3, 1)
         quantize_hidden(3, 0)
-        second_product(2, (0,), 2)
+        second_product(2, 0, 2)
         scatter(SCA, 1, 2)
         apply_gate(2, 0)
-        second_product(2, (2, 1), 6)
+        second_products(2, (2, 1), 6)
         scatter(SCA, 2, 0)
         quantize_hidden(3, 1)
-        second_pass(3, (0,), (0,), 0)
+        second_pass(3, 0, 0, 0)
         apply_gate(2, 2)
-        second_pass(3, (1,), (0,), 1)
+        second_pass(3, 1, 0, 1)
         scatter(SCA, 2, 2)
         apply_gate(2, 1)
-        second_pass(3, (2,), (0,), 5)
+        second_pass(3, 2, 0, 5)
         scatter(VEC, 2, 1)
-        second_pass(3, (1,), (1,))
+        second_pass(3, 1, 1)
         apply_gate(3, 1)
-        second_pass(3, (0,), (1,))
+        second_pass(3, 0, 1)
         apply_gate(3, 0)
-        second_pass(3, (2,), (1,))
+        second_pass(3, 2, 1)
         scatter(SCA, 3, 0)
         apply_gate(3, 2)
         scatter(SCA, 3, 2)

@@ -41,8 +41,8 @@ PLACE = {
     "woven1_3": 2.5,
     "woven1_0": 4,
     "x0_2_words": 4,
-    "x0_3_words": 4.25,
-    "x1_1_words": 5,
+    "x0_3_words": 5.25,
+    "x1_1_words": 5.125,
     "x1_2_words": 5,
     "x1_1_scales": 6,
     "x1_3_words": 6,
@@ -312,7 +312,8 @@ def tile_moe_res_mlp_relu2_kernel(tc, xT, xr, w1_words, w1_scales, w2_words, w2_
         pick(SCA, 0, 2, 2, 4)
         pick(VEC, 0, 2, 0, 2)
         pick(SCA, 0, 3, 2, 4)
-        pick(VEC, 0, 3, 0, 2)
+        pick(VEC, 0, 3, 0, 1)
+        pick(VEC, 0, 3, 1, 2)
         pick(SCA, 1, 0, 1, 2)
         weave(VEC, 0, 0)
         pick(SCA, 1, 0, 2, 4)
@@ -345,7 +346,6 @@ def tile_moe_res_mlp_relu2_kernel(tc, xT, xr, w1_words, w1_scales, w2_words, w2_
         first_pass(0, 1, 1)
         weave(VEC, 1, 1)
         quantize_slots(0, 2)
-        quantize_slots(0, 3)
         quantize_slots(1, 1)
         first_pass(1, 0, 1)
         first_pass(1, 1, 1)
@@ -362,6 +362,7 @@ def tile_moe_res_mlp_relu2_kernel(tc, xT, xr, w1_words, w1_scales, w2_words, w2_
         turn(1, 1, 7)
         square(0, 0)
         square(0, 1)
+        quantize_slots(0, 3)
         quantize_slots(1, 2)
         quantize_slots(1, 3)
         square(1, 0)
@@ -413,14 +414,14 @@ def tile_moe_res_mlp_relu2_kernel(tc, xT, xr, w1_words, w1_scales, w2_words, w2_
         second_product(2, 0, 2)
         scatter(SCA, 1, 2)
         apply_gate(2, 0)
-        second_products(2, (2, 1), 6)
+        second_products(2, (1, 2), 6)
         scatter(SCA, 2, 0)
+        apply_gate(2, 1)
         quantize_hidden(3, 1)
         second_pass(3, 0, 0, 0)
         apply_gate(2, 2)
         second_pass(3, 1, 0, 1)
         scatter(SCA, 2, 2)
-        apply_gate(2, 1)
         second_pass(3, 2, 0, 5)
         scatter(VEC, 2, 1)
         second_pass(3, 1, 1)
@@ -436,5 +437,5 @@ def tile_moe_res_mlp_relu2_kernel(tc, xT, xr, w1_words, w1_scales, w2_words, w2_
         add_and_store(nc.vector, 1, 320, T)
         add_and_store(nc.vector, 0, 0, 320)
         add_and_store(nc.vector, 0, 320, T)
-        add_and_store(nc.vector, 2, 0, 320)
-        add_and_store(nc.vector, 2, 320, T)
+        add_and_store(nc.vector, 2, 0, 384)
+        add_and_store(nc.vector, 2, 384, T)

@@ -171,7 +171,8 @@ def tile_moe_res_mlp_relu2_kernel(tc, xT, xr, w1_words, w1_scales, w2_words, w2_
 
         def weave(on_scalar, s, st):
             woven[s, st] = new_tile([P, P, 4], BF16, f"woven{s}_{st}")
-            move(on_scalar, woven[s, st][:], picked[s, st].rearrange("p j c -> p c j"))
+            dst = woven[s, st][:].rearrange("p (c i) j -> p c j i", i=4)
+            move(on_scalar, dst, picked[s, st].rearrange("p j (c i) -> p c j i", i=4))
 
         def pick_woven(on_scalar, s, j, st):
             if (s, st) not in woven:

@@ -130,9 +130,10 @@ def tile_moe_res_mlp_relu2_kernel(tc, xT, xr, w1_words, w1_scales, w2_words, w2_
             load_rows(0, j, j + 1)
         load_rows(1, 0, 1)
         load_w1_scales(0)
-        load_w1(0, 0, 1, 0, 2)
+        load_w1(0, 0, 1, 0, 1)
         for j in range(1, 4):
             load_rows(1, j, j + 1)
+        load_w1(0, 0, 1, 1, 2)
         load_w1(0, 1, 2, 0, 2)
         load_w1_scales(1)
         load_w1(1, 0, 2, 0, 1)
@@ -332,9 +333,9 @@ def tile_moe_res_mlp_relu2_kernel(tc, xT, xr, w1_words, w1_scales, w2_words, w2_
         weave_on_gpsimd(0, 3)
         pick(SCA, 1, 2, 3, 4)
         pick_woven(VEC, 1, 1, 0)
-        first_pass(0, 1, 0, 1)
         pick(SCA, 1, 3, 1, 2)
         pick(VEC, 1, 1, 2, 3)
+        first_pass(0, 1, 0, 1)
         first_pass(1, 1, 0, 3)
         pick(SCA, 1, 3, 3, 4)
         pick_woven(VEC, 1, 2, 0)

@@ -320,27 +320,24 @@ def tile_moe_res_mlp_relu2_kernel(tc, xT, xr, w1_words, w1_scales, w2_words, w2_
         weave(VEC, 0, 0)
         pick(SCA, 1, 0, 2, 4)
         weave(VEC, 0, 1)
-        pick(SCA, 1, 1, 1, 2)
+        pick(SCA, 1, 1, 2, 4)
         quantize_slots(0, 0)
         first_pass(0, 0, 0, 0, 0, 2)
-        pick(SCA, 1, 1, 3, 4)
         pick_woven(VEC, 1, 0, 0)
         first_pass(0, 0, 0, 7, 1, 2)
-        pick(SCA, 1, 2, 1, 2)
+        pick(SCA, 1, 2, 2, 4)
         quantize_slots(0, 1)
         first_pass(1, 0, 0, 2)
         weave_on_gpsimd(0, 2)
         weave_on_gpsimd(0, 3)
-        pick(SCA, 1, 2, 3, 4)
         pick_woven(VEC, 1, 1, 0)
         pick(SCA, 1, 3, 1, 2)
-        pick(VEC, 1, 1, 2, 3)
+        pick(VEC, 1, 1, 1, 2)
         first_pass(0, 1, 0, 1)
         first_pass(1, 1, 0, 3)
-        pick(SCA, 1, 3, 3, 4)
+        pick(SCA, 1, 3, 2, 4)
         pick_woven(VEC, 1, 2, 0)
-        pick(SCA, 1, 3, 2, 3)
-        pick(VEC, 1, 2, 2, 3)
+        pick(VEC, 1, 2, 1, 2)
         pick_woven(VEC, 1, 3, 0)
         quantize_slots(1, 0)
         first_pass(0, 0, 1, None, 0, 2)

@@ -31,7 +31,7 @@ ALIGN = 64
 SLOT = 2048
 
 SCALE_GROUPS = ((0, 0, 1), (0, 1, 2), (1, 0, 2))
-GROUPS = (((0, 2), (2, 4)), ((1, 2), (2, 4)))
+GROUPS = (((0, 4),), ((1, 2), (2, 4)))
 PLACE = {
     "woven0_2": 0,
     "woven0_1": 0.25,
@@ -140,10 +140,11 @@ def tile_moe_res_mlp_relu2_kernel(tc, xT, xr, w1_words, w1_scales, w2_words, w2_
         load_w1_scales(2)
         load_w1(1, 0, 1, 1, 2)
         load_w2(0)
-        nc.sync.dma_start(out=gates[:], in_=gate[0:P, :])
+        nc.sync.dma_start(out=gates[:, :C], in_=gate[0:P, :C])
         load_scales(w2s, w2s_rows)
         load_w1(1, 1, 2, 1, 2)
         load_w2(1)
+        nc.sync.dma_start(out=gates[:, C:], in_=gate[0:P, C:])
         for n in range(NT):
             nc.sync.dma_start(out=residual[n][:], in_=xr[n * P : (n + 1) * P, :])
 
@@ -247,6 +248,14 @@ def tile_moe_res_mlp_relu2_kernel(tc, xT, xr, w1_words, w1_scales, w2_words, w2_
             woven[s, st] = new_tile([P, P, 4], BF16, f"woven{s}_{st}")
             nc.gpsimd.tensor_scalar(woven[s, st][:], picked[s, st].rearrange("p j c -> p c j"), 1.0, 0.0, ALU.mult, ALU.add)
 
+        def pick_slots(on_scalar, j, c0, c1):
+            if (0, 0) not in picked:
+                planes = new_tile([P, 4, S], F32, "picked0_0")
+                for st in range(ST):
+                    picked[0, st] = planes[:, :, st * P : (st + 1) * P]
+                picked[0, (0, ST)] = planes
+            move(on_scalar, picked[0, (0, ST)][:, j, c0:c1], rows[0, j].indirect(offsets[:, c0 // PER_COLUMN : c1 // PER_COLUMN]))
+
         h_codes = {}
 
         def quantize_hidden(st, g):
@@ -307,12 +316,9 @@ def tile_moe_res_mlp_relu2_kernel(tc, xT, xr, w1_words, w1_scales, w2_words, w2_
             nc.sync.dma_start(out=out[n * P : (n + 1) * P, c0:c1], in_=total[:])
 
         VEC, SCA = False, True
-        pick(SCA, 0, 0, 2, 4)
-        pick(VEC, 0, 0, 0, 2)
-        pick(SCA, 0, 1, 2, 4)
-        pick(VEC, 0, 1, 0, 2)
-        pick(SCA, 0, 2, 2, 4)
-        pick(VEC, 0, 2, 0, 2)
+        for j in range(3):
+            pick_slots(SCA, j, 288, S)
+            pick_slots(VEC, j, 0, 288)
         pick(SCA, 0, 3, 2, 4)
         pick(VEC, 0, 3, 0, 1)
         pick(VEC, 0, 3, 1, 2)

@@ -358,7 +358,7 @@ def tile_moe_res_mlp_relu2_kernel(tc, xT, xr, w1_words, w1_scales, w2_words, w2_
         weave_on_gpsimd(1, 3)
         relu(SCA, 0, 0, 1, 2)
         relu(VEC, 0, 0, 0, 2)
-        relu(SCA, 0, 1)
+        relu(VEC, 0, 1)
         relu(SCA, 1, 0)
         relu(VEC, 1, 1)
         turn(0, 0, 4)

@@ -31,7 +31,7 @@ ALIGN = 64
 SLOT = 2048
 
 SCALE_GROUPS = ((0, 0, 1), (0, 1, 2), (1, 0, 2))
-GROUPS = (((0, 4),), ((1, 2), (2, 4)))
+GROUPS = (((0, 4),), ((1, 4),))
 PLACE = {
     "woven0_2": 0,
     "woven0_1": 0.25,
@@ -256,6 +256,9 @@ def tile_moe_res_mlp_relu2_kernel(tc, xT, xr, w1_words, w1_scales, w2_words, w2_
                 picked[0, (0, ST)] = planes
             move(on_scalar, picked[0, (0, ST)][:, j, c0:c1], rows[0, j].indirect(offsets[:, c0 // PER_COLUMN : c1 // PER_COLUMN]))
 
+        def pick_rest(on_scalar, j, c0, c1):
+            move(on_scalar, picked[1, (1, ST)][:, j, c0 - P : c1 - P], rows[1, j].indirect(offsets[:, c0 // PER_COLUMN : c1 // PER_COLUMN]))
+
         h_codes = {}
 
         def quantize_hidden(st, g):
@@ -317,33 +320,32 @@ def tile_moe_res_mlp_relu2_kernel(tc, xT, xr, w1_words, w1_scales, w2_words, w2_
 
         VEC, SCA = False, True
         for j in range(3):
-            pick_slots(SCA, j, 288, S)
-            pick_slots(VEC, j, 0, 288)
+            pick_slots(SCA, j, 320, S)
+            pick_slots(VEC, j, 0, 320)
         pick(SCA, 0, 3, 2, 4)
         pick(VEC, 0, 3, 0, 1)
         pick(VEC, 0, 3, 1, 2)
-        pick(SCA, 1, 0, 1, 2)
+        pick(SCA, 1, 0, 1, 4)
         weave(VEC, 0, 0)
-        pick(SCA, 1, 0, 2, 4)
         weave(VEC, 0, 1)
-        pick(SCA, 1, 1, 2, 4)
+        pick_rest(SCA, 1, 224, S)
         quantize_slots(0, 0)
         first_pass(0, 0, 0, 0, 0, 2)
         pick_woven(VEC, 1, 0, 0)
         first_pass(0, 0, 0, 7, 1, 2)
-        pick(SCA, 1, 2, 2, 4)
+        pick_rest(SCA, 2, 224, S)
         quantize_slots(0, 1)
         first_pass(1, 0, 0, 2)
         weave_on_gpsimd(0, 2)
         weave_on_gpsimd(0, 3)
         pick_woven(VEC, 1, 1, 0)
         pick(SCA, 1, 3, 1, 2)
-        pick(VEC, 1, 1, 1, 2)
+        pick_rest(VEC, 1, P, 224)
         first_pass(0, 1, 0, 1)
         first_pass(1, 1, 0, 3)
         pick(SCA, 1, 3, 2, 4)
         pick_woven(VEC, 1, 2, 0)
-        pick(VEC, 1, 2, 1, 2)
+        pick_rest(VEC, 2, P, 224)
         pick_woven(VEC, 1, 3, 0)
         quantize_slots(1, 0)
         first_pass(0, 0, 1, None, 0, 2)
@@ -442,5 +444,6 @@ def tile_moe_res_mlp_relu2_kernel(tc, xT, xr, w1_words, w1_scales, w2_words, w2_
         add_and_store(nc.vector, 1, 320, T)
         add_and_store(nc.vector, 0, 0, 320)
         add_and_store(nc.vector, 0, 320, T)
-        add_and_store(nc.vector, 2, 0, 384)
-        add_and_store(nc.vector, 2, 384, T)
+        add_and_store(nc.vector, 2, 0, 256)
+        add_and_store(nc.vector, 2, 256, 512)
+        add_and_store(nc.vector, 2, 512, T)

@@ -328,24 +328,24 @@ def tile_moe_res_mlp_relu2_kernel(tc, xT, xr, w1_words, w1_scales, w2_words, w2_
         pick(SCA, 1, 0, 1, 4)
         weave(VEC, 0, 0)
         weave(VEC, 0, 1)
-        pick_rest(SCA, 1, 224, S)
+        pick_rest(SCA, 1, 256, S)
         quantize_slots(0, 0)
         first_pass(0, 0, 0, 0, 0, 2)
         pick_woven(VEC, 1, 0, 0)
         first_pass(0, 0, 0, 7, 1, 2)
-        pick_rest(SCA, 2, 224, S)
+        pick_rest(SCA, 2, 256, S)
         quantize_slots(0, 1)
         first_pass(1, 0, 0, 2)
         weave_on_gpsimd(0, 2)
         weave_on_gpsimd(0, 3)
         pick_woven(VEC, 1, 1, 0)
         pick(SCA, 1, 3, 1, 2)
-        pick_rest(VEC, 1, P, 224)
+        pick_rest(VEC, 1, P, 256)
         first_pass(0, 1, 0, 1)
         first_pass(1, 1, 0, 3)
         pick(SCA, 1, 3, 2, 4)
         pick_woven(VEC, 1, 2, 0)
-        pick_rest(VEC, 2, P, 224)
+        pick_rest(VEC, 2, P, 256)
         pick_woven(VEC, 1, 3, 0)
         quantize_slots(1, 0)
         first_pass(0, 0, 1, None, 0, 2)

from contextlib import ExitStack

import concourse.mybir as mybir
from concourse.masks import make_identity

K, T, E, C, H, N = 1024, 640, 2, 256, 1024, 384
S = E * C
FLOPS = 2 * S * (K * H + H * N)

F32 = mybir.dt.float32
BF16 = mybir.dt.bfloat16
I32 = mybir.dt.int32
U32 = mybir.dt.uint32
U16 = mybir.dt.uint16
U8 = mybir.dt.uint8
E4M3 = mybir.dt.float8_e4m3fn_x4
E2M1 = mybir.dt.float4_e2m1fn_x4
ACT = mybir.ActivationFunctionType
ALU = mybir.AluOpType

P = 128
PASS = 4 * P
KP = K // PASS
HP = H // PASS
NT = N // P
ST = S // P
PER_COLUMN = 16
HALF_BYTES = 2 * PASS
HALF_INTS = HALF_BYTES // 4
ALIGN = 64
SLOT = 2048

SCALE_GROUPS = ((0, 0, 1), (0, 1, 2), (1, 0, 2))
GROUPS = (((0, 4),), ((1, 4),))
PLACE = {
    "woven0_2": 0,
    "woven0_1": 0.25,
    "woven0_3": 0.5,
    "woven1_2": 2,
    "woven1_1": 2.25,
    "woven1_3": 2.5,
    "woven1_0": 4,
    "x0_2_words": 4,
    "x0_3_words": 5.25,
    "x1_1_words": 5.125,
    "x1_2_words": 5,
    "x1_1_scales": 6,
    "x1_3_words": 6,
    "x0_2_scales": 7,
    "h1_0_words": 7,
    "h1_1_words": 4,
    "relu3_1": 8,
    "values1_2": 8,
    "values3_1": 14,
    "total0_0": 13.5,
    "total0_320": 14.125,
}


def tile_moe_res_mlp_relu2_kernel(tc, xT, xr, w1_words, w1_scales, w2_words, w2_scales, gate, offs, out):
    nc = tc.nc
    with ExitStack() as ctx:
        keep = ctx.enter_context(tc.tile_pool(name="keep", bufs=1))
        shared = ctx.enter_context(tc.tile_pool(name="shared", bufs=1))
        psum = ctx.enter_context(tc.psum_pool(name="psum", bufs=1))

        def new_tile(shape, dtype, name):
            if name in PLACE:
                return shared.tile(shape, dtype, name=name, align_bytes=ALIGN, offset=int(PLACE[name] * SLOT))
            return keep.tile(shape, dtype, name=name, align_bytes=ALIGN)

        def new_bank(shape, name, bank_no):
            return psum.tile(shape, F32, name=name, tag=f"bank{bank_no}")

        offsets = keep.tile([P, S // PER_COLUMN], U16, name="offsets")

        w1s = {(e, s0): new_tile([P, s1 - s0, H], U8, f"w1s{e}_{s0}") for e, s0, s1 in SCALE_GROUPS}
        w2s = new_tile([P, E * HP, N], U8, "w2s")
        for plane in (*w1s.values(), w2s):
            nc.vector.memset(plane[:].rearrange("p g i -> p (g i)").bitcast(I32), 0)
        ident = keep.tile([P, P], F32, name="ident")
        make_identity(nc, ident[:])
        windows = [keep.tile([P, T], F32, name=f"window{n}") for n in range(NT)]
        for n in range(NT):
            nc.vector.memset(windows[n][:], 0.0)

        rows = {}

        def load_rows(s, j0, j1):
            t = new_tile([P, j1 - j0, T], F32, f"rows{s}_{j0}")
            nc.sync.dma_start(out=t[:], in_=xT[s * PASS : (s + 1) * PASS, :].rearrange("(q j) w -> q j w", j=4)[:, j0:j1, :])
            for j in range(j0, j1):
                rows[s, j] = t[:, j - j0, :]

        def load_scales(plane, src):
            for r in range(4):
                nc.sync.dma_start(out=plane[r:P:32, :, :].bitcast(I32), in_=src[r])

        w1s_rows = w1_scales.bitcast(I32).rearrange("e s (a r) i -> e r a s i", r=4)
        w2s_rows = w2_scales.bitcast(I32).rearrange("e s (a r) i -> r a (e s) i", r=4)
        w1_rows = w1_words.bitcast(I32).rearrange("e s p w -> e p s w")
        w2_rows = w2_words.bitcast(I32).rearrange("e s p w -> e p s w")
        w1w = {}

        def load_w1(e, s0, s1, g0, g1):
            t = new_tile([P, s1 - s0, (g1 - g0) * HALF_BYTES], U8, f"w1w{e}_{s0}_{g0}")
            nc.sync.dma_start(out=t[:].bitcast(I32), in_=w1_rows[e, :, s0:s1, g0 * HALF_INTS : g1 * HALF_INTS])
            for s in range(s0, s1):
                for g in range(g0, g1):
                    w1w[e, s, g] = t[:, s - s0, (g - g0) * HALF_BYTES : (g - g0 + 1) * HALF_BYTES]

        def load_w1_scales(group):
            e, s0, s1 = SCALE_GROUPS[group]
            load_scales(w1s[e, s0], w1s_rows[e][:, :, s0:s1, :])

        def w1_plane(e, s, g):
            s0 = max(c[1] for c in SCALE_GROUPS if c[0] == e and c[1] <= s)
            return w1s[e, s0][:, s - s0, g * PASS : (g + 1) * PASS]

        w2w = [new_tile([P, HP, 2 * N], U8, f"w2w{e}") for e in range(E)]
        gates = keep.tile([P, S], F32, name="gates")
        residual = [new_tile([P, T], F32, f"residual{n}") for n in range(NT)]

        def load_w2(e):
            nc.sync.dma_start(out=w2w[e][:].bitcast(I32), in_=w2_rows[e])

        load_rows(0, 0, 1)
        nc.sync.dma_start(offsets[:], offs)
        for j in range(1, 4):
            load_rows(0, j, j + 1)
        load_rows(1, 0, 1)
        load_w1_scales(0)
        load_w1(0, 0, 1, 0, 1)
        for j in range(1, 4):
            load_rows(1, j, j + 1)
        load_w1(0, 0, 1, 1, 2)
        load_w1(0, 1, 2, 0, 2)
        load_w1_scales(1)
        load_w1(1, 0, 2, 0, 1)
        load_w1_scales(2)
        load_w1(1, 0, 1, 1, 2)
        load_w2(0)
        nc.sync.dma_start(out=gates[:, :C], in_=gate[0:P, :C])
        load_scales(w2s, w2s_rows)
        load_w1(1, 1, 2, 1, 2)
        load_w2(1)
        nc.sync.dma_start(out=gates[:, C:], in_=gate[0:P, C:])
        for n in range(NT):
            nc.sync.dma_start(out=residual[n][:], in_=xr[n * P : (n + 1) * P, :])

        def slots(st0, st1):
            return offsets[:, st0 * P // PER_COLUMN : st1 * P // PER_COLUMN]

        def move(on_scalar, dst, src):
            if on_scalar:
                nc.scalar.activation(dst, src, ACT.Copy)
            else:
                nc.vector.tensor_copy(out=dst, in_=src)

        picked = {}
        woven = {}

        def pick(on_scalar, s, j, st0, st1):
            for group in GROUPS[s]:
                if group[0] <= st0 < group[1]:
                    if (s, group[0]) not in picked:
                        planes = new_tile([P, 4, (group[1] - group[0]) * P], F32, f"picked{s}_{group[0]}")
                        for st in range(*group):
                            picked[s, st] = planes[:, :, (st - group[0]) * P : (st - group[0] + 1) * P]
                        picked[s, group] = planes
                    dst = picked[s, group][:, j, (st0 - group[0]) * P : (st1 - group[0]) * P]
                    move(on_scalar, dst, rows[s, j].indirect(slots(st0, st1)))

        def weave(on_scalar, s, st):
            woven[s, st] = new_tile([P, P, 4], BF16, f"woven{s}_{st}")
            dst = woven[s, st][:].rearrange("p (c i) j -> p c j i", i=4)
            move(on_scalar, dst, picked[s, st].rearrange("p j (c i) -> p c j i", i=4))

        def pick_woven(on_scalar, s, j, st):
            if (s, st) not in woven:
                woven[s, st] = new_tile([P, P, 4], BF16, f"woven{s}_{st}")
            move(on_scalar, woven[s, st][:, :, j], rows[s, j].indirect(slots(st, st + 1)))

        x_codes = {}

        def quantize(src, name):
            words = new_tile([P, P], U32, f"{name}_words")
            scales = new_tile([P, P], U8, f"{name}_scales")
            nc.vector.quantize_mx(out=words[:].bitcast(E4M3), scales=scales[:], in_=src[:].rearrange("p c t -> p (c t)"))
            return words[:].bitcast(E4M3), scales[:]

        def quantize_slots(s, st):
            x_codes[s, st] = quantize(woven[s, st], f"x{s}_{st}")

        sums = {}

        def first_pass(st, g, s, bank_no=None, part=0, parts=1):
            w = PASS // parts
            if bank_no is not None:
                sums[st, g, part] = new_bank([P, w], f"sums{st}{g}{part}", bank_no)[:]
            e = st * P // C
            nc.tensor.matmul_mx(
                out=sums[st, g, part],
                lhsT=x_codes[s, st][0],
                lhsT_scale=x_codes[s, st][1],
                rhs=w1w[e, s, g][:, 2 * w * part : 2 * w * (part + 1)].bitcast(E2M1),
                rhs_scale=w1_plane(e, s, g)[:, w * part : w * (part + 1)],
                start=(s == 0),
                stop=(s == KP - 1),
            )

        def two_banks(name):
            return psum.tile([P, HP, PASS], F32, name=name, tag="two_banks")

        def first_product(st, g, bank_no):
            first_pass(st, g, 0, bank_no)
            first_pass(st, g, 1)

        relus = {}

        def leave_bank(on_scalar, dst, src):
            if on_scalar:
                nc.scalar.activation(dst, src, ACT.Relu)
            else:
                nc.vector.tensor_scalar_max(dst, src, 0.0)

        def relu(on_scalar, st, g, part=0, parts=1):
            if (st, g) not in relus:
                relus[st, g] = new_tile([P, 4, P], F32, f"relu{st}_{g}")
            m = P // parts
            leave_bank(on_scalar, relus[st, g][:, :, m * part : m * (part + 1)], sums[st, g, part].rearrange("p (m t) -> p t m", t=4))

        turned = {}

        def turn(st, g, bank_no=None):
            if bank_no is not None:
                turned[st, g] = new_bank([P, 4, P], f"turned{st}{g}", bank_no)[:]
            for t in range(4):
                nc.tensor.transpose(turned[st, g][:, t, :], relus[st, g][:, t, :], ident[:])

        hidden = {}

        def square(st, g):
            hidden[st, g] = new_tile([P, P, 4], BF16, f"hidden{st}_{g}")
            nc.scalar.activation(hidden[st, g][:], turned[st, g].rearrange("p t c -> p c t"), ACT.Square)

        def weave_on_gpsimd(s, st):
            woven[s, st] = new_tile([P, P, 4], BF16, f"woven{s}_{st}")
            nc.gpsimd.tensor_scalar(woven[s, st][:], picked[s, st].rearrange("p j c -> p c j"), 1.0, 0.0, ALU.mult, ALU.add)

        def pick_slots(on_scalar, j, c0, c1):
            if (0, 0) not in picked:
                planes = new_tile([P, 4, S], F32, "picked0_0")
                for st in range(ST):
                    picked[0, st] = planes[:, :, st * P : (st + 1) * P]
                picked[0, (0, ST)] = planes
            move(on_scalar, picked[0, (0, ST)][:, j, c0:c1], rows[0, j].indirect(offsets[:, c0 // PER_COLUMN : c1 // PER_COLUMN]))

        def pick_rest(on_scalar, j, c0, c1):
            move(on_scalar, picked[1, (1, ST)][:, j, c0 - P : c1 - P], rows[1, j].indirect(offsets[:, c0 // PER_COLUMN : c1 // PER_COLUMN]))

        h_codes = {}

        def quantize_hidden(st, g):
            h_codes[st, g] = quantize(hidden[st, g], f"h{st}_{g}")

        y_sums = {}

        def second_pass(st, n, g, bank_no=None):
            e = st * P // C
            if bank_no is not None:
                y_sums[st, n] = new_bank([P, P], f"y{st}_{n}", bank_no)[:]
            nc.tensor.matmul_mx(
                out=y_sums[st, n],
                lhsT=w2w[e][:, g, 2 * P * n : 2 * P * (n + 1)].bitcast(E2M1),
                lhsT_scale=w2s[:, e * HP + g, P * n : P * (n + 1)],
                rhs=h_codes[st, g][0],
                rhs_scale=h_codes[st, g][1],
                start=(g == 0),
                stop=(g == HP - 1),
            )

        def second_product(st, n, bank_no=None):
            second_pass(st, n, 0, bank_no)
            second_pass(st, n, 1)

        def second_product_beside(st, n, bank_no, key):
            bank = new_bank([P, 3, P], f"y{st}_{n}", bank_no)
            y_sums[st, n] = bank[:, 0, :]
            turned[key] = bank[:, 1:, :]
            second_pass(st, n, 0)
            second_pass(st, n, 1)

        def second_products(st, blocks, bank_no):
            bank = new_bank([P, len(blocks), P], f"y{st}_{blocks[0]}", bank_no)
            for a, n in enumerate(blocks):
                y_sums[st, n] = bank[:, a, :]
                second_product(st, n)

        values = {}

        def empty(st, n):
            values[st, n] = new_tile([P, P], F32, f"values{st}_{n}")[:]
            nc.scalar.activation(values[st, n], y_sums[st, n], ACT.Copy)

        def scatter_times_gate(st, n):
            nc.vector.tensor_tensor(windows[n][:].indirect(slots(st, st + 1)), values[st, n], gates[:, st * P : (st + 1) * P], ALU.mult)

        def apply_gate(st, n):
            values[st, n] = new_tile([P, P], F32, f"values{st}_{n}")[:]
            nc.vector.tensor_tensor(values[st, n], y_sums[st, n], gates[:, st * P : (st + 1) * P], ALU.mult)

        def scatter(on_scalar, st, n):
            move(on_scalar, windows[n][:].indirect(slots(st, st + 1)), values[st, n])

        def add_and_store(engine, n, c0, c1):
            total = new_tile([P, c1 - c0], F32, f"total{n}_{c0}")
            engine.tensor_tensor(total[:], windows[n][:, c0:c1], residual[n][:, c0:c1], ALU.add)
            nc.sync.dma_start(out=out[n * P : (n + 1) * P, c0:c1], in_=total[:])

        VEC, SCA = False, True
        for j in range(3):
            pick_slots(SCA, j, 320, S)
            pick_slots(VEC, j, 0, 320)
        pick(SCA, 0, 3, 2, 4)
        pick(VEC, 0, 3, 0, 1)
        pick(VEC, 0, 3, 1, 2)
        pick(SCA, 1, 0, 1, 4)
        weave(VEC, 0, 0)
        weave(VEC, 0, 1)
        pick_rest(SCA, 1, 256, S)
        quantize_slots(0, 0)
        first_pass(0, 0, 0, 0, 0, 2)
        pick_woven(VEC, 1, 0, 0)
        first_pass(0, 0, 0, 7, 1, 2)
        pick_rest(SCA, 2, 256, S)
        quantize_slots(0, 1)
        first_pass(1, 0, 0, 2)
        weave_on_gpsimd(0, 2)
        weave_on_gpsimd(0, 3)
        pick_woven(VEC, 1, 1, 0)
        pick(SCA, 1, 3, 1, 2)
        pick_rest(VEC, 1, P, 256)
        first_pass(0, 1, 0, 1)
        first_pass(1, 1, 0, 3)
        pick(SCA, 1, 3, 2, 4)
        pick_woven(VEC, 1, 2, 0)
        pick_rest(VEC, 2, P, 256)
        pick_woven(VEC, 1, 3, 0)
        quantize_slots(1, 0)
        first_pass(0, 0, 1, None, 0, 2)
        first_pass(0, 0, 1, None, 1, 2)
        first_pass(0, 1, 1)
        weave(VEC, 1, 1)
        quantize_slots(0, 2)
        quantize_slots(1, 1)
        first_pass(1, 0, 1)
        first_pass(1, 1, 1)
        weave_on_gpsimd(1, 2)
        weave_on_gpsimd(1, 3)
        relu(SCA, 0, 0, 1, 2)
        relu(VEC, 0, 0, 0, 2)
        relu(VEC, 0, 1)
        relu(SCA, 1, 0)
        relu(VEC, 1, 1)
        turn(0, 0, 4)
        turn(0, 1, 5)
        turn(1, 0, 6)
        turn(1, 1, 7)
        square(0, 0)
        square(0, 1)
        quantize_slots(0, 3)
        quantize_slots(1, 2)
        quantize_slots(1, 3)
        square(1, 0)
        square(1, 1)
        first_pass(2, 0, 0, 0)
        quantize_hidden(0, 0)
        first_pass(2, 0, 1)
        first_pass(2, 1, 0, 1)
        quantize_hidden(0, 1)
        second_product(0, 0, 2)
        empty(0, 0)
        relu(VEC, 2, 0)
        second_product(0, 1, 3)
        empty(0, 1)
        quantize_hidden(1, 0)
        second_product(0, 2, 4)
        first_pass(2, 1, 1)
        empty(0, 2)
        quantize_hidden(1, 1)
        first_pass(3, 0, 0, 2)
        relu(SCA, 2, 1)
        scatter_times_gate(0, 0)
        first_pass(3, 0, 1)
        relu(SCA, 3, 0)
        scatter_times_gate(0, 1)
        turn(2, 0, 3)
        square(2, 0)
        scatter_times_gate(0, 2)
        second_product(1, 0, 1)
        empty(1, 0)
        scatter_times_gate(1, 0)
        first_pass(3, 1, 0, 4)
        quantize_hidden(2, 0)
        first_pass(3, 1, 1)
        relu(SCA, 3, 1)
        turn(2, 1, 5)
        square(2, 1)
        quantize_hidden(2, 1)
        second_product(1, 1, 2)
        empty(1, 1)
        second_product(1, 2, 3)
        apply_gate(1, 2)
        turn(3, 0, 6)
        square(3, 0)
        scatter_times_gate(1, 1)
        turn(3, 1, 7)
        square(3, 1)
        quantize_hidden(3, 0)
        second_product(2, 0, 2)
        scatter(SCA, 1, 2)
        apply_gate(2, 0)
        second_products(2, (1, 2), 6)
        scatter(SCA, 2, 0)
        apply_gate(2, 1)
        quantize_hidden(3, 1)
        second_pass(3, 0, 0, 0)
        apply_gate(2, 2)
        second_pass(3, 1, 0, 1)
        scatter(SCA, 2, 2)
        second_pass(3, 2, 0, 5)
        scatter(VEC, 2, 1)
        second_pass(3, 1, 1)
        apply_gate(3, 1)
        second_pass(3, 0, 1)
        apply_gate(3, 0)
        second_pass(3, 2, 1)
        scatter(SCA, 3, 0)
        apply_gate(3, 2)
        scatter(SCA, 3, 2)
        scatter(VEC, 3, 1)
        add_and_store(nc.vector, 1, 0, 320)
        add_and_store(nc.vector, 1, 320, T)
        add_and_store(nc.vector, 0, 0, 320)
        add_and_store(nc.vector, 0, 320, T)
        add_and_store(nc.vector, 2, 0, 256)
        add_and_store(nc.vector, 2, 256, 512)
        add_and_store(nc.vector, 2, 512, T)
